import numpy as np, ml_dtypes
CORES = [16,17,18,19,32,33,34,35]
N = 8
BF = ml_dtypes.bfloat16
V, SQ, M, S, J = 3712, 16, 24, 3, 384
PAR = [0, 0, 0, 0, 0, 0, 0, 0, 0, 1, 1, 1, 2, 2, 2, 3, 3, 5, 5, 9, 9, 12, 12, 15]
ROW = [0, 0, 1, 2, 3, 4, 5, 6, 7, 0, 8, 9, 0, 10, 11, 0, 12, 13, 14, 0, 15, 0, 1, 0]
C = 64
def parts(rng):
    gi = np.arange(8)[:, None, None]
    od = np.argsort(rng.random((8, V)), axis=1); blk = ((np.argsort(od, axis=1) // C) * C)[:, None, :]
    base = od[gi, blk + rng.integers(0, C, (8, 16, V))]
    turn = (rng.integers(0, 8, (N, 8, 1, V)) * 2 + 1) * np.arange(16)[:, None] + rng.integers(0, 16, (N, 8, 1, V))
    q = np.take_along_axis(base[None], turn & 15, 2)
    own = rng.random(q.shape, dtype=np.float32)
    q = np.where(own < 0.2, od[gi, blk + rng.integers(0, C, q.shape)], q); q = np.where(own > 0.9, rng.integers(0, V, q.shape), q)
    size = np.exp2(rng.integers(-1, 2, (8, 16, 1))).astype(np.float32)
    k = (0.8 * rng.standard_normal((8, 16, V), dtype=np.float32) + 0.6 * rng.standard_normal((N, 8, 16, V), dtype=np.float32)) * size
    x = rng.standard_normal((N, 8, 16, SQ), dtype=np.float32) * size
    kp = (1.5 * rng.random((N, 8, 16, 1)) - 0.25) * size
    cm = np.take_along_axis(rng.integers(0, V // C, (N, 8, 4)), rng.integers(0, 4, (N, 8, SQ)), 2)
    tk = od[np.arange(8)[:, None], C * cm + rng.integers(0, C, (N, 8, SQ))]
    return q, k, x, kp, tk
def tidy(v):
    return np.where(np.abs(v) < 2.0 ** -60, 0, v)
def pack(q, k, x, kp, tk):
    return {"qt": np.ascontiguousarray(q.reshape(N, 128, V)).astype(np.int32), "kt": np.ascontiguousarray(tidy(k).reshape(N, 128, V)).astype(np.float32).astype(BF),
            "x0": np.ascontiguousarray(tidy(x).reshape(N, 128, SQ)).astype(np.float32), "kap": np.ascontiguousarray(tidy(kp).reshape(N, 128, 1)).astype(np.float32),
            "tok": np.ascontiguousarray(tk).astype(np.int32)}
def branch(rng, q, tk, g, e):
    w = rng.permutation(V)[:SQ * (e + 3)].reshape(e + 3, SQ); dep = [0]
    for n in range(1, M): dep.append(dep[PAR[n]] + 1)
    rows = sorted({ROW[n] for n in range(1, M) if dep[n] == e + 1}, reverse=True)
    tk[:, g] = w[0]
    for s in range(SQ):
        for i in range(e + 1): q[:, g, :, int(w[i, s])] = w[i + 1, s]
        for n in range(0, N, 2):
            q[n, g, :, int(w[e, s])] = w[e + 2, s]; q[n, g, rows[(s + SQ * (n // 2)) % len(rows)], int(w[e, s])] = w[e + 1, s]
def setup_inputs(rng):
    return pack(*parts(rng))
def setup_inputs_spread(rng):
    q, k, x, kp, tk = parts(rng)
    k = k * np.exp2(rng.integers(-3, 4, (8, 1, V))) * (rng.random((8, 1, V)) > 0.0625)
    x = x * np.exp2(rng.integers(-3, 4, (N, 8, 1, SQ))); kp = kp * np.exp2(rng.integers(-3, 3, (N, 8, 16, 1)))
    g = rng.permutation(8); z = np.ones((8, 1, 1)); z[g[:3]] = np.array([2.0 ** 12, 2.0 ** -50, 2.0 ** -57])[:, None, None]
    k = np.clip(k * z, -65536, 65536); x = np.clip(x * z, -65536, 65536); kp = np.clip(kp * z, -65536, 65536)
    branch(rng, q, tk, int(g[3]), 2); branch(rng, q, tk, int(g[4]), 1)
    return pack(q, k, x, kp, tk)
def setup_inputs_ends(rng):
    q, k, x, kp, tk = parts(rng)
    q = np.where(rng.random(q.shape, dtype=np.float32) < 0.72, rng.integers(0, 2, q.shape) * (V - 1), q)
    q[:, :, 15, V - 1] = V - 1; q[:, :, 14, V - 1] = 0; q[:, :, 0, 0] = 0; q[:, :, 1, 0] = V - 1
    tk = rng.integers(0, 2, tk.shape) * (V - 1); tk[:, :, 0] = 0; tk[:, :, SQ - 1] = V - 1
    k = np.clip(np.rint(2 * k) * 0.5, -4, 4); x = np.clip(np.rint(2 * x) * 0.5, -4, 4); kp = np.rint(2 * kp) * 0.5
    k[:, ::2, :, V - 1] = k[:, ::2, :, 0]
    k[:, 5, :, V - 1] = 40; k[:, 5, :, 0] = -40; k[:, 1, :, V - 1] = -40; k[:, 1, :, 0] = 40
    kp[N - 1, 7] = 64; kp[0, 7] = -64; kp[0, 4] = 64; kp[1, 4] = -64
    return pack(q, k, x, kp, tk)
def setup_inputs_corners(rng):
    q, k, x, kp, tk = parts(rng); ar = np.arange(V); g = rng.permutation(8)
    q[:, g[0]] = ar
    q[:, g[1]] = (ar + 1) % V; tk[:, g[1]] = V - 1 - rng.integers(0, 4, (N, SQ))
    q[:, g[2], 0::2] = (ar - 1) % V; q[:, g[2], 1::2] = ar; tk[:, g[2]] = rng.integers(0, 4, (N, SQ))
    for n in range(N): q[n, g[3]] = (q[n, g[3]] // N) * N + n
    tk[:, g[4]] = tk[:, g[4], :1]
    q[:, g[5]] = rng.permutation(V)
    q[:, g[6]] = np.where(rng.random((N, 16, V)) < 0.3, ar, rng.integers(0, 2, (N, 16, V)) * (V - 1))
    tk[:, g[7]] = rng.integers(0, 2, (N, SQ)) * (V - 1)
    return pack(q, k, x, kp, tk)
def setup_inputs_crowd(rng):
    q, k, x, kp, tk = parts(rng); g = rng.permutation(8)
    size = np.ones(M, np.int64); full = 256 // M; left = 256 - full * M; rows = []
    for n in range(M - 1, 0, -1): size[PAR[n]] += size[n]
    for n in range(1, M):
        if PAR[n] == 0 and size[n] <= left: left -= int(size[n]); rows.append(ROW[n])
    for i in range(4):
        h = int(g[i]); v = (V - 1, int(rng.integers(1, V - 1)), 0, int(rng.integers(1, V - 1)))[i]
        w = rng.permutation(V); w = w[w != v][:19]; u, p, z = int(w[0]), int(w[1]), int(w[2])
        q[:, h, :, v] = v; q[:, h, :, u] = v; q[:, h, :, z] = z; q[:, h, :, p] = z
        for c in rows: q[:, h, c, p] = v
        for c in w[3:]: q[:, h, :, int(c)] = v
        q[1::2, h, :, v] = w[3:][np.argsort(rng.random((N // 2, 16)), axis=1)]
        tk[:, h] = v
        for n in range(N):
            o = rng.permutation(SQ)
            if i % 2 == 1 and full < SQ: tk[n, h, o[full:]] = z; tk[n, h, o[full]] = p
            if i > 1: tk[n, h, o[0]] = u
    for i in (4, 5):
        w = rng.permutation(V)[:3]
        if i == 4: w = np.array([0, V - 1, 1 + int(rng.integers(0, V - 2))])
        for c in w: q[:, g[i], :, int(c)] = w[rng.integers(0, 3, (N, 16))]
        tk[:, g[i]] = w[rng.integers(0, 3, (N, SQ))]
    tk[:, g[6]] = tk[:, g[6], :1]; tk[:, g[7]] = tk[0, g[7], 0]
    return pack(q, k, x, kp, tk)
def setup_inputs_ties(rng):
    q, k, x, kp, tk = parts(rng)
    e = rng.integers(1, 4, (8, 16, 1)) * 2.0 ** -12 * np.where(rng.random((8, 16, 1)) < 0.6, -1, 1)
    k = np.clip(np.rint(4 * k) * 0.25, -2, 2); x = np.clip(np.rint(4 * x) * 0.25, -2, 2) + e
    kp = np.zeros((N, 1, 1, 1)) + e
    g = rng.permutation(8)[:4]; m = 2.0 ** -14 * np.array([1, 2, 3, 8, 16, 24, -1, -3])
    k[:, g] = np.where(rng.random((N, 4, 16, V), dtype=np.float32) < 0.3, 4096.0, 0.0)
    x[:, g] = rng.choice(m, (N, 4, 16, SQ))
    kp[:, g] = -4096.0
    x[:, g[3]] = 4096.0; kp[:, g[3]] = -rng.choice(m, (N, 16, 1))
    return pack(q, k, x, kp, tk)
def check_inputs(d):
    bad = []
    for k in ("qt", "tok"):
        if np.min(d[k]) < 0 or np.max(d[k]) > V - 1: bad.append("range of " + k)
    for k in ("kt", "x0", "kap"):
        v = np.asarray(d[k]).astype(np.float32)
        if not np.all(np.isfinite(v)) or not np.all(np.abs(v) <= 65536) or not np.all((v == 0) | (np.abs(v) >= 2.0 ** -60)): bad.append("size of " + k)
    return bad
def reference(qt, kt, x0, kap, tok):
    Q = qt.astype(np.int64).reshape(N, 8, 16, V); K = kt.astype(np.float32).reshape(N, 8, 16, V)
    x = np.array(x0, np.float32).reshape(N, 8, 16, SQ); kp = kap.astype(np.float32).reshape(N, 8, 16, 1, 1)
    A = np.array(Q); s = np.array(tok, np.int64); half = np.float32(0.5); gi = np.arange(8); trace = []; yn = np.zeros((N, 8, 16, M, SQ), np.float32)
    for t in range(S):
        for r in range(N):
            q = (r + 1 + t % (N - 1)) % N
            node = [s[r]]
            for n in range(1, M): node.append(np.take_along_axis(A[r][:, ROW[n]], node[PAR[n]], 1))
            tk = np.stack(node, axis=1)
            flat = tk.reshape(8, 1, J)
            kn = np.take_along_axis(K[q], flat, 2).reshape(8, 16, M, SQ)
            xs = [x[r]]
            for n in range(1, M): xs.append(xs[PAR[n]] * half + kn[:, :, n])
            xn = np.stack(xs, axis=2)
            th = (xn - kp[q]).reshape(8, 16, 1, J)
            cand = np.take_along_axis(Q[q], flat, 2)
            kc = np.take_along_axis(K[q], cand.reshape(8, 1, 16 * J), 2).reshape(8, 16, 16, J)
            score = np.add.reduce((kc >= th).astype(np.int64), axis=1)
            cols = np.take_along_axis(cand, np.argsort(-score, axis=1, kind="stable"), 1)
            top = cols[:, 0].reshape(8, M, SQ)
            ok = np.zeros((8, M, SQ), bool); ok[:, 0] = True; best = np.zeros((8, SQ), np.int64)
            for n in range(1, M):
                ok[:, n] = ok[:, PAR[n]] & (tk[:, n] == top[:, PAR[n]]); best = np.where(ok[:, n], n, best)
            s[r] = np.take_along_axis(top, best[:, None, :], 1)[:, 0]
            x[r] = np.take_along_axis(xn, best[:, None, None, :], 2)[:, :, 0]
            if t < S - 1:
                for j in range(J): A[r][gi, :, flat[:, 0, j]] = cols[:, :, j]
            else: yn[r] = xn
        trace.append(np.array(s))
    return {"yt": np.stack(trace, axis=2).reshape(N, 8, S * SQ).astype(np.float32), "yx": x.reshape(N, 128, SQ), "yn": yn.reshape(N, 128, J)}

@@ -1,0 +1,629 @@
+import numpy as np
+from concourse.bass import DstId, RemoteDMATransfer
+from concourse.mybir import AluOpType as Op, AxisListType, ActivationFunctionType as AF
+
+N, V, M = 8, 3712, 24
+PAR = [0, 0, 0, 0, 0, 0, 0, 0, 0, 1, 1, 1, 2, 2, 2, 3, 3, 5, 5, 9, 9, 12, 12, 15]
+ROW = [0, 0, 1, 2, 3, 4, 5, 6, 7, 0, 8, 9, 0, 10, 11, 0, 12, 13, 14, 0, 15, 0, 1, 0]
+DEP = [0] * M
+for _n in range(1, M):
+    DEP[_n] = DEP[PAR[_n]] + 1
+INNER = sorted(set(PAR))
+MID = 1856
+CH = 8
+
+_A, _B, _C, _D, _E, _F = [0, 1, 2, 3], [4, 5, 6, 7], [0, 1, 4, 5], [2, 3, 6, 7], [0, 2, 4, 6], [1, 3, 5, 7]
+NET = [
+    [("max", 0, _A + _B, _A + _B, _A + _B), ("min", 1, _A + _B, _A + _B, _A + _B)],
+    [("max", 0, _B, _A, _B), ("min", 0, _A, _B, _A), ("max", 1, _A, _B, _D), ("min", 1, _B, _A, _C)],
+    [("max", 0, _C, _A, _C), ("min", 0, _C, _A, _D), ("max", 1, _D, _B, _D), ("min", 1, _D, _B, _C)],
+    [("max", 0, _A, _B, _F), ("min", 0, _B, _A, _E), ("max", 1, _B, _A, _F), ("min", 1, _A, _B, _E)],
+    [("max", 0, _B, _B, _D), ("min", 0, _A, _A, _C), ("max", 1, _A, _A, _D), ("min", 1, _B, _B, _C)],
+    [("max", 0, _B, _B, _F), ("min", 0, _B, _B, _E), ("max", 1, _A, _A, _E), ("min", 1, _A, _A, _F)],
+    [("max", 0, [2, 3], [4, 5], [2, 3]), ("max", 0, [4, 5], [2, 3], [6, 7]), ("min", 0, [6, 7], [0, 1], [0, 1]),
+     ("min", 0, [0, 1], [6, 7], [4, 5]), ("max", 1, [6, 7], [0, 1], [4, 5]), ("max", 1, [0, 1], [6, 7], [6, 7]),
+     ("min", 1, [2, 3], [4, 5], [0, 1]), ("min", 1, [4, 5], [2, 3], [2, 3])],
+    [("max", 0, _B, _C, _A), ("min", 0, _B, _C, _B), ("max", 1, _A, _D, _A), ("min", 1, _A, _D, _B)],
+    [("max", 0, _E, _E, _E), ("min", 0, _F, _F, _F), ("max", 1, _F, _F, _E), ("min", 1, _E, _E, _F)],
+    [("max", 2, _D, _D, _E), ("max", 2, _C, _C, [8, 10, 12, 14]), ("min", 2, _D, _D, _F), ("min", 2, _C, _C, [9, 11, 13, 15])],
+]
+
+F32, BF, H16, I32, U16 = "float32", "bfloat16", "float16", "int32", "uint16"
+SCRATCH = {}
+
+
+def _decl(where, dtype, **shapes):
+    for name, shape in shapes.items():
+        SCRATCH[name] = (where, [128] + list(shape), dtype)
+
+
+_decl("sbuf", I32, Q=[V], A=[V + 384], tokI=[4], lane=[4], li=[4], bci=[16], H=[4], H2=[4], srt=[24, 4, 4], srm=[24, 16], topi=[24], topm=[24])
+_decl("sbuf", BF, K=[V], kc=[5120], geA=[5120], geB=[1024], gec=[256], colg=[128], colb=[128], cm=[128], SelT=[4, 128], Gm=[8], tie=[24, 16],
+      IdB=[128], own=[64], i4=[64], mid=[192], ones=[128], Mi=[384], Eq=[24, 16 * CH], kns=[384], knl=[384])
+_decl("sbuf", H16, Mk=[384], Id=[8, 16], Iev=[128], Iod=[128], Sel=[16, 128], G=[8, 128], Wh=[24], candh=[384], srh=[24, 16], E=[3, 8, 8], ch=[32], cT=[32])
+_decl("sbuf", U16, bc=[16], parl=[36], sell=[12], rootd=[2], dup3=[16], Ws0=[32], Ws1=[32], Ws2=[48], Wl0=[24], Wl1=[24], Wl2=[24], cand=[384],
+      Os0=[384], Os1=[384], Ol0=[384], Ol1=[384], L=[24], bl=[2], CT=[8], cu=[32])
+_decl("sbuf", F32, kp=[4], sc=[12], cnt=[24], z4=[4], m4=[4], i16=[16], d16=[16], n8=[8],
+      RR=[96], Rm=[96], Rs=[8], PR=[36], trash=[24], cmpN=[24], Tt=[288], Gt=[256], Wf=[24], Wc=[24], Vc=[24], t24=[24], u24=[24], ok=[24], cmp=[24], mm=[24],
+      v=[4], v2=[2], x0s=[16], mv0=[16], mv1=[20], mv2=[20], md0=[20], md1=[20], ms0=[20], ms1=[20], CX=[72], mdC=[72], c4=[4], mdD=[4], fin=[20], chx=[16], thc=[256],
+      xn=[384], xh=[256], kn=[384], thb=[1024], S0=[24, 2, 4], S1=[24, 2, 4], S2=[24, 2, 4], tr4=[24, 4], tr2=[24, 2])
+_decl("psum", F32, comp=[64, 2, 4], comq=[64, 2, 4], P=[64, 2, 4], back=[512], rep=[512], th=[512], tw=[512], req=[512])
+SC = ["lf", "l16", "grp", "odd", "l4", "evn", "o16", "g4", "nkp", "tokf"]
+
+DMAS = ["dtok", "dx0", "dkap", "dQ", "dK", "dA", "dy0", "dy1", "dy2", "dyx", "dn0", "dn1"]
+MSGS = ["rx0", "rWa0", "rWb0", "rWa1", "rWb1", "rWa2", "rWb2", "rOa0", "rOb0", "rOa1", "rOb1", "rd0", "rd1", "rv1", "rv2", "rC", "rD", "rka", "rkb", "rkc", "rWc2", "rOc0", "rOc1"]
+SEMAPHORES = ["eV", "eA", "eT", "eG", "left"] + DMAS + MSGS
+
+PL = dict(cyc=1.04e-3, gather=1.56, scatter=3.8, hop=2.4, pe=1.04e-3, issue=0.3, byte=1.2e-3, same=0.06, cross=0.1)
+OCUT = [0, 128, 384]
+NV = 6
+BUMP = {'v0.kn': 6, 'v1.kn': 6, 'm1.tr4': 2.8, 'm1.ms1': 2.5, 'v1.geA': 1.9, 'h.rC': 2.0, 'm0.cmp': 1.7, 'c.Mi': 1.7, 'v1.thb': 2.5, 'v0.thb': 2.5,
+        'v0.xh': 2.9, 'v1.back': 1.9, 'c.i4': 0.4, 'v0.rOa0': 2.5, 'm0.md0': 0.2, 'm0.E': 1.7, 'h.cT': 0.9, 'c.Q': -0.1, 'm1.mm': -1.4, 'v1.srh': 0.2,
+        'm1.rd1': 2.7, 'v1.S0': -0.1, 'm2.ok': -0.4, 'm1.cmp': -2.3, 'm0.tw': 0.2, 'c.G': -0.2, 'v0.geB': -3.0, 'm2.bl': -0.5, 'h.chx': 1.5, 'd2.Ws2': 0.7}
+
+
+def c(name, *idx):
+    return (name, (slice(None),) + idx)
+
+
+def p(name, lo, hi, *idx):
+    return (name, (slice(lo, hi),) + idx)
+
+
+def s(a, b, step=None):
+    return slice(a, b, step)
+
+
+def ind(win, off):
+    return ("*", win, off)
+
+
+def cube(name, wires, rows=slice(0, 24)):
+    def ax(vals):
+        vals = sorted(set(vals))
+        if len(vals) == 1:
+            return slice(vals[0], vals[0] + 1)
+        return slice(vals[0], vals[-1] + 1, vals[1] - vals[0])
+    return c(name, rows, ax([w // 4 for w in wires]), ax([w % 4 for w in wires]))
+
+
+def elems(r):
+    shape = SCRATCH[r[0]][1][1:]
+    return np.arange(int(np.prod(shape))).reshape(shape)[r[1][1:]].reshape(-1)
+
+
+def build():
+    ops, tag = [], ["c"]
+    CYC, GATHER, SCATTER, HOP = PL["cyc"], PL["gather"], PL["scatter"], PL["hop"]
+
+    def add(eng, meth, args, outs, ins, cost, kw=None, **more):
+        reads = []
+        for r in ins:
+            if isinstance(r, tuple):
+                reads += [r[1], r[2]] if r[0] == "*" else [r]
+        writes = []
+        for r in outs:
+            if r[0] == "*":
+                writes.append(r[1])
+                reads.append(r[2])
+            else:
+                writes.append(r)
+        d = dict(e=eng, m=meth, a=args, k=kw or {}, r=[x for x in reads if x[0] in SCRATCH], w=[x for x in writes if x[0] in SCRATCH], c=cost, lat=0.0)
+        d["key"] = tag[0] + "." + (args[0][3] if meth == "send" else writes[0][0])
+        d.update(more)
+        ops.append(d)
+
+    def vcost(out, ins, two=False):
+        if out[0] == "*":
+            return 0.06 + SCATTER * CYC * 16 * len(elems(out[2]))
+        if ins[0][0] == "*":
+            return 0.06 + GATHER * CYC * len(elems(out))
+        n = len(elems(ins[0]))
+        if two:
+            n *= 1 if "psum" in (SCRATCH[ins[0][0]][0], SCRATCH[ins[1][0]][0]) else 2
+        elif all(SCRATCH[x[0]][2] in (BF, H16, U16) for x in [out] + ins):
+            n *= 0.5
+        return max(64, n) * CYC
+
+    def cp(out, a): add("V", "cp", [out, a], [out], [a], vcost(out, [a]))
+    def tt(out, a, b, op): add("V", "tt", [out, a, b, op], [out], [a, b], vcost(out, [a, b], True))
+    def ts(out, a, s1, op0, s2=None, op1=None):
+        add("V", "ts", [out, a, s1, s2, op0] + ([op1] if op1 is not None else []), [out], [a, s1, s2], vcost(out, [a]))
+    def red(out, a, op): add("V", "red", [out, a, AxisListType.X, op], [out], [a], vcost(out, [a]))
+    def trn(out, a): add("V", "trn", [out, a], [out], [a], vcost(out, [a]))
+    def ms(out, val): add("V", "ms", [out, val], [out], [], vcost(out, [out]))
+    def scan(out, a, b, init, op0, op1): add("V", "scan", [out, a, b, init, op0, op1], [out], [a, b], vcost(out, [a, b]))
+    def act(out, a, bias=None, fn=AF.Identity):
+        n = vcost(out, [a]) if a[0] == "*" else max(64, len(elems(a))) * CYC
+        add("A", "act", [out, a, fn if bias else AF.Copy], [out], [a, bias], n + 0.02, {"bias": bias} if bias else None)
+    def mmul(out, l, r, st, sp): add("T", "mm", [out, l, r, st, sp], [out], [l, r], max(64, len(elems(r))) * PL["pe"], st=st, sp=sp)
+    def iota(out, pat, base, cmul):
+        kw = {} if SCRATCH[out[0]][2] == I32 else {"allow_small_or_imprecise_dtypes": True}
+        add("G", "iota", [out, pat, base, cmul], [out], [], 0.16 + 2 * CYC * len(elems(out)), kw)
+    def pcopy(out, a, pat): add("G", "sel", [out, a, pat, Op.is_gt, 0.0, 1, 0], [out], [a], 0.21 + 2 * CYC * len(elems(out)))
+    def dma(q, out, a, sem, lat, behind=None): add(q, "dma", [out, a], [out], [a, behind], 0.06, sem=sem, lat=lat)
+    def send(parts):
+        nb = len(elems(parts[0][1])) * (4 if SCRATCH[parts[0][1][0]][2] in (F32, I32) else 2)
+        add("G", "send", parts, [], [x[1] for x in parts], PL["issue"])
+        me = len(ops) - 1
+        for i, x in enumerate(parts):
+            add("R", "recv", [parts, i], [x[2]], [], 0.0, sem=x[3], after=me, lat=HOP + nb * PL["byte"])
+
+    col = lambda name, j: c("sc", s(SC.index(name), SC.index(name) + 1)) if name in SC else c(name, s(j, j + 1))
+    Kw, Qw, Aw = c("K"), c("Q"), c("A", s(0, V))
+
+    dma("A", col("tokI", 0), ("tok", (slice(None),)), "dtok", 2.0)
+    dma("A", c("x0s"), ("x0", (slice(None),)), "dx0", 2.0)
+    dma("A", col("kp", 0), ("kap", (slice(None),)), "dkap", 2.0)
+    dma("S", Qw, ("qt", (slice(None),)), "dQ", 7.0)
+    dma("S", Kw, ("kt", (slice(None),)), "dK", 9.5)
+    send([(1, c("x0s"), c("mv0"), "rx0")])
+
+    iota(col("lane", 0), [[0, 1]], 0, 1)
+    iota(c("i16"), [[1, 16]], 0, 0)
+    iota(c("colb"), [[1, 128]], 0, 0)
+    iota(c("colg"), [[1, 8], [0, 16]], 0, 0)
+    iota(c("bci"), [[1, 16]], 0, 0)
+    iota(c("trash"), [[16, 24]], V, 0)
+    iota(c("cmpN"), [[4096, 24]], MID, 0)
+    iota(c("Mi"), [[0, 24], [1, 16]], 0, 0)
+    iota(c("i4"), [[1, 4], [0, 16]], 0, 0)
+    iota(c("cm"), [[1, 32], [0, 4]], 0, 0)
+    iota(p("tie", 0, 1), [[0, 24], [-4096, 16]], 15 * 4096, 0)
+    cp(col("lf", 0), col("lane", 0))
+    for j, (sh, an, name) in enumerate([(0, 15, "l16"), (4, 7, "grp"), (4, 1, "odd"), (0, 3, "l4")]):
+        ts(col("li", j), col("lane", 0), sh, Op.arith_shift_right, an, Op.bitwise_and)
+        cp(col(name, 0), col("li", j))
+    l16, grp = col("l16", 0), col("grp", 0)
+    ts(col("evn", 0), col("odd", 0), -1.0, Op.mult, 1.0, Op.add)
+    ts(col("o16", 0), col("odd", 0), 16.0, Op.mult)
+    ts(col("g4", 0), grp, 4.0, Op.mult)
+    ts(c("d16"), c("i16"), l16, Op.is_equal)
+    ms(c("z4"), 0.0); ms(c("m4"), -float(MID)); ms(c("Tt"), 0.0); ms(col("ok", 0), 1.0)
+    child = lambda n: 32 + 32 * INNER.index(PAR[n]) + ROW[n] if n else 0
+    lists = [[child(n) for n in (1, 1, 2, 2, 3, 3, 5, 5)] + [child(n) for n in range(8)],
+             [child(n) - 64 for n in (9, 9, 12, 12, 15, 15)] + [0] * 10,
+             [child(n) for n in range(8, 24)],
+             [child(n) for n in (1, 1, 2, 2, 3, 3, 5, 5)] + [child(n) for n in range(1, 9)],
+             [child(n) - 64 for n in list(range(9, 19)) + [9, 9, 12, 12, 15, 15]],
+             [child(n) - 192 for n in range(19, 24)] + [0] * 11]
+    flat = sum(lists, [])
+    j = 0
+    while j < 96:
+        e = j
+        while e < 96 and flat[e] == flat[j] and e // 16 == j // 16:
+            e += 1
+        ms(c("RR", s(j, e)), float(flat[j]))
+        j = e
+    for j in range(6):
+        tt(c("Rm", s(16 * j, 16 * j + 16)), c("RR", s(16 * j, 16 * j + 16)), c("d16"), Op.mult)
+        red(col("Rs", j), c("Rm", s(16 * j, 16 * j + 16)), Op.add)
+        ts(col("sell", 2 * j), col("Rs", j), col("o16", 0), Op.add)
+    pr = [0] * 8 + [16 * PAR[n] for n in range(8, 19)] + [0] + [16 * (PAR[n] - 8) for n in range(19, 24)] + [0]
+    pr += [16 * PAR[n] for n in range(9, 19)]
+    j = 0
+    while j < 36:
+        e = j
+        while e < 36 and pr[e] == pr[j]:
+            e += 1
+        ms(c("PR", s(j, e)), float(pr[j]))
+        j = e
+    ts(c("parl"), c("PR"), l16, Op.add)
+    cp(c("bc"), c("bci"))
+    ts(c("trash"), c("trash"), l16, Op.add)
+    ts(c("Mk"), c("Mi"), l16, Op.is_le, 8192.0, Op.mult)
+    ts(c("own"), c("i4"), col("l4", 0), Op.is_equal, 2.0 ** 21, Op.mult)
+    ts(c("IdB"), c("colb"), col("lf", 0), Op.is_equal)
+    ts(c("n8"), c("i16", s(0, 8)), grp, Op.is_equal)
+    ts(c("Gm"), c("i16", s(0, 8)), grp, Op.is_equal, 65536.0, Op.mult)
+    ms(p("mid", 0, 1), float(MID)); ms(p("ones", 0, 1), 1.0)
+    ts(c("Id"), c("colb"), col("lf", 0), Op.is_equal)
+    ts(c("Iev"), c("colb"), col("lf", 0), Op.is_equal, col("evn", 0), Op.mult)
+    ts(c("Iod"), c("colb"), col("lf", 0), Op.is_equal, col("odd", 0), Op.mult)
+    ts(c("cm"), c("cm"), col("g4", 0), Op.subtract)
+    for j in range(16):
+        ts(c("Sel", j), c("colg"), grp, Op.is_equal, col("d16", j), Op.mult)
+    for j in range(8):
+        ts(c("G", j), c("colb"), l16, Op.subtract, 16.0 * j, Op.is_equal)
+    for j in range(4):
+        ts(c("SelT", j), c("cm"), float(j), Op.is_equal, 65536.0, Op.mult)
+    ts(col("nkp", 0), col("kp", 0), -1.0, Op.mult)
+    cp(col("tokf", 0), col("tokI", 0))
+    kp = col("kp", 0)
+
+    def draft(t, root):
+        tab, W = (Qw if t == 0 else Aw), "Ws%d" % t
+        ts(c("rootd"), c("z4", s(0, 2)), root, Op.add)
+        ts(c("Tt", s(0, 32, 16)), c("z4", s(0, 2)), root, Op.add)
+        cp(c("Gt", s(0, 32)), ind(tab, c("rootd")))
+        trn(c("Tt", s(32, 64)), c("Gt", s(0, 32)))
+        if t == 2:
+            cp(c(W, s(0, 16)), ind(c("Tt", s(0, 64)), col("sell", 6)))
+            send([(3, c(W, s(8, 16)), c("Wl2", s(0, 8)), "rWa2")])
+            cp(c("Gt", s(32, 160)), ind(tab, c(W, s(0, 8))))
+            trn(c("Tt", s(64, 192)), c("Gt", s(32, 160)))
+            cp(c(W, s(16, 32)), ind(c("Tt", s(64, 192)), col("sell", 8)))
+            send([(3, c(W, s(16, 26)), c("Wl2", s(8, 18)), "rWb2")])
+            cp(c("Gt", s(160, 256)), ind(tab, c(W, s(26, 32))))
+            trn(c("Tt", s(192, 288)), c("Gt", s(160, 256)))
+            cp(c(W, s(32, 48)), ind(c("Tt", s(192, 288)), col("sell", 10)))
+            send([(3, c(W, s(32, 38)), c("Wl2", s(18, 24)), "rWc2")])
+            return
+        cp(c(W, s(0, 16)), ind(c("Tt", s(0, 64)), col("sell", 0)))
+        send([(1 + t, c(W, s(8, 16)), c("Wl%d" % t, s(0, 8)), "rWa%d" % t)])
+        cp(c("Gt", s(32, 160)), ind(tab, c(W, s(0, 8))))
+        trn(c("Tt", s(64, 192)), c("Gt", s(32, 160)))
+        cp(c("dup3"), ind(c("Tt", s(64, 192)), col("sell", 2)))
+        cp(c("Gt", s(160, 256)), ind(tab, c("dup3", s(0, 6))))
+        trn(c("Tt", s(192, 288)), c("Gt", s(160, 256)))
+        cp(c(W, s(16, 32)), ind(c("Tt"), col("sell", 4)))
+        send([(1 + t, c(W, s(16, 32)), c("Wl%d" % t, s(8, 24)), "rWb%d" % t)])
+
+    def dedupe(t):
+        W = c("Ws%d" % t, s(8, 32))
+        ts(c("Wh"), W, -float(MID), Op.add)
+        ts(c("Wc"), W, -1.0, Op.mult, float(MID), Op.add)
+        cp(c("Wf"), W)
+        mmul(c("req", s(0, 384)), c("Id"), c("Mk"), True, False)
+        for j in range(16):
+            mmul(c("req", s(j, 384, 16)), c("Sel", j), c("Wh"), False, j == 15)
+        for j in range(16):
+            mmul(c("rep", s(j, 384, 16)), c("Sel", j), c("Wh"), True, True)
+        for a in range(24):
+            w = 16 * (CH - a % CH)
+            act(c("Eq", a, s(0, 16)), c("req", s(16 * a, 16 * a + 16)), col("Wc", a), AF.Abs)
+            if w > 16:
+                act(c("Eq", a, s(16, w)), c("rep", s(16 * a + 16, 16 * a + w)), col("Wc", a), AF.Abs)
+            e = c("Eq", a, s(0, w))
+            add("A", "act", [e, e, AF.Relu], [e, col("cnt", a)], [e], max(64, w) * CYC + 0.04,
+                {"bias": 4096.0, "scale": -4096.0, "accum_out": col("cnt", a)})
+        tt(c("t24"), c("cnt"), c("trash"), Op.min)
+        tt(c("u24"), c("t24"), c("Wf"), Op.max)
+        cp(c("L"), c("u24"))
+
+    def scatter(t):
+        for k in range(24 // CH):
+            cp(ind(c("A"), c("L", s(k * CH, k * CH + CH))), c("Ol%d" % t, s(16 * CH * k, 16 * CH * (k + 1))))
+
+    def states(x, kn, cut, at):
+        cp(c("xn", s(0, 16)), x)
+        ts(c("xh", s(0, 16)), x, 0.5, Op.mult)
+        tt(c("xn", s(16, 16 * cut)), ind(c("xh", s(0, 16)), c("parl", s(0, cut - 1))), c(kn, s(16, 16 * cut)), Op.add)
+        ts(c("xh", s(16, 96)), c("xn", s(16, 96)), 0.5, Op.mult)
+        tt(c("xn", s(16 * cut, 304)), ind(c("xh", s(0, 96)), c("parl", s(at, at + 19 - cut))), c(kn, s(16 * cut, 304)), Op.add)
+        ts(c("xh", s(128, 256)), c("xn", s(128, 256)), 0.5, Op.mult)
+        tt(c("xn", s(304, 384)), ind(c("xh", s(128, 256)), c("parl", s(20, 25))), c(kn, s(304, 384)), Op.add)
+
+    def commit(W, top, win, out):
+        for q in INNER:
+            kids = [n for n in range(1, M) if PAR[n] == q]
+            ts(c("ok", s(kids[0], kids[-1] + 1)), c(W, s(kids[0], kids[-1] + 1)), top(q), Op.is_equal, col("ok", q), Op.mult)
+        tt(c("mm"), c("ok"), c("cmp"), Op.mult)
+        red(col("v", 0), c("mm"), Op.max)
+        ts(c("H"), c("m4"), col("v", 0), Op.add, 2.0 ** -12, Op.mult)
+        ts(c(out, s(16, 20)), c("H"), -4096.0, Op.mult, col("v", 0), Op.add)
+        ts(col("bl", 0), col("H", 0), 16.0, Op.mult, l16, Op.add)
+        cp(c(out, s(0, 16)), ind(win, col("bl", 0)))
+
+    def tops(t):
+        for j in range(8):
+            ts(c("E", s(0, 3), j), c("topm"), -float(MID), Op.add, col("n8", j), Op.mult)
+        for j in range(8):
+            mmul(c("tw", s(0, 24)), c("G", j), c("E", s(0, 3), s(0, 8), j), j == 0, j == 7)
+        tt(c("cmp"), c("tw", s(0, 24)), c("cmpN"), Op.add)
+        commit("Vc", lambda q: col("tw", q), c("xn"), "ms%d" % t)
+        send([(-1 - t, c("ms%d" % t), c("md%d" % t), "rd%d" % t), (1, c("ms%d" % t), c("mv%d" % (t + 1)), "rv%d" % (t + 1))])
+
+    def verify(t):
+        W = "Wl%d" % t
+        for j, bank in enumerate(("comp", "comq")):
+            mmul(c(bank, s(0, 24)), p("ones", 0, 1), p("tie", 0, 1, s(0, 24), s(8 * j, 8 * j + 8)), True, False)
+            mmul(c(bank, s(0, 24)), p("ones", 0, 1), p("mid", 0, 1), False, False)
+        for a, b in ((0, 4), (4, 8), (8, 12), (12, 24)):
+            cp(c("cand", s(16 * a, 16 * b)), ind(Qw, c(W, s(a, b))))
+        act(c("kn", s(0, 128)), ind(Kw, c(W, s(0, 8))))
+        act(c("kn", s(128, 384)), ind(Kw, c(W, s(8, 24))))
+        states(c("mv%d" % t, s(0, 16)), "kn", 8, 8)
+        ts(c("Vc"), c(W), -float(MID), Op.add)
+        ts(c("thb", s(0, 1024, 16)), c("xn", s(64, 128)), kp, Op.subtract)
+        for k in range(1, NV):
+            ts(c("thb", s(k, 1024, 16)), c("xn", s(64, 128)), kp, Op.subtract)
+        for k in range(NV, 16):
+            pcopy(c("thb", s(k, 1024, 16)), c("thb", s(0, 1024, 16)), [[0, 64]])
+        for a, b in ((0, 64), (128, 304), (304, 384)):
+            ts(c("th", s(a, b)), c("xn", s(a, b)), kp, Op.subtract)
+        for b in range(3):
+            ts(c("candh", s(128 * b, 128 * b + 128)), c("cand", s(128 * b, 128 * b + 128)), -float(MID), Op.add)
+            for j, bank in enumerate(("comp", "comq")):
+                mmul(c(bank, s(8 * b, 8 * b + 8)), c("candh", s(128 * b, 128 * b + 128)), c("Id", s(0, 8), s(8 * j, 8 * j + 8)), False, False)
+        at = lambda lo, hi, b, k: p("comq" if k > 7 else "comp", lo, hi, s(8 * b, 8 * b + 8), k % 8 // 4, k % 4)
+        for u, h in enumerate((0, 2, 3, 4, 5)):
+            act(c("kc", s(1024 * u, 1024 * u + 1024)), ind(Kw, c("cand", s(64 * h, 64 * h + 64))))
+        tt(c("geB"), ind(Kw, c("cand", s(64, 128))), c("thb"), Op.is_ge)
+        for k in range(16):
+            mmul(at(64, 128, 0, k), c("geB", s(k, 1024, 16)), c("Gm"), False, False)
+        for u, h in enumerate((0, 2, 3, 4, 5)):
+            for k in range(15, -1, -1):
+                tt(c("geA", s(320 * k + 64 * u, 320 * k + 64 * u + 64)), c("kc", s(1024 * u + k, 1024 * u + 1024, 16)), c("th", s(64 * h, 64 * h + 64)), Op.is_ge)
+                if h == 0:
+                    mmul(at(0, 64, 0, k), c("geA", s(320 * k, 320 * k + 64)), c("Gm"), False, False)
+                elif h % 2:
+                    mmul(at(0, 128, h // 2, k), c("geA", s(320 * k + 64 * u - 64, 320 * k + 64 * u + 64)), c("Gm"), False, h == 5 and k % 8 == 0)
+        act(c("S0"), c("comq", s(0, 24)))
+        for L, layer in enumerate(NET):
+            sin, sout = ("S0", "S2") if L == 0 else ("S2" if L == 1 else "S%d" % (L % 2), "S%d" % ((L + 1) % 2))
+            rin, rout = s(32 * (L % 2), 32 * (L % 2) + 24), s(32 - 32 * (L % 2), 56 - 32 * (L % 2))
+            for op, mem, a, b, o in layer:
+                tt(cube("P", o, rout) if mem == 1 else cube([sout, None, "srt"][mem], o), cube(sin, a), cube("P" if L else "comp", b, rin),
+                   Op.max if op == "max" else Op.min)
+            if L == 0 and t == 1:
+                tag[0] = "m1"
+                tt(c("tr4"), c("S2", s(0, 24), 0), c("S2", s(0, 24), 1), Op.max)
+                tt(c("tr2"), c("tr4", s(0, 24), s(0, 2)), c("tr4", s(0, 24), s(2, 4)), Op.max)
+                tt(c("topi"), c("tr2", s(0, 24), 0), c("tr2", s(0, 24), 1), Op.max)
+                ts(c("topm"), c("topi"), 4095, Op.bitwise_and)
+                tops(t)
+                tag[0] = "v1"
+        O = "Os%d" % t
+        for b, bank in enumerate((c("back", s(0, 128)), c("th", s(0, 128)), c("comq", s(0, 16)))):
+            rows = s(8 * b, 8 * b + 8)
+            ts(c("srm", rows), c("srt", rows), 4095, Op.bitwise_and)
+            ts(c("srh", rows), c("srm", rows), -float(MID), Op.add)
+            mmul(bank, c("srh", rows), c("Id"), True, True)
+            ts(c(O, s(128 * b, 128 * b + 128)), bank, float(MID), Op.add)
+            if 128 * b + 128 in OCUT:
+                j = OCUT.index(128 * b + 128)
+                send([(-1 - t, c(O, s(OCUT[j - 1], OCUT[j])), c("Ol%d" % t, s(OCUT[j - 1], OCUT[j])), "rO%s%d" % ("abc"[j - 1], t))])
+        if t == 0:
+            tag[0] = "m0"
+            ts(c("topm"), c("srt", s(0, 24), 0, 0), 4095, Op.bitwise_and)
+            tops(t)
+
+    def chain():
+        ts(c("CT", s(0, 2)), c("z4", s(0, 2)), col("mv2", 16), Op.add)
+        cp(c("CX", s(0, 16)), c("mv2", s(0, 16)))
+        for l in range(4):
+            tk, x = c("CT", s(2 * l, 2 * l + 2)), c("CX", s(16 * l, 16 * l + 16))
+            cp(c("cu"), ind(Qw, tk))
+            if l:
+                tt(x, ind(Kw, col("CT", 2 * l)), c("chx"), Op.add)
+            for j in range(2):
+                act(c("thc", s(128 * j, 128 * j + 128)), ind(x, c("bc", s(8 * j, 8 * j + 8))), col("nkp", 0))
+            ts(c("ch"), c("cu"), -float(MID), Op.add)
+            trn(c("cT"), c("ch"))
+            if l < 3:
+                ts(c("chx"), x, 0.5, Op.mult)
+            out = c("tw", s(32, 96))
+            mmul(out, p("ones", 0, 1), p("tie", 0, 1, s(0, 4)), True, False)
+            mmul(out, p("ones", 0, 1), p("mid", 0, 1, s(0, 64)), False, False)
+            mmul(out, c("IdB"), c("own"), False, False)
+            for j in range(4):
+                mmul(c("tw", s(32 + 16 * j, 48 + 16 * j)), c("Iev"), c("cT", s(0, 16)), False, False)
+                mmul(c("tw", s(32 + 16 * j, 48 + 16 * j)), c("Iod"), c("cT", s(16, 32)), False, False)
+            for j in range(2):
+                tt(c("gec", s(128 * j, 128 * j + 128)), ind(Kw, c("cu", s(8 * j, 8 * j + 8))), c("thc", s(128 * j, 128 * j + 128)), Op.is_ge)
+            for j in range(4):
+                mmul(out, c("SelT", j), c("gec", s(64 * j, 64 * j + 64)), False, j == 3)
+            red(col("v2", 0), out, Op.max)
+            if l < 3:
+                ts(c("H2", s(0, 2)), c("m4", s(0, 2)), col("v2", 0), Op.add, 2.0 ** -12, Op.mult)
+                ts(c("CT", s(2 * l + 2, 2 * l + 4)), c("H2", s(0, 2)), -4096.0, Op.mult, col("v2", 0), Op.add)
+        ts(c("H2"), c("m4"), col("v2", 0), Op.add, 2.0 ** -12, Op.mult)
+        ts(c("c4"), c("H2"), -4096.0, Op.mult, col("v2", 0), Op.add)
+        cp(c("CX", s(64, 72)), c("CT"))
+        send([(-3, c("CX"), c("mdC"), "rC")])
+        send([(-3, c("c4"), c("mdD"), "rD")])
+
+    yt = lambda t: ("yt", (slice(None), s(16 * t, 16 * t + 16)))
+    for t in range(2):
+        tag[0] = "d%d" % t
+        draft(t, col("tokf", 0) if t == 0 else col("md0", 16))
+        if t == 0:
+            dma("S", Aw, ("qt", (slice(None),)), "dA", 7.0, c("Wl0", s(8, 24)))
+        tag[0] = "u%d" % t
+        dedupe(t)
+        tag[0] = "v%d" % t
+        verify(t)
+        dma("S", yt(t), col("md%d" % t, 16), "dy%d" % t, 2.0)
+        if t == 1:
+            tag[0] = "h"
+            chain()
+        tag[0] = "s%d" % t
+        scatter(t)
+    tag[0] = "d2"
+    draft(2, col("md1", 16))
+    tag[0] = "v2"
+    for (a, b), (lo, hi), sem in (((0, 8), (16, 144), "rka"), ((8, 18), (144, 304), "rkb"), ((18, 23), (304, 384), "rkc")):
+        act(c("kns", s(lo, hi)), ind(Kw, c("Wl2", s(a, b))))
+        send([(-3, c("kns", s(lo, hi)), c("knl", s(lo, hi)), sem)])
+    states(c("md1", s(0, 16)), "knl", 9, 26)
+    dma("S", ("yn", (slice(None), s(0, 304))), c("xn", s(0, 304)), "dn0", 2.4)
+    dma("A", ("yn", (slice(None), s(304, 384))), c("xn", s(304, 384)), "dn1", 2.1)
+    tag[0] = "m2"
+    cp(c("Wf", s(1, 19)), c("Ws2", s(8, 26)))
+    cp(c("Wf", s(19, 24)), c("Ws2", s(32, 37)))
+    ms(c("cmp", s(19, 24)), 3 * 4096.0)
+    for d in range(3):
+        at = [n for n in range(M) if DEP[n] == d]
+        ms(c("t24", s(at[0], at[-1] + 1)), 4096.0 * d)
+        ts(c("cmp", s(at[0], at[-1] + 1)), c("t24", s(at[0], at[-1] + 1)), col("mdC", 66 + 2 * d), Op.add)
+    commit("Wf", lambda q: col("mdC", 66 + 2 * DEP[q]), c("mdC", s(0, 64)), "fin")
+    ts(col("v", 1), col("H", 0), 3.0, Op.is_equal)
+    ts(col("v", 2), col("mdD", 0), col("v", 1), Op.mult, col("fin", 16), Op.add)
+    dma("S", yt(2), col("v", 2), "dy2", 2.0)
+    dma("A", ("yx", (slice(None),)), c("fin", s(0, 16)), "dyx", 2.0)
+    return ops
+
+
+def plan():
+    ops = build()
+    n = len(ops)
+    lastw, readers, bank, group = {}, {}, {}, {}
+    deps, order = [set() for _ in ops], [set() for _ in ops]
+    for i, o in enumerate(ops):
+        for r in o["r"]:
+            w = lastw.setdefault(r[0], np.full(len(elems(c(r[0]))), -1))
+            deps[i].update(int(x) for x in np.unique(w[elems(r)]) if x >= 0)
+        for r in o["w"]:
+            e = elems(r)
+            w = lastw.setdefault(r[0], np.full(len(elems(c(r[0]))), -1))
+            deps[i].update(int(x) for x in np.unique(w[e]) if x >= 0)
+            keep = []
+            for j, mask in readers.get(r[0], []):
+                if mask[e].any():
+                    deps[i].add(j)
+                    mask[e] = False
+                if mask.any():
+                    keep.append((j, mask))
+            readers[r[0]] = keep
+            w[e] = i
+        for r in o["r"]:
+            mask = np.zeros(len(lastw[r[0]]), bool)
+            mask[elems(r)] = True
+            readers.setdefault(r[0], []).append((i, mask))
+        for name in {r[0] for r in o["r"] + o["w"] if SCRATCH[r[0]][0] == "psum"}:
+            b = bank.setdefault(name, [o["e"], [], []])
+            if b[0] != o["e"]:
+                b[0], b[1], b[2] = o["e"], [], b[1]
+            deps[i].update(b[2])
+            b[1].append(i)
+        if o["m"] == "mm":
+            name = o["w"][0][0]
+            if o["st"]:
+                order[i].update(group.get(name, [])[-1:])
+                group[name] = [i]
+            else:
+                order[i].update(group[name] if o["sp"] else group[name][:1])
+                group[name].append(i)
+        if "after" in o:
+            order[i].add(o["after"])
+        deps[i].discard(i)
+        if o["e"] == "T":
+            deps[i] = {j for j in deps[i] if ops[j]["e"] != "T"}
+    return arrange(ops, deps, order, BUMP)
+
+
+def arrange(ops, deps, order, bump):
+    n = len(ops)
+    gap = lambda j, i: ops[j]["lat"] + (0.0 if j in order[i] else PL["same"] if ops[j]["e"] == ops[i]["e"] else PL["cross"])
+    allp = [deps[i] | order[i] for i in range(n)]
+    succ = [[] for _ in ops]
+    for i in range(n):
+        for j in allp[i]:
+            succ[j].append(i)
+    prio = [0.0] * n
+    for i in range(n - 1, -1, -1):
+        prio[i] = bump.get(ops[i]["key"], 0.0) + ops[i]["c"] + max([gap(i, k) + prio[k] for k in succ[i]] + [ops[i]["lat"]])
+    left = [len(x) for x in allp]
+    rt, fin, free = [0.0] * n, [0.0] * n, {}
+    ready = {}
+    for i in range(n):
+        if not left[i]:
+            ready.setdefault(ops[i]["e"], []).append(i)
+    seq = []
+    while len(seq) < n:
+        te, e = min((max(free.get(e, 0.0), min(rt[i] for i in l)), e) for e, l in ready.items() if l)
+        i = max((i for i in ready[e] if rt[i] <= te + 0.04), key=lambda i: (prio[i], -i))
+        ready[e].remove(i)
+        fin[i] = max(te, rt[i]) + ops[i]["c"]
+        free[e] = fin[i]
+        seq.append(i)
+        for k in succ[i]:
+            rt[k] = max(rt[k], fin[i] + gap(i, k))
+            left[k] -= 1
+            if not left[k]:
+                ready.setdefault(ops[k]["e"], []).append(k)
+    return ops, deps, seq, fin, order
+
+
+PLAN = []
+
+
+def masks(topo, src, dsts):
+    out, used = {}, set()
+    todo = sorted(range(len(dsts)), key=lambda i: len(topo.engines(src, dsts[i])))
+    for pos, i in enumerate(todo):
+        can = [e for e in topo.engines(src, dsts[i]) if e not in used]
+        rivals = sum(1 for j in todo[pos:] if set(topo.engines(src, dsts[j])) <= set(topo.engines(src, dsts[i])))
+        k = len(can) // rivals
+        k = 1 << (k.bit_length() - 1)
+        out[i] = can[:k]
+        used.update(can[:k])
+    return [out[i] for i in range(len(dsts))]
+
+
+def rank_program(g, core, T, topo):
+    rank = T.rank_of(core)
+    if rank is None:
+        return
+    if not PLAN:
+        PLAN.append(plan())
+    ops, deps, seq = PLAN[0][:3]
+    queue = {"V": g.vector, "A": g.scalar, "T": g.tensor, "G": g, "S": g.sync}
+    call = {
+        "cp": lambda a, k: g.vector.tensor_copy(*a), "tt": lambda a, k: g.vector.tensor_tensor(*a),
+        "ts": lambda a, k: g.vector.tensor_scalar(*a), "red": lambda a, k: g.vector.tensor_reduce(*a),
+        "trn": lambda a, k: g.vector.transpose(*a), "ms": lambda a, k: g.vector.memset(*a),
+        "scan": lambda a, k: g.vector.tensor_tensor_scan(*a), "act": lambda a, k: g.scalar.activation(*a, **k),
+        "mm": lambda a, k: g.tensor.matmul(*a), "iota": lambda a, k: g.iota(*a, **k), "sel": lambda a, k: g.affine_select(*a),
+    }
+
+    def ap(r):
+        if not isinstance(r, tuple):
+            return r
+        if r[0] == "*":
+            return ap(r[1]).indirect(ap(r[2]))
+        return T[r[0]][r[1]]
+
+    peer = lambda r, off: T.cores[(r + off) % N]
+    needed = set()
+    for d in deps:
+        needed.update(d)
+    count, mark, known, total = {}, {}, {e: {} for e in queue}, {}
+    for i in seq:
+        o = ops[i]
+        e = o["e"]
+        if e == "R":
+            parts, k = o["a"]
+            sender = (rank - parts[k][0]) % N
+            n = len(masks(topo, T.cores[sender], [peer(sender, x[0]) for x in parts])[k])
+            mark[i] = (o["sem"], n, {})
+            total[o["sem"]] = n
+            continue
+        want = {}
+        for j in deps[i]:
+            if j in mark and mark[j][1] > want.get(mark[j][0], (0,))[0]:
+                want[mark[j][0]] = mark[j][1:]
+        for sem, (val, clock) in sorted(want.items(), key=lambda z: -len(z[1][1])):
+            if known[e].get(sem, 0) < val:
+                queue[e].wait_ge(T.sem[sem], val)
+                known[e][sem] = val
+            for s2, v2 in clock.items():
+                known[e][s2] = max(known[e].get(s2, 0), v2)
+        if o["m"] == "send":
+            dsts = [peer(rank, x[0]) for x in o["a"]]
+            trs = []
+            for x, d, eng in zip(o["a"], dsts, masks(topo, core, dsts)):
+                rid, pid = topo.addr(d)[:2]
+                trs.append((ap(x[2]), ap(x[1]), T.sem[x[3]], pid, rid, sum(1 << b for b in eng)))
+                total["left"] = total.get("left", 0) + len(eng)
+            if len(trs) == 1:
+                dst, src, sem, pid, rid, m = trs[0]
+                g.remote_dma(dst, src, sem, T.sem.left, pid, rid, m)
+            else:
+                g.remote_dma_fused([RemoteDMATransfer(dst_ids=[DstId(rid=rid, pnc=pid)], dma_engine_mask=m, remote_sem=sem, src=src, dst=dst)
+                                    for dst, src, sem, pid, rid, m in trs], local_sem=T.sem.left)
+        elif o["m"] == "dma":
+            queue[e].dma_start(ap(o["a"][0]), ap(o["a"][1])).then_inc(T.sem[o["sem"]], 16)
+            mark[i] = (o["sem"], 16, dict(known[e]))
+            total[o["sem"]] = 16
+        else:
+            ins = call[o["m"]]([ap(x) for x in o["a"]], {k: ap(x) for k, x in o["k"].items()})
+            if i in needed:
+                count[e] = count.get(e, 0) + 1
+                ins.then_inc(T.sem["e" + e], 1)
+                mark[i] = ("e" + e, count[e], dict(known[e]))
+                total["e" + e] = count[e]
+    for sem, val in total.items():
+        if known["G"].get(sem, 0) < val:
+            g.wait_ge(T.sem[sem], val)

@@ -5,28 +5,11 @@ from concourse.mybir import AluOpType as Op, AxisListType, ActivationFunctionTyp
 N, V, M = 8, 3712, 24
 PAR = [0, 0, 0, 0, 0, 0, 0, 0, 0, 1, 1, 1, 2, 2, 2, 3, 3, 5, 5, 9, 9, 12, 12, 15]
 ROW = [0, 0, 1, 2, 3, 4, 5, 6, 7, 0, 8, 9, 0, 10, 11, 0, 12, 13, 14, 0, 15, 0, 1, 0]
-DEP = [0] * M
-for _n in range(1, M):
-    DEP[_n] = DEP[PAR[_n]] + 1
 INNER = sorted(set(PAR))
+DEPTH = [(1, 9), (9, 19), (19, 24)]
 MID = 1856
-CH = 8
-
-_A, _B, _C, _D, _E, _F = [0, 1, 2, 3], [4, 5, 6, 7], [0, 1, 4, 5], [2, 3, 6, 7], [0, 2, 4, 6], [1, 3, 5, 7]
-NET = [
-    [("max", 0, _A + _B, _A + _B, _A + _B), ("min", 1, _A + _B, _A + _B, _A + _B)],
-    [("max", 0, _B, _A, _B), ("min", 0, _A, _B, _A), ("max", 1, _A, _B, _D), ("min", 1, _B, _A, _C)],
-    [("max", 0, _C, _A, _C), ("min", 0, _C, _A, _D), ("max", 1, _D, _B, _D), ("min", 1, _D, _B, _C)],
-    [("max", 0, _A, _B, _F), ("min", 0, _B, _A, _E), ("max", 1, _B, _A, _F), ("min", 1, _A, _B, _E)],
-    [("max", 0, _B, _B, _D), ("min", 0, _A, _A, _C), ("max", 1, _A, _A, _D), ("min", 1, _B, _B, _C)],
-    [("max", 0, _B, _B, _F), ("min", 0, _B, _B, _E), ("max", 1, _A, _A, _E), ("min", 1, _A, _A, _F)],
-    [("max", 0, [2, 3], [4, 5], [2, 3]), ("max", 0, [4, 5], [2, 3], [6, 7]), ("min", 0, [6, 7], [0, 1], [0, 1]),
-     ("min", 0, [0, 1], [6, 7], [4, 5]), ("max", 1, [6, 7], [0, 1], [4, 5]), ("max", 1, [0, 1], [6, 7], [6, 7]),
-     ("min", 1, [2, 3], [4, 5], [0, 1]), ("min", 1, [4, 5], [2, 3], [2, 3])],
-    [("max", 0, _B, _C, _A), ("min", 0, _B, _C, _B), ("max", 1, _A, _D, _A), ("min", 1, _A, _D, _B)],
-    [("max", 0, _E, _E, _E), ("min", 0, _F, _F, _F), ("max", 1, _F, _F, _E), ("min", 1, _E, _E, _F)],
-    [("max", 2, _D, _D, _E), ("max", 2, _C, _C, [8, 10, 12, 14]), ("min", 2, _D, _D, _F), ("min", 2, _C, _C, [9, 11, 13, 15])],
-]
+HIGH = 2.0 ** 24
+STEP = 2.0 ** 17
 
 F32, BF, H16, I32, U16 = "float32", "bfloat16", "float16", "int32", "uint16"
 SCRATCH = {}
@@ -37,29 +20,29 @@ def _decl(where, dtype, **shapes):
         SCRATCH[name] = (where, [128] + list(shape), dtype)
 
 
-_decl("sbuf", I32, Q=[V], A=[V + 384], tokI=[4], lane=[4], li=[4], bci=[16], H=[4], H2=[4], srt=[24, 4, 4], srm=[24, 16], topi=[24], topm=[24])
-_decl("sbuf", BF, K=[V], kc=[5120], geA=[5120], geB=[1024], gec=[256], colg=[128], colb=[128], cm=[128], SelT=[4, 128], Gm=[8], tie=[24, 16],
-      IdB=[128], own=[64], i4=[64], mid=[192], ones=[128], Mi=[384], Eq=[24, 16 * CH], kns=[384], knl=[384])
-_decl("sbuf", H16, Mk=[384], Id=[8, 16], Iev=[128], Iod=[128], Sel=[16, 128], G=[8, 128], Wh=[24], candh=[384], srh=[24, 16], E=[3, 8, 8], ch=[32], cT=[32])
-_decl("sbuf", U16, bc=[16], parl=[36], sell=[12], rootd=[2], dup3=[16], Ws0=[32], Ws1=[32], Ws2=[48], Wl0=[24], Wl1=[24], Wl2=[24], cand=[384],
-      Os0=[384], Os1=[384], Ol0=[384], Ol1=[384], L=[24], bl=[2], CT=[8], cu=[32])
-_decl("sbuf", F32, kp=[4], sc=[12], cnt=[24], z4=[4], m4=[4], i16=[16], d16=[16], n8=[8],
-      RR=[96], Rm=[96], Rs=[8], PR=[36], trash=[24], cmpN=[24], Tt=[288], Gt=[256], Wf=[24], Wc=[24], Vc=[24], t24=[24], u24=[24], ok=[24], cmp=[24], mm=[24],
-      v=[4], v2=[2], x0s=[16], mv0=[16], mv1=[20], mv2=[20], md0=[20], md1=[20], ms0=[20], ms1=[20], CX=[72], mdC=[72], c4=[4], mdD=[4], fin=[20], chx=[16], thc=[256],
-      xn=[384], xh=[256], kn=[384], thb=[1024], S0=[24, 2, 4], S1=[24, 2, 4], S2=[24, 2, 4], tr4=[24, 4], tr2=[24, 2])
-_decl("psum", F32, comp=[64, 2, 4], comq=[64, 2, 4], P=[64, 2, 4], back=[512], rep=[512], th=[512], tw=[512], req=[512])
-SC = ["lf", "l16", "grp", "odd", "l4", "evn", "o16", "g4", "nkp", "tokf"]
+_decl("sbuf", I32, Q=[V], A=[V + 64], lane=[12], H=[8], Pi=[80], Pj=[80], Ti=[24], Tj=[24])
+_decl("sbuf", BF, K=[V], kc=[6144], ge=[16, 384], gec=[256], colb=[128], cm=[128], SelT=[4, 128], Ge=[144], tie=[64], depb=[24],
+      IdB=[128], own=[64], mid=[64], ones=[128], B3=[128], Ea=[224], Eb=[512], kns=[384], knl=[384])
+_decl("sbuf", H16, Mk=[512], Id=[128], Pk=[4, 128], Sel=[16, 128], Wx=[96], Wy=[96], E=[24], ch=[32], cT=[32], candh=[384])
+_decl("sbuf", U16, bc=[16], parl=[24], sell=[20], l17=[6], pairs=[4], rootd=[2], rootv=[2], Ws0=[48], Ws1=[48], Ws2=[48], Wp1=[16], Wq1=[16], Wp2=[16], Wq2=[16],
+      Wl0=[26], Wl1=[26], Wl2=[26], cand=[384], L=[24], bl=[2], CT=[8], cu=[32])
+_decl("sbuf", F32, sc=[16], z4=[4], m4=[4], i16=[16], d16=[16], sg=[4], wide=[144], RR=[224], Rm=[224], Rn=[224], Rz=[224],
+      PR=[24], Tt=[288], Gt=[256], t24=[24], u24=[24], w24=[24], mn=[24], trash=[24], Wf=[24], Z=[28], tf=[12], dep=[24], g8=[24], ok=[24], cmp=[24], mm=[24], Kt=[384], Km=[384], RS=[160], v=[8], x0s=[20], mv0=[20], mv1=[20], mv2=[20],
+      md0=[20], md1=[20], md2=[20], ms0=[20], ms1=[20], ms2=[20], CX=[64], chx=[16], thc=[256], xn=[384], xh=[256], kn=[384],
+      RL=[68], RT=[32], X2=[80], S1=[272], S2=[656], S3=[164], Os0=[384], Os1=[384], Ol0=[384], Ol1=[384])
+_decl("psum", F32, kA=[512], kB=[512], kC=[512], thA=[512], thB=[512], tw=[512], dif=[512], cnt=[512])
+SC = ["lf", "l16", "grp", "odd", "l4", "evn", "o16", "g4", "nkp", "tokf", "g16", "look", "place", "back", "", "", "kp"]
+SCRATCH["sc"] = ("sbuf", [128, 20], F32)
 
 DMAS = ["dtok", "dx0", "dkap", "dQ", "dK", "dA", "dy0", "dy1", "dy2", "dyx", "dn0", "dn1"]
-MSGS = ["rx0", "rWa0", "rWb0", "rWa1", "rWb1", "rWa2", "rWb2", "rOa0", "rOb0", "rOa1", "rOb1", "rd0", "rd1", "rv1", "rv2", "rC", "rD", "rka", "rkb", "rkc", "rWc2", "rOc0", "rOc1"]
+MSGS = ["rx0", "rd0", "rd1", "rd2", "rv1", "rv2", "rka", "rkb", "rkc"] + ["r%s%d%d" % (m, t, j) for m in "WO" for t in range(3) for j in range(5)]
 SEMAPHORES = ["eV", "eA", "eT", "eG", "left"] + DMAS + MSGS
 
-PL = dict(cyc=1.04e-3, gather=1.56, scatter=3.8, hop=2.4, pe=1.04e-3, issue=0.3, byte=1.2e-3, same=0.06, cross=0.1)
-OCUT = [0, 128, 384]
-NV = 6
-BUMP = {'v0.kn': 6, 'v1.kn': 6, 'm1.tr4': 2.8, 'm1.ms1': 2.5, 'v1.geA': 1.9, 'h.rC': 2.0, 'm0.cmp': 1.7, 'c.Mi': 1.7, 'v1.thb': 2.5, 'v0.thb': 2.5,
-        'v0.xh': 2.9, 'v1.back': 1.9, 'c.i4': 0.4, 'v0.rOa0': 2.5, 'm0.md0': 0.2, 'm0.E': 1.7, 'h.cT': 0.9, 'c.Q': -0.1, 'm1.mm': -1.4, 'v1.srh': 0.2,
-        'm1.rd1': 2.7, 'v1.S0': -0.1, 'm2.ok': -0.4, 'm1.cmp': -2.3, 'm0.tw': 0.2, 'c.G': -0.2, 'v0.geB': -3.0, 'm2.bl': -0.5, 'h.chx': 1.5, 'd2.Ws2': 0.7}
+PL = dict(cyc=0.83e-3, gather=1.56, scatter=3.8, hop=1.6, pe=0.83e-3, issue=0.3, byte=1.2e-3, same=0.24, cross=0.15, look=0.04, passes=800)
+CHAINS = (2,)
+PIECES = [(0, 8), (8, 16), (16, 24)]
+CHUNKS = [(0, 4), (4, 8), (8, 12), (12, 16), (16, 20), (20, 24)]
+GATHERS = [(0, 1, "V"), (1, 3, "V"), (3, 5, "A"), (5, 9, "A"), (9, 12, "A"), (12, 16, "A"), (16, 19, "A"), (19, 21, "V"), (21, 24, "A")]
 
 
 def c(name, *idx):
@@ -78,18 +61,15 @@ def ind(win, off):
     return ("*", win, off)
 
 
-def cube(name, wires, rows=slice(0, 24)):
-    def ax(vals):
-        vals = sorted(set(vals))
-        if len(vals) == 1:
-            return slice(vals[0], vals[0] + 1)
-        return slice(vals[0], vals[-1] + 1, vals[1] - vals[0])
-    return c(name, rows, ax([w // 4 for w in wires]), ax([w % 4 for w in wires]))
-
-
 def elems(r):
-    shape = SCRATCH[r[0]][1][1:]
-    return np.arange(int(np.prod(shape))).reshape(shape)[r[1][1:]].reshape(-1)
+    key = (r[0], str(r[1][1:]))
+    if key not in ELEMS:
+        shape = SCRATCH[r[0]][1][1:]
+        ELEMS[key] = np.arange(int(np.prod(shape))).reshape(shape)[r[1][1:]].reshape(-1)
+    return ELEMS[key]
+
+
+ELEMS = {}
 
 
 def build():
@@ -115,9 +95,9 @@ def build():
 
     def vcost(out, ins, two=False):
         if out[0] == "*":
-            return 0.06 + SCATTER * CYC * 16 * len(elems(out[2]))
+            return 0.05 + SCATTER * CYC * 16 * len(elems(out[2]))
         if ins[0][0] == "*":
-            return 0.06 + GATHER * CYC * len(elems(out))
+            return 0.05 + GATHER * CYC * len(elems(out))
         n = len(elems(ins[0]))
         if two:
             n *= 1 if "psum" in (SCRATCH[ins[0][0]][0], SCRATCH[ins[1][0]][0]) else 2
@@ -129,18 +109,17 @@ def build():
     def tt(out, a, b, op): add("V", "tt", [out, a, b, op], [out], [a, b], vcost(out, [a, b], True))
     def ts(out, a, s1, op0, s2=None, op1=None):
         add("V", "ts", [out, a, s1, s2, op0] + ([op1] if op1 is not None else []), [out], [a, s1, s2], vcost(out, [a]))
-    def red(out, a, op): add("V", "red", [out, a, AxisListType.X, op], [out], [a], vcost(out, [a]))
+    def red(out, a, op, **kw): add("V", "red", [out, a, AxisListType.X, op], [out], [a], vcost(out, [a]), kw)
     def trn(out, a): add("V", "trn", [out, a], [out], [a], vcost(out, [a]))
     def ms(out, val): add("V", "ms", [out, val], [out], [], vcost(out, [out]))
     def scan(out, a, b, init, op0, op1): add("V", "scan", [out, a, b, init, op0, op1], [out], [a, b], vcost(out, [a, b]))
-    def act(out, a, bias=None, fn=AF.Identity):
+    def act(out, a, fn=AF.Copy, **kw):
         n = vcost(out, [a]) if a[0] == "*" else max(64, len(elems(a))) * CYC
-        add("A", "act", [out, a, fn if bias else AF.Copy], [out], [a, bias], n + 0.02, {"bias": bias} if bias else None)
+        add("A", "act", [out, a, fn], [out], [a] + list(kw.values()), n + 0.015, kw)
     def mmul(out, l, r, st, sp): add("T", "mm", [out, l, r, st, sp], [out], [l, r], max(64, len(elems(r))) * PL["pe"], st=st, sp=sp)
     def iota(out, pat, base, cmul):
         kw = {} if SCRATCH[out[0]][2] == I32 else {"allow_small_or_imprecise_dtypes": True}
-        add("G", "iota", [out, pat, base, cmul], [out], [], 0.16 + 2 * CYC * len(elems(out)), kw)
-    def pcopy(out, a, pat): add("G", "sel", [out, a, pat, Op.is_gt, 0.0, 1, 0], [out], [a], 0.21 + 2 * CYC * len(elems(out)))
+        add("G", "iota", [out, pat, base, cmul], [out], [], 0.14 + 2 * CYC * len(elems(out)), kw)
     def dma(q, out, a, sem, lat, behind=None): add(q, "dma", [out, a], [out], [a, behind], 0.06, sem=sem, lat=lat)
     def send(parts):
         nb = len(elems(parts[0][1])) * (4 if SCRATCH[parts[0][1][0]][2] in (F32, I32) else 2)
@@ -148,316 +127,370 @@ def build():
         me = len(ops) - 1
         for i, x in enumerate(parts):
             add("R", "recv", [parts, i], [x[2]], [], 0.0, sem=x[3], after=me, lat=HOP + nb * PL["byte"])
+    def fill(name, vals, at=0):
+        j = 0
+        while j < len(vals):
+            e = j + 1
+            while e < len(vals) and vals[e] == vals[j]:
+                e += 1
+            ms(c(name, s(at + j, at + e)), float(vals[j]))
+            j = e
 
-    col = lambda name, j: c("sc", s(SC.index(name), SC.index(name) + 1)) if name in SC else c(name, s(j, j + 1))
+    col = lambda name, j=0: c("sc", s(SC.index(name), SC.index(name) + 1)) if name in SC else c(name, s(j, j + 1))
+    cols = lambda a, b: s(16 * a, 16 * b)
     Kw, Qw, Aw = c("K"), c("Q"), c("A", s(0, V))
 
-    dma("A", col("tokI", 0), ("tok", (slice(None),)), "dtok", 2.0)
-    dma("A", c("x0s"), ("x0", (slice(None),)), "dx0", 2.0)
-    dma("A", col("kp", 0), ("kap", (slice(None),)), "dkap", 2.0)
+    dma("A", col("lane", 8), ("tok", (slice(None),)), "dtok", 2.0)
+    dma("A", c("x0s", s(0, 16)), ("x0", (slice(None),)), "dx0", 2.0)
+    dma("A", col("kp"), ("kap", (slice(None),)), "dkap", 2.0)
     dma("S", Qw, ("qt", (slice(None),)), "dQ", 7.0)
     dma("S", Kw, ("kt", (slice(None),)), "dK", 9.5)
-    send([(1, c("x0s"), c("mv0"), "rx0")])
+    ops[-1]["after"] = len(ops) - 2
 
     iota(col("lane", 0), [[0, 1]], 0, 1)
     iota(c("i16"), [[1, 16]], 0, 0)
-    iota(c("colb"), [[1, 128]], 0, 0)
-    iota(c("colg"), [[1, 8], [0, 16]], 0, 0)
-    iota(c("bci"), [[1, 16]], 0, 0)
-    iota(c("trash"), [[16, 24]], V, 0)
-    iota(c("cmpN"), [[4096, 24]], MID, 0)
-    iota(c("Mi"), [[0, 24], [1, 16]], 0, 0)
-    iota(c("i4"), [[1, 4], [0, 16]], 0, 0)
+    iota(c("wide"), [[1, 144]], -15, 0)
+    iota(c("Ea"), [[0, 14], [1, 16]], 0, 0)
+    iota(c("Eb"), [[0, 8], [32, 4], [1, 16]], 0, 0)
+    iota(c("trash"), [[0, 6], [16, 4]], V, 0)
+    iota(c("own"), [[1, 4], [0, 16]], 0, 0)
     iota(c("cm"), [[1, 32], [0, 4]], 0, 0)
-    iota(p("tie", 0, 1), [[0, 24], [-4096, 16]], 15 * 4096, 0)
-    cp(col("lf", 0), col("lane", 0))
-    for j, (sh, an, name) in enumerate([(0, 15, "l16"), (4, 7, "grp"), (4, 1, "odd"), (0, 3, "l4")]):
-        ts(col("li", j), col("lane", 0), sh, Op.arith_shift_right, an, Op.bitwise_and)
-        cp(col(name, 0), col("li", j))
-    l16, grp = col("l16", 0), col("grp", 0)
-    ts(col("evn", 0), col("odd", 0), -1.0, Op.mult, 1.0, Op.add)
-    ts(col("o16", 0), col("odd", 0), 16.0, Op.mult)
-    ts(col("g4", 0), grp, 4.0, Op.mult)
-    ts(c("d16"), c("i16"), l16, Op.is_equal)
-    ms(c("z4"), 0.0); ms(c("m4"), -float(MID)); ms(c("Tt"), 0.0); ms(col("ok", 0), 1.0)
-    child = lambda n: 32 + 32 * INNER.index(PAR[n]) + ROW[n] if n else 0
-    lists = [[child(n) for n in (1, 1, 2, 2, 3, 3, 5, 5)] + [child(n) for n in range(8)],
-             [child(n) - 64 for n in (9, 9, 12, 12, 15, 15)] + [0] * 10,
-             [child(n) for n in range(8, 24)],
-             [child(n) for n in (1, 1, 2, 2, 3, 3, 5, 5)] + [child(n) for n in range(1, 9)],
-             [child(n) - 64 for n in list(range(9, 19)) + [9, 9, 12, 12, 15, 15]],
-             [child(n) - 192 for n in range(19, 24)] + [0] * 11]
-    flat = sum(lists, [])
-    j = 0
-    while j < 96:
-        e = j
-        while e < 96 and flat[e] == flat[j] and e // 16 == j // 16:
-            e += 1
-        ms(c("RR", s(j, e)), float(flat[j]))
-        j = e
-    for j in range(6):
-        tt(c("Rm", s(16 * j, 16 * j + 16)), c("RR", s(16 * j, 16 * j + 16)), c("d16"), Op.mult)
-        red(col("Rs", j), c("Rm", s(16 * j, 16 * j + 16)), Op.add)
-        ts(col("sell", 2 * j), col("Rs", j), col("o16", 0), Op.add)
-    pr = [0] * 8 + [16 * PAR[n] for n in range(8, 19)] + [0] + [16 * (PAR[n] - 8) for n in range(19, 24)] + [0]
-    pr += [16 * PAR[n] for n in range(9, 19)]
-    j = 0
-    while j < 36:
-        e = j
-        while e < 36 and pr[e] == pr[j]:
-            e += 1
-        ms(c("PR", s(j, e)), float(pr[j]))
-        j = e
+    iota(c("B3"), [[1, 8], [0, 16]], 0, 0)
+    iota(p("tie", 0, 1), [[0, 4], [-4096, 16]], 15 * 4096, 0)
+    iota(c("depb"), [[1, 24]], 0, 0)
+    ts(c("dep"), c("depb"), STEP, Op.mult)
+    cp(c("depb"), c("dep"))
+    cp(col("lf"), col("lane", 0))
+    for j, (sh, an) in enumerate([(0, 15), (4, 7), (4, 1), (0, 3)]):
+        ts(col("lane", 1 + j), col("lane", 0), sh, Op.arith_shift_right, an, Op.bitwise_and)
+    cp(c("sc", s(1, 5)), c("lane", s(1, 5)))
+    l16, grp = col("l16"), col("grp")
+    ts(col("evn"), col("odd"), -1.0, Op.mult, 1.0, Op.add)
+    ts(col("o16"), col("odd"), 16.0, Op.mult)
+    ts(col("g4"), grp, 4.0, Op.mult)
+    ts(col("g16"), grp, 16.0, Op.mult)
+    ts(col("place"), l16, -4096.0, Op.mult, 15 * 4096.0, Op.add)
+    ts(col("back"), col("place"), float(MID), Op.add)
+    ts(col("look"), col("odd"), 2.0 ** 22, Op.mult, col("place"), Op.add)
+    ms(c("z4"), 0.0); ms(c("m4"), -float(MID)); ms(col("ok", 0), 1.0); ms(col("tf", 3), 0.0)
+    ms(c("RS"), HIGH); ms(c("RS", s(0, 160, 16)), 0.0)
+    cp(col("tokf"), col("lane", 8))
+    ts(c("x0s", s(16, 20)), c("z4"), col("tokf"), Op.add)
+    send([(1, c("x0s"), c("mv0"), "rx0")])
+    ts(col("nkp"), col("kp"), -1.0, Op.mult)
+    lane = lambda n: ([1, 2, 3, 5] if n < 19 else [12, 9, 15]).index(PAR[n])
+    pick = lambda j: col("sell", 2 * j)
+
+    def entries(a, b):
+        ts(c("Rm", s(a, b)), c("Ea", s(a, b)), l16, Op.is_equal)
+        tt(c("RR", s(a, b)), c("RR", s(a, b)), c("Rm", s(a, b)), Op.mult)
+        ts(c("Rn", s(a, b)), c("Ea", s(a, b)), 0.5, Op.is_gt)
+        scan(c("Rz", s(a, b)), c("Rn", s(a, b)), c("RR", s(a, b)), 0.0, Op.mult, Op.add)
+
+    iota(c("RR", s(0, 6)), [[1, 3], [0, 2]], 0, 0)
+    iota(c("RR", s(8, 16)), [[1, 8]], 0, 0)
+    fill("RR", [4, 4], 6)
+    fill("RR", [32 * lane(n) + ROW[n] for n in range(9, 19)] + [32, 32, 0, 0, 64, 64], 16)
+    fill("RR", [32 * lane(n) + ROW[n] for n in range(19, 24)] + [64] * 11, 32)
+    entries(0, 48)
+    ts(c("sell", s(0, 6, 2)), c("Rz", s(15, 48, 16)), col("o16"), Op.add)
+    iota(c("RR", s(48, 133)), [[32, 5], [1, 17]], 0, 0)
+    fill("RR", [96 + 70 * (ROW[n] - 8) + 17 * lane(n) + 16 if ROW[n] else 32 * lane(n) + 15 for n in range(9, 19)] + [15] * 6, 128)
+    fill("RR", [{0: 16 + 32 * lane(n), 1: 115, 15: 147}[ROW[n]] for n in range(19, 24)] + [80] * 11, 144)
+    iota(c("RR", s(160, 192)), [[1, 8], [1, 4]], 0, 0)
+    iota(c("RR", s(192, 224)), [[1, 8], [0, 4]], 0, 0)
+    ts(c("RR", s(160, 176)), c("RR", s(160, 176)), 3.0, Op.min)
+    ts(c("RR", s(176, 192)), c("RR", s(176, 192)), 7.0, Op.min)
+    entries(48, 224)
+    ts(c("l17", s(0, 5)), c("Rz", s(63, 128, 16)), col("o16"), Op.add)
+    ts(col("sg", 0), col("Rz", 15), 34.0, Op.mult, 16.0, Op.add)
+    ts(pick(3), col("sg", 0), col("o16"), Op.add)
+    ts(col("sg", 1), col("sg", 0), 34.0 * 4 + 16, Op.min)
+    ts(pick(7), col("sg", 1), col("o16"), Op.add)
+    ts(col("sg", 2), col("Rz", 143), 96.0, Op.is_lt, col("o16"), Op.mult)
+    ts(pick(4), col("Rz", 143), col("sg", 2), Op.add)
+    ts(pick(5), col("Rz", 159), col("o16"), Op.add)
+    ts(pick(6), pick(1), 15.0, Op.add, 95.0, Op.min)
+    cp(c("pairs"), c("Rz", s(175, 224, 16)))
+    fill("PR", [16 * PAR[n] for n in range(1, 19)] + [16 * (PAR[n] - 8) for n in range(19, 24)] + [112])
     ts(c("parl"), c("PR"), l16, Op.add)
-    cp(c("bc"), c("bci"))
-    ts(c("trash"), c("trash"), l16, Op.add)
-    ts(c("Mk"), c("Mi"), l16, Op.is_le, 8192.0, Op.mult)
-    ts(c("own"), c("i4"), col("l4", 0), Op.is_equal, 2.0 ** 21, Op.mult)
-    ts(c("IdB"), c("colb"), col("lf", 0), Op.is_equal)
-    ts(c("n8"), c("i16", s(0, 8)), grp, Op.is_equal)
-    ts(c("Gm"), c("i16", s(0, 8)), grp, Op.is_equal, 65536.0, Op.mult)
+    cp(c("bc"), c("i16"))
+    cp(c("colb"), c("wide", s(15, 143)))
+    ts(c("Mk"), c("Eb"), l16, Op.is_le, 8192.0, Op.mult)
+    ts(c("own"), c("own"), col("l4"), Op.is_equal, 2.0 ** 21, Op.mult)
+    ts(c("IdB"), c("colb"), col("lf"), Op.is_equal)
+    ts(c("Id"), c("colb"), col("lf"), Op.is_equal)
+    ts(c("Ge"), c("wide"), col("g16"), Op.is_equal, 2.0 ** 17, Op.mult)
     ms(p("mid", 0, 1), float(MID)); ms(p("ones", 0, 1), 1.0)
-    ts(c("Id"), c("colb"), col("lf", 0), Op.is_equal)
-    ts(c("Iev"), c("colb"), col("lf", 0), Op.is_equal, col("evn", 0), Op.mult)
-    ts(c("Iod"), c("colb"), col("lf", 0), Op.is_equal, col("odd", 0), Op.mult)
-    ts(c("cm"), c("cm"), col("g4", 0), Op.subtract)
-    for j in range(16):
-        ts(c("Sel", j), c("colg"), grp, Op.is_equal, col("d16", j), Op.mult)
-    for j in range(8):
-        ts(c("G", j), c("colb"), l16, Op.subtract, 16.0 * j, Op.is_equal)
+    ts(c("colb"), c("colb"), col("lf"), Op.subtract)
+    for j, (shift, who) in enumerate([(0, "evn"), (-16, "odd"), (16, "evn"), (0, "odd")]):
+        ts(c("Pk", j), c("colb"), float(shift), Op.is_equal, col(who), Op.mult)
+    ts(c("cm"), c("cm"), col("g4"), Op.subtract)
     for j in range(4):
         ts(c("SelT", j), c("cm"), float(j), Op.is_equal, 65536.0, Op.mult)
-    ts(col("nkp", 0), col("kp", 0), -1.0, Op.mult)
-    cp(col("tokf", 0), col("tokI", 0))
-    kp = col("kp", 0)
+    ts(c("d16"), c("i16"), l16, Op.is_equal)
+    for j in range(16):
+        ts(c("Sel", j), c("B3"), grp, Op.is_equal, col("d16", j), Op.mult)
+    ts(c("trash"), c("trash"), l16, Op.add)
+    ms(c("RL"), 0.0); ms(c("RL", s(16, 68, 17)), HIGH); ms(c("RT"), 0.0); ms(c("RT", s(0, 32, 16)), HIGH)
+    ms(c("S1", s(0, 272, 34)), 0.0); ms(c("S1", s(33, 272, 34)), 0.0); ms(c("S2", s(96, 656, 70)), HIGH); ms(c("S2", s(165, 656, 70)), 0.0)
+    ms(col("S3", 0), 0.0); ms(c("S3", s(97, 100)), 0.0); ms(c("Tt", s(256, 288)), 0.0)
 
-    def draft(t, root):
-        tab, W = (Qw if t == 0 else Aw), "Ws%d" % t
-        ts(c("rootd"), c("z4", s(0, 2)), root, Op.add)
-        ts(c("Tt", s(0, 32, 16)), c("z4", s(0, 2)), root, Op.add)
-        cp(c("Gt", s(0, 32)), ind(tab, c("rootd")))
-        trn(c("Tt", s(32, 64)), c("Gt", s(0, 32)))
-        if t == 2:
-            cp(c(W, s(0, 16)), ind(c("Tt", s(0, 64)), col("sell", 6)))
-            send([(3, c(W, s(8, 16)), c("Wl2", s(0, 8)), "rWa2")])
-            cp(c("Gt", s(32, 160)), ind(tab, c(W, s(0, 8))))
-            trn(c("Tt", s(64, 192)), c("Gt", s(32, 160)))
-            cp(c(W, s(16, 32)), ind(c("Tt", s(64, 192)), col("sell", 8)))
-            send([(3, c(W, s(16, 26)), c("Wl2", s(8, 18)), "rWb2")])
-            cp(c("Gt", s(160, 256)), ind(tab, c(W, s(26, 32))))
-            trn(c("Tt", s(192, 288)), c("Gt", s(160, 256)))
-            cp(c(W, s(32, 48)), ind(c("Tt", s(192, 288)), col("sell", 10)))
-            send([(3, c(W, s(32, 38)), c("Wl2", s(18, 24)), "rWc2")])
-            return
-        cp(c(W, s(0, 16)), ind(c("Tt", s(0, 64)), col("sell", 0)))
-        send([(1 + t, c(W, s(8, 16)), c("Wl%d" % t, s(0, 8)), "rWa%d" % t)])
-        cp(c("Gt", s(32, 160)), ind(tab, c(W, s(0, 8))))
-        trn(c("Tt", s(64, 192)), c("Gt", s(32, 160)))
-        cp(c("dup3"), ind(c("Tt", s(64, 192)), col("sell", 2)))
-        cp(c("Gt", s(160, 256)), ind(tab, c("dup3", s(0, 6))))
-        trn(c("Tt", s(192, 288)), c("Gt", s(160, 256)))
-        cp(c(W, s(16, 32)), ind(c("Tt"), col("sell", 4)))
-        send([(1 + t, c(W, s(16, 32)), c("Wl%d" % t, s(8, 24)), "rWb%d" % t)])
+    SPAN = [(0, 32), (128, 256), (32, 128)]
+    WS = [(0, 16), (16, 32), (32, 48)]
 
-    def dedupe(t):
-        W = c("Ws%d" % t, s(8, 32))
-        ts(c("Wh"), W, -float(MID), Op.add)
-        ts(c("Wc"), W, -1.0, Op.mult, float(MID), Op.add)
-        cp(c("Wf"), W)
-        mmul(c("req", s(0, 384)), c("Id"), c("Mk"), True, False)
-        for j in range(16):
-            mmul(c("req", s(j, 384, 16)), c("Sel", j), c("Wh"), False, j == 15)
-        for j in range(16):
-            mmul(c("rep", s(j, 384, 16)), c("Sel", j), c("Wh"), True, True)
-        for a in range(24):
-            w = 16 * (CH - a % CH)
-            act(c("Eq", a, s(0, 16)), c("req", s(16 * a, 16 * a + 16)), col("Wc", a), AF.Abs)
-            if w > 16:
-                act(c("Eq", a, s(16, w)), c("rep", s(16 * a + 16, 16 * a + w)), col("Wc", a), AF.Abs)
-            e = c("Eq", a, s(0, w))
-            add("A", "act", [e, e, AF.Relu], [e, col("cnt", a)], [e], max(64, w) * CYC + 0.04,
-                {"bias": 4096.0, "scale": -4096.0, "accum_out": col("cnt", a)})
-        tt(c("t24"), c("cnt"), c("trash"), Op.min)
-        tt(c("u24"), c("t24"), c("Wf"), Op.max)
-        cp(c("L"), c("u24"))
+    def ship(t, level, W=None):
+        a, b, at = [(8, 16, 2), (16, 26, 10), (32, 38, 20), (8, 12, 2), (12, 16, 6)][level]
+        send([(1 + t, c(W or "Ws%d" % t, s(a, b)), c("Wl%d" % t, s(at, at + b - a)), "rW%d%d" % (t, level))])
+
+    def draft0():
+        cp(c("rootd"), c("x0s", s(16, 18)))
+        for level, twice in enumerate((c("rootd"), c("Ws0", s(0, 8)), c("Ws0", s(26, 32)))):
+            a, b = SPAN[level]
+            cp(c("Gt", s(a, b)), ind(Qw, twice))
+            trn(c("Tt", s(a, b)), c("Gt", s(a, b)))
+            cp(c("Ws0", s(*WS[level])), ind(c("Tt", s(a, b)), pick(level)))
+            ship(0, level)
+
+
+    def tokens(out, win, lst, at):
+        cp(c("Pi", s(at, at + 16)), ind(win, pick(lst)))
+        ts(c("Pj", s(at, at + 16)), c("Pi", s(at, at + 16)), 4095, Op.bitwise_and)
+        cp(out, c("Pj", s(at, at + 16)))
+
+    def draft(t):
+        W = "Ws%d" % t
+        cp(c("rootd"), c("md%d" % (t - 1), s(16, 18)))
+        Wp, Wq = "Wp%d" % t, "Wq%d" % t
+
+        def turn(a, b, twice):
+            ts(c("Gt", s(a, b)), ind(Aw, twice), col("look"), Op.add)
+            trn(c("Tt", s(a, b)), c("Gt", s(a, b)))
+
+        tag[0] = "d%d0" % t
+        turn(0, 32, c("rootd"))
+        for r in range(8):
+            scan(c("S1", s(34 * r + 1, 34 * r + 33)), c("Tt", s(0, 32)), c("S1", s(34 * r - 34, 34 * r - 2)) if r else c("Tt", s(0, 32)), 0.0, Op.max, Op.min if r else Op.max)
+            if r == 4:
+                tokens(c(Wp), c("S1", s(0, 170)), 7, 64)
+                if t == 1:
+                    ship(t, 3, Wp)
+                tag[0] = "e%d0" % t
+        tokens(c(W, s(0, 16)), c("S1"), 3, 0)
+        ship(t, 4 if t == 1 else 0)
+        tag[0] = "d%d1" % t
+        turn(128, 256, c(Wp, s(0, 8)))
+        scan(c("S2", s(0, 96)), c("RS", s(0, 96)), c("Tt", s(128, 224)), 0.0, Op.min, Op.max)
+        tokens(c(Wq), c("S2", s(0, 96)), 6, 48)
+        tag[0] = "e%d1" % t
+        cp(c("X2"), ind(c("Tt", s(128, 288)), c("l17", s(0, 5))))
+        for r in range(7, -1, -1):
+            at = 96 + 70 * r
+            scan(c("S2", s(at + 1, at + 69)), c("X2", s(0, 68)), c("RL") if r == 7 else c("S2", s(at + 70, at + 138)), HIGH, Op.min, Op.max)
+        tokens(c(W, s(16, 32)), c("S2"), 4, 16)
+        ship(t, 1)
+        tag[0] = "d%d2" % t
+        turn(32, 128, c(Wq, s(10, 16)))
+        scan(c("S3", s(1, 97)), c("RS", s(0, 96)), c("Tt", s(32, 128)), 0.0, Op.min, Op.max)
+        scan(c("S3", s(132, 164)), c("RT"), c("Tt", s(64, 96)), 0.0, Op.max, Op.min)
+        scan(c("S3", s(100, 132)), c("Tt", s(32, 64)), c("S3", s(0, 32)), 0.0, Op.max, Op.min)
+        tokens(c(W, s(32, 48)), c("S3"), 5, 32)
+        ship(t, 2)
+
+    def spare(t):
+        W = "Ws%d" % t
+        cp(col("Wf", 0), col("rootd", 0))
+        cp(c("Wf", s(1, 9)), c(W, s(8, 16)))
+        cp(c("Wf", s(9, 19)), c(W, s(16, 26)))
+        cp(c("Wf", s(19, 24)), c(W, s(32, 37)))
+        for j, bank in enumerate(("dif", "cnt", "dif")):
+            a, b = 8 * j, 8 * j + 8
+            later, own = c("Wx", s(32 * j, 32 * j + 32)), c("Wy", s(32 * j, 32 * j + 32))
+            ts(later, ind(c("Wf", s(a, b)), c("pairs", s(0, 2))), -float(MID), Op.add)
+            ts(own, ind(c("Wf", s(a, b)), c("pairs", s(2, 4))), -1.0, Op.mult, float(MID), Op.add)
+            mmul(c(bank), c("Id"), c("Mk"), True, False)
+            for q in range(16):
+                mmul(c(bank, s(q, 512, 16)), c("Sel", q), later, False, False)
+                mmul(c(bank, s(q, 512, 16)), c("Id"), own, False, q == 15)
+            for n in range(8):
+                red(col("mn", a + n), c(bank, s(64 * n, 64 * n + 64 - 16 * (n % 4))), Op.min, apply_absolute_value=True)
+            ts(c("t24", s(a, b)), c("mn", s(a, b)), 0.5, Op.is_lt, 8192.0, Op.mult)
+            tt(c("u24", s(a, b)), c("t24", s(a, b)), c("trash", s(a, b)), Op.min)
+            tt(c("w24", s(a, b)), c("u24", s(a, b)), c("Wf", s(a, b)), Op.max)
+            cp(c("L", s(a, b)), c("w24", s(a, b)))
 
     def scatter(t):
-        for k in range(24 // CH):
-            cp(ind(c("A"), c("L", s(k * CH, k * CH + CH))), c("Ol%d" % t, s(16 * CH * k, 16 * CH * (k + 1))))
+        for n in range(0, M, 4):
+            cp(ind(c("A"), c("L", s(n, n + 4))), c("Ol%d" % t, cols(n, n + 4)))
 
-    def states(x, kn, cut, at):
-        cp(c("xn", s(0, 16)), x)
-        ts(c("xh", s(0, 16)), x, 0.5, Op.mult)
-        tt(c("xn", s(16, 16 * cut)), ind(c("xh", s(0, 16)), c("parl", s(0, cut - 1))), c(kn, s(16, 16 * cut)), Op.add)
-        ts(c("xh", s(16, 96)), c("xn", s(16, 96)), 0.5, Op.mult)
-        tt(c("xn", s(16 * cut, 304)), ind(c("xh", s(0, 96)), c("parl", s(at, at + 19 - cut))), c(kn, s(16 * cut, 304)), Op.add)
-        ts(c("xh", s(128, 256)), c("xn", s(128, 256)), 0.5, Op.mult)
-        tt(c("xn", s(304, 384)), ind(c("xh", s(128, 256)), c("parl", s(20, 25))), c(kn, s(304, 384)), Op.add)
-
-    def commit(W, top, win, out):
-        for q in INNER:
-            kids = [n for n in range(1, M) if PAR[n] == q]
-            ts(c("ok", s(kids[0], kids[-1] + 1)), c(W, s(kids[0], kids[-1] + 1)), top(q), Op.is_equal, col("ok", q), Op.mult)
-        tt(c("mm"), c("ok"), c("cmp"), Op.mult)
-        red(col("v", 0), c("mm"), Op.max)
-        ts(c("H"), c("m4"), col("v", 0), Op.add, 2.0 ** -12, Op.mult)
-        ts(c(out, s(16, 20)), c("H"), -4096.0, Op.mult, col("v", 0), Op.add)
-        ts(col("bl", 0), col("H", 0), 16.0, Op.mult, l16, Op.add)
-        cp(c(out, s(0, 16)), ind(win, col("bl", 0)))
-
-    def tops(t):
-        for j in range(8):
-            ts(c("E", s(0, 3), j), c("topm"), -float(MID), Op.add, col("n8", j), Op.mult)
-        for j in range(8):
-            mmul(c("tw", s(0, 24)), c("G", j), c("E", s(0, 3), s(0, 8), j), j == 0, j == 7)
-        tt(c("cmp"), c("tw", s(0, 24)), c("cmpN"), Op.add)
-        commit("Vc", lambda q: col("tw", q), c("xn"), "ms%d" % t)
-        send([(-1 - t, c("ms%d" % t), c("md%d" % t), "rd%d" % t), (1, c("ms%d" % t), c("mv%d" % (t + 1)), "rv%d" % (t + 1))])
+    def states(depth, kn, x=None, near=False):
+        if depth == 1:
+            act(c("xn", s(0, 16)), x)
+            act(c("xh", s(0, 16)), x, AF.Identity, scale=0.5)
+            for a, b in ((1, 9),) if near else ((1, 5), (5, 9)):
+                tt(c("xn", cols(a, b)), ind(c("xh", s(0, 16)), c("parl", s(a - 1, b - 1))), c(kn, cols(a, b)), Op.add)
+            act(c("xh", s(16, 96)), c("xn", s(16, 96)), AF.Identity, scale=0.5)
+        elif depth == 2:
+            tt(c("xn", s(144, 304)), ind(c("xh", s(0, 96)), c("parl", s(8, 18))), c(kn, s(144, 304)), Op.add)
+            if near:
+                ts(c("xh", s(128, 256)), c("xn", s(128, 256)), 0.5, Op.mult)
+            else:
+                act(c("xh", s(128, 256)), c("xn", s(128, 256)), AF.Identity, scale=0.5)
+        else:
+            tt(c("xn", s(304, 384)), ind(c("xh", s(128, 256)), c("parl", s(18, 23))), c(kn, s(304, 384)), Op.add)
 
     def verify(t):
-        W = "Wl%d" % t
-        for j, bank in enumerate(("comp", "comq")):
-            mmul(c(bank, s(0, 24)), p("ones", 0, 1), p("tie", 0, 1, s(0, 24), s(8 * j, 8 * j + 8)), True, False)
-            mmul(c(bank, s(0, 24)), p("ones", 0, 1), p("mid", 0, 1), False, False)
-        for a, b in ((0, 4), (4, 8), (8, 12), (12, 24)):
-            cp(c("cand", s(16 * a, 16 * b)), ind(Qw, c(W, s(a, b))))
-        act(c("kn", s(0, 128)), ind(Kw, c(W, s(0, 8))))
-        act(c("kn", s(128, 384)), ind(Kw, c(W, s(8, 24))))
-        states(c("mv%d" % t, s(0, 16)), "kn", 8, 8)
-        ts(c("Vc"), c(W), -float(MID), Op.add)
-        ts(c("thb", s(0, 1024, 16)), c("xn", s(64, 128)), kp, Op.subtract)
-        for k in range(1, NV):
-            ts(c("thb", s(k, 1024, 16)), c("xn", s(64, 128)), kp, Op.subtract)
-        for k in range(NV, 16):
-            pcopy(c("thb", s(k, 1024, 16)), c("thb", s(0, 1024, 16)), [[0, 64]])
-        for a, b in ((0, 64), (128, 304), (304, 384)):
-            ts(c("th", s(a, b)), c("xn", s(a, b)), kp, Op.subtract)
-        for b in range(3):
-            ts(c("candh", s(128 * b, 128 * b + 128)), c("cand", s(128 * b, 128 * b + 128)), -float(MID), Op.add)
-            for j, bank in enumerate(("comp", "comq")):
-                mmul(c(bank, s(8 * b, 8 * b + 8)), c("candh", s(128 * b, 128 * b + 128)), c("Id", s(0, 8), s(8 * j, 8 * j + 8)), False, False)
-        at = lambda lo, hi, b, k: p("comq" if k > 7 else "comp", lo, hi, s(8 * b, 8 * b + 8), k % 8 // 4, k % 4)
-        for u, h in enumerate((0, 2, 3, 4, 5)):
-            act(c("kc", s(1024 * u, 1024 * u + 1024)), ind(Kw, c("cand", s(64 * h, 64 * h + 64))))
-        tt(c("geB"), ind(Kw, c("cand", s(64, 128))), c("thb"), Op.is_ge)
-        for k in range(16):
-            mmul(at(64, 128, 0, k), c("geB", s(k, 1024, 16)), c("Gm"), False, False)
-        for u, h in enumerate((0, 2, 3, 4, 5)):
-            for k in range(15, -1, -1):
-                tt(c("geA", s(320 * k + 64 * u, 320 * k + 64 * u + 64)), c("kc", s(1024 * u + k, 1024 * u + 1024, 16)), c("th", s(64 * h, 64 * h + 64)), Op.is_ge)
-                if h == 0:
-                    mmul(at(0, 64, 0, k), c("geA", s(320 * k, 320 * k + 64)), c("Gm"), False, False)
-                elif h % 2:
-                    mmul(at(0, 128, h // 2, k), c("geA", s(320 * k + 64 * u - 64, 320 * k + 64 * u + 64)), c("Gm"), False, h == 5 and k % 8 == 0)
-        act(c("S0"), c("comq", s(0, 24)))
-        for L, layer in enumerate(NET):
-            sin, sout = ("S0", "S2") if L == 0 else ("S2" if L == 1 else "S%d" % (L % 2), "S%d" % ((L + 1) % 2))
-            rin, rout = s(32 * (L % 2), 32 * (L % 2) + 24), s(32 - 32 * (L % 2), 56 - 32 * (L % 2))
-            for op, mem, a, b, o in layer:
-                tt(cube("P", o, rout) if mem == 1 else cube([sout, None, "srt"][mem], o), cube(sin, a), cube("P" if L else "comp", b, rin),
-                   Op.max if op == "max" else Op.min)
-            if L == 0 and t == 1:
-                tag[0] = "m1"
-                tt(c("tr4"), c("S2", s(0, 24), 0), c("S2", s(0, 24), 1), Op.max)
-                tt(c("tr2"), c("tr4", s(0, 24), s(0, 2)), c("tr4", s(0, 24), s(2, 4)), Op.max)
-                tt(c("topi"), c("tr2", s(0, 24), 0), c("tr2", s(0, 24), 1), Op.max)
-                ts(c("topm"), c("topi"), 4095, Op.bitwise_and)
-                tops(t)
-                tag[0] = "v1"
-        O = "Os%d" % t
-        for b, bank in enumerate((c("back", s(0, 128)), c("th", s(0, 128)), c("comq", s(0, 16)))):
-            rows = s(8 * b, 8 * b + 8)
-            ts(c("srm", rows), c("srt", rows), 4095, Op.bitwise_and)
-            ts(c("srh", rows), c("srm", rows), -float(MID), Op.add)
-            mmul(bank, c("srh", rows), c("Id"), True, True)
-            ts(c(O, s(128 * b, 128 * b + 128)), bank, float(MID), Op.add)
-            if 128 * b + 128 in OCUT:
-                j = OCUT.index(128 * b + 128)
-                send([(-1 - t, c(O, s(OCUT[j - 1], OCUT[j])), c("Ol%d" % t, s(OCUT[j - 1], OCUT[j])), "rO%s%d" % ("abc"[j - 1], t))])
-        if t == 0:
-            tag[0] = "m0"
-            ts(c("topm"), c("srt", s(0, 24), 0, 0), 4095, Op.bitwise_and)
-            tops(t)
+        W, mv = "Wl%d" % t, "mv%d" % t
+        cp(c("rootv"), c(mv, s(16, 18)))
+        cp(c("cand", cols(0, 1)), ind(Qw, col("rootv", 0)))
+        for a, b in [(1, 5), (5, 9)] + DEPTH[1:]:
+            cp(c("cand", cols(a, b)), ind(Qw, c(W, s(a + 1, b + 1))))
+            act(c("kn", cols(a, b)), ind(Kw, c(W, s(a + 1, b + 1))))
+        for d in range(3):
+            states(d + 1, "kn", c(mv, s(0, 16)))
+        for lo, hi, who in GATHERS:
+            (cp if who == "V" else act)(c("kc", s(256 * lo, 256 * hi)), ind(Kw, c("cand", cols(lo, hi))))
+        for j, (a, b) in enumerate(PIECES):
+            bank = "k" + "ABC"[j % 3]
+            ts(c("candh", cols(a, b)), c("cand", cols(a, b)), -float(MID), Op.add)
+            mmul(c(bank, cols(a, b)), c("Id"), c("candh", cols(a, b)), True, False)
+            for u, (lo, hi) in enumerate(CHUNKS):
+                if a <= lo < b:
+                    th = "th" + "AB"[u % 2]
+                    act(c(th, cols(lo, hi)), c("xn", cols(lo, hi)), AF.Identity, bias=col("nkp"))
+                    for k in range(16):
+                        tt(c("ge", k, cols(lo, hi)), c("kc", s(256 * lo + k, 256 * hi, 16)), c(th, cols(lo, hi)), Op.is_ge)
+                        mmul(c(bank, cols(lo, hi)), c("Ge", s(15 - k, 143 - k)), c("ge", k, cols(lo, hi)), False, hi == b and k == 15)
+            act(c("Os%d" % t, cols(a, b)), c(bank, cols(a, b)), AF.Identity, bias=col("back"))
+            send([(-1 - t, c("Os%d" % t, cols(a, b)), c("Ol%d" % t, cols(a, b)), "rO%d%d" % (t, j))])
 
-    def chain():
-        ts(c("CT", s(0, 2)), c("z4", s(0, 2)), col("mv2", 16), Op.add)
-        cp(c("CX", s(0, 16)), c("mv2", s(0, 16)))
+    def chain(t):
+        mv = "mv%d" % t
+        cp(c("CT", s(0, 2)), c(mv, s(16, 18)))
+        act(c("CX", s(0, 16)), c(mv, s(0, 16)))
         for l in range(4):
             tk, x = c("CT", s(2 * l, 2 * l + 2)), c("CX", s(16 * l, 16 * l + 16))
             cp(c("cu"), ind(Qw, tk))
             if l:
                 tt(x, ind(Kw, col("CT", 2 * l)), c("chx"), Op.add)
             for j in range(2):
-                act(c("thc", s(128 * j, 128 * j + 128)), ind(x, c("bc", s(8 * j, 8 * j + 8))), col("nkp", 0))
+                act(c("thc", s(128 * j, 128 * j + 128)), ind(x, c("bc", s(8 * j, 8 * j + 8))), AF.Identity, bias=col("nkp"))
             ts(c("ch"), c("cu"), -float(MID), Op.add)
             trn(c("cT"), c("ch"))
             if l < 3:
-                ts(c("chx"), x, 0.5, Op.mult)
-            out = c("tw", s(32, 96))
-            mmul(out, p("ones", 0, 1), p("tie", 0, 1, s(0, 4)), True, False)
-            mmul(out, p("ones", 0, 1), p("mid", 0, 1, s(0, 64)), False, False)
+                act(c("chx"), x, AF.Identity, scale=0.5)
+            out = c("tw", s(0, 64))
+            mmul(out, p("ones", 0, 1), p("tie", 0, 1), True, False)
+            mmul(out, p("ones", 0, 1), p("mid", 0, 1), False, False)
             mmul(out, c("IdB"), c("own"), False, False)
             for j in range(4):
-                mmul(c("tw", s(32 + 16 * j, 48 + 16 * j)), c("Iev"), c("cT", s(0, 16)), False, False)
-                mmul(c("tw", s(32 + 16 * j, 48 + 16 * j)), c("Iod"), c("cT", s(16, 32)), False, False)
+                mmul(c("tw", s(16 * j, 16 * j + 16)), c("Pk", 0), c("cT", s(0, 16)), False, False)
+                mmul(c("tw", s(16 * j, 16 * j + 16)), c("Pk", 3), c("cT", s(16, 32)), False, False)
             for j in range(2):
                 tt(c("gec", s(128 * j, 128 * j + 128)), ind(Kw, c("cu", s(8 * j, 8 * j + 8))), c("thc", s(128 * j, 128 * j + 128)), Op.is_ge)
             for j in range(4):
                 mmul(out, c("SelT", j), c("gec", s(64 * j, 64 * j + 64)), False, j == 3)
-            red(col("v2", 0), out, Op.max)
+            red(col("v", l), out, Op.max)
+            ts(c("H", s(0, 2)), c("m4", s(0, 2)), col("v", l), Op.add, 2.0 ** -12, Op.mult)
             if l < 3:
-                ts(c("H2", s(0, 2)), c("m4", s(0, 2)), col("v2", 0), Op.add, 2.0 ** -12, Op.mult)
-                ts(c("CT", s(2 * l + 2, 2 * l + 4)), c("H2", s(0, 2)), -4096.0, Op.mult, col("v2", 0), Op.add)
-        ts(c("H2"), c("m4"), col("v2", 0), Op.add, 2.0 ** -12, Op.mult)
-        ts(c("c4"), c("H2"), -4096.0, Op.mult, col("v2", 0), Op.add)
-        cp(c("CX", s(64, 72)), c("CT"))
-        send([(-3, c("CX"), c("mdC"), "rC")])
-        send([(-3, c("c4"), c("mdD"), "rD")])
+                ts(c("CT", s(2 * l + 2, 2 * l + 4)), c("H", s(0, 2)), -4096.0, Op.mult, col("v", l), Op.add)
+            if l == 2:
+                cp(c("tf", s(0, 3)), c("CT", s(2, 8, 2)))
+                tt(c("Z", s(0, 4)), c("tf", s(0, 4)), c("dep", s(0, 4)), Op.add)
+                cp(col("Z", 4), col("Z", 0))
+            if l == 3:
+                ts(col("tf", 4), col("H", 0), -4096.0, Op.mult, col("v", l), Op.add)
 
-    yt = lambda t: ("yt", (slice(None), s(16 * t, 16 * t + 16)))
+    kids = lambda q, by: s(PAR.index(q, 1) + by, M - PAR[::-1].index(q) + by)
+
+    def settle(t, keys, win):
+        out = "ms%d" % t
+        red(col("v", 4), keys, Op.max)
+        ts(col("bl", 0), col("v", 4), 16.0 / STEP, Op.mult, l16, Op.add)
+        ts(c("H", s(4, 8)), c("z4"), col("v", 4), Op.add, 1.0 / STEP, Op.mult)
+        if t not in CHAINS:
+            ts(c(out, s(16, 20)), c("H", s(4, 8)), -STEP, Op.mult, col("v", 4), Op.add)
+        else:
+            ts(col("v", 5), col("H", 4), -STEP, Op.mult, col("v", 4), Op.add)
+            ts(c("tf", s(8, 12)), c("H", s(4, 8)), 3.0, Op.is_equal)
+            ts(c(out, s(16, 20)), c("tf", s(8, 12)), col("tf", 4), Op.mult, col("v", 5), Op.add)
+        cp(c(out, s(0, 16)), ind(win, col("bl", 0)))
+        send([(-1 - t, c(out), c("md%d" % t), "rd%d" % t)] + [(1, c(out), c("mv%d" % (t + 1)), "rv%d" % (t + 1))] * (t < 2))
+        dma("S", ("yt", (slice(None), cols(t, t + 1))), col("md%d" % t, 16), "dy%d" % t, 2.0)
+
+    def commit(t):
+        W, O = "Wl%d" % t, "Os%d" % t
+        for a, b in PIECES:
+            trn(c("Kt", cols(a, b)), c(O, cols(a, b)))
+            scan(c("Km", cols(a, b)), c("RS", cols(0, b - a)), c("Kt", cols(a, b)), 0.0, Op.min, Op.max)
+            cp(c("Ti", s(a, b)), c("Km", s(16 * a + 15, 16 * b, 16)))
+            ts(c("Tj", s(a, b)), c("Ti", s(a, b)), 4095, Op.bitwise_and)
+            ts(c("E", s(a, b)), c("Tj", s(a, b)), -float(MID), Op.add)
+            mmul(c("tw", s(a, b)), p("ones", 0, 1), p("mid", 0, 1, s(a, b)), True, False)
+            if b == M:
+                mmul(c("tw", s(a, b)), p("ones", 0, 1), p("depb", 0, 1, s(a, b)), False, False)
+            for j in range(4):
+                mmul(c("tw", s(a + j % 2, b, 2)), c("Pk", j), c("E", s(a + j // 2, b, 2)), False, j == 3)
+            if b < M:
+                tt(c("cmp", s(a, b)), c("tw", s(a, b)), c("dep", s(a, b)), Op.add)
+            for q in INNER:
+                if a <= q < b:
+                    ts(c("ok", kids(q, 0)), c(W, kids(q, 1)), col("tw", q), Op.is_equal, col("ok", q), Op.mult)
+        tt(c("mm", s(0, a)), c("ok", s(0, a)), c("cmp", s(0, a)), Op.mult)
+        tt(c("mm", s(a, M)), c("ok", s(a, M)), c("tw", s(a, M)), Op.mult)
+        settle(t, c("mm"), c("xn"))
+
+    def chain_commit(t):
+        W = "Wl%d" % t
+        ts(c("Z", kids(0, 4)), c(W, kids(0, 1)), col("tf", 0), Op.is_equal, col("Z", 1), Op.mult)
+        ts(c("g8", s(1, 6)), c("Z", s(5, 10)), 0.5, Op.is_gt, col("Z", 2), Op.mult)
+        ts(c("g8", s(17, 20)), c("Z", s(5, 8)), 0.5, Op.is_gt, col("Z", 3), Op.mult)
+        for q in INNER[1:]:
+            if q > 8:
+                ts(col("g8", q), col(W, q + 1), col("tf", 1), Op.is_equal, col("g8", 16 + PAR[q]), Op.mult)
+            ts(c("Z", kids(q, 4)), c(W, kids(q, 1)), col("tf", 1 + (q > 8)), Op.is_equal, col("g8", q), Op.mult)
+        settle(t, c("Z", s(4, 28)), c("CX"))
+
     for t in range(2):
         tag[0] = "d%d" % t
-        draft(t, col("tokf", 0) if t == 0 else col("md0", 16))
         if t == 0:
-            dma("S", Aw, ("qt", (slice(None),)), "dA", 7.0, c("Wl0", s(8, 24)))
+            draft0()
+            dma("S", Aw, ("qt", (slice(None),)), "dA", 7.0, c("Wl0", s(20, 26)))
+        else:
+            draft(t)
         tag[0] = "u%d" % t
-        dedupe(t)
+        spare(t)
+        if t in CHAINS:
+            tag[0] = "h%d" % t
+            chain(t)
         tag[0] = "v%d" % t
         verify(t)
-        dma("S", yt(t), col("md%d" % t, 16), "dy%d" % t, 2.0)
-        if t == 1:
-            tag[0] = "h"
-            chain()
+        tag[0] = "m%d" % t
+        (chain_commit if t in CHAINS else commit)(t)
         tag[0] = "s%d" % t
         scatter(t)
     tag[0] = "d2"
-    draft(2, col("md1", 16))
+    draft(2)
+    tag[0] = "h2"
+    chain(2)
     tag[0] = "v2"
-    for (a, b), (lo, hi), sem in (((0, 8), (16, 144), "rka"), ((8, 18), (144, 304), "rkb"), ((18, 23), (304, 384), "rkc")):
-        act(c("kns", s(lo, hi)), ind(Kw, c("Wl2", s(a, b))))
-        send([(-3, c("kns", s(lo, hi)), c("knl", s(lo, hi)), sem)])
-    states(c("md1", s(0, 16)), "knl", 9, 26)
+    for d, (a, b) in enumerate(DEPTH):
+        act(c("kns", cols(a, b)), ind(Kw, c("Wl2", s(a + 1, b + 1))))
+        send([(-3, c("kns", cols(a, b)), c("knl", cols(a, b)), "rk" + "abc"[d])])
+    tag[0] = "m2"
+    chain_commit(2)
+    tag[0] = "f"
+    states(1, "knl", c("md1", s(0, 16)), near=True)
+    states(2, "knl", near=True)
+    states(3, "knl")
     dma("S", ("yn", (slice(None), s(0, 304))), c("xn", s(0, 304)), "dn0", 2.4)
     dma("A", ("yn", (slice(None), s(304, 384))), c("xn", s(304, 384)), "dn1", 2.1)
-    tag[0] = "m2"
-    cp(c("Wf", s(1, 19)), c("Ws2", s(8, 26)))
-    cp(c("Wf", s(19, 24)), c("Ws2", s(32, 37)))
-    ms(c("cmp", s(19, 24)), 3 * 4096.0)
-    for d in range(3):
-        at = [n for n in range(M) if DEP[n] == d]
-        ms(c("t24", s(at[0], at[-1] + 1)), 4096.0 * d)
-        ts(c("cmp", s(at[0], at[-1] + 1)), c("t24", s(at[0], at[-1] + 1)), col("mdC", 66 + 2 * d), Op.add)
-    commit("Wf", lambda q: col("mdC", 66 + 2 * DEP[q]), c("mdC", s(0, 64)), "fin")
-    ts(col("v", 1), col("H", 0), 3.0, Op.is_equal)
-    ts(col("v", 2), col("mdD", 0), col("v", 1), Op.mult, col("fin", 16), Op.add)
-    dma("S", yt(2), col("v", 2), "dy2", 2.0)
-    dma("A", ("yx", (slice(None),)), c("fin", s(0, 16)), "dyx", 2.0)
+    dma("A", ("yx", (slice(None),)), c("md2", s(0, 16)), "dyx", 2.0)
     return ops
 
 
 def plan():
     ops = build()
-    n = len(ops)
     lastw, readers, bank, group = {}, {}, {}, {}
     deps, order = [set() for _ in ops], [set() for _ in ops]
     for i, o in enumerate(ops):
@@ -500,40 +533,84 @@ def plan():
         deps[i].discard(i)
         if o["e"] == "T":
             deps[i] = {j for j in deps[i] if ops[j]["e"] != "T"}
-    return arrange(ops, deps, order, BUMP)
+    return arrange(ops, deps, order)
 
 
-def arrange(ops, deps, order, bump):
+def arrange(ops, deps, order):
     n = len(ops)
-    gap = lambda j, i: ops[j]["lat"] + (0.0 if j in order[i] else PL["same"] if ops[j]["e"] == ops[i]["e"] else PL["cross"])
-    allp = [deps[i] | order[i] for i in range(n)]
+    gap = lambda j, i: (ops[j]["lat"] + (PL["same"] if ops[j]["e"] == ops[i]["e"] else PL["cross"])) * (j in deps[i])
+    pred = [[(j, gap(j, i)) for j in deps[i] | order[i]] for i in range(n)]
     succ = [[] for _ in ops]
     for i in range(n):
-        for j in allp[i]:
-            succ[j].append(i)
+        for j, w in pred[i]:
+            succ[j].append((i, w))
+
+    def sweep(before, after, prio, start):
+        left = [len(x) for x in before]
+        rt, fin, busy, turn = list(start), [0.0] * n, {}, [0] * n
+        ready = [i for i in range(n) if not left[i]]
+        for step in range(n):
+            i = max(ready, key=lambda i: (prio[i], -i))
+            ready.remove(i)
+            at, took, slots = rt[i], ops[i]["c"], busy.setdefault(ops[i]["e"], [])
+            if took:
+                pos = len(slots)
+                while pos and slots[pos - 1][1] > at:
+                    pos -= 1
+                while pos < len(slots) and at + took > slots[pos][0] + 1e-9:
+                    at = max(at, slots[pos][1])
+                    pos += 1
+                slots.insert(pos, (at, at + took))
+            fin[i], turn[i] = at + took, step
+            for k, w in after[i]:
+                rt[k] = max(rt[k], fin[i] + w)
+                left[k] -= 1
+                if not left[k]:
+                    ready.append(k)
+        return sorted(range(n), key=lambda i: (round(fin[i] - ops[i]["c"], 6), turn[i])), fin
+
+    def eager(before, after, prio, start):
+        left = [len(x) for x in before]
+        rt, fin, free, ready, seq = list(start), [0.0] * n, {}, {}, []
+        for i in range(n):
+            if not left[i]:
+                ready.setdefault(ops[i]["e"], []).append(i)
+        while len(seq) < n:
+            te, e = min((max(free.get(e, 0.0), min(rt[i] for i in l)), e) for e, l in ready.items() if l)
+            i = max((i for i in ready[e] if rt[i] <= te + PL["look"]), key=lambda i: (prio[i], -i))
+            ready[e].remove(i)
+            fin[i] = free[e] = max(te, rt[i]) + ops[i]["c"]
+            seq.append(i)
+            for k, w in after[i]:
+                rt[k] = max(rt[k], fin[i] + w)
+                left[k] -= 1
+                if not left[k]:
+                    ready.setdefault(ops[k]["e"], []).append(k)
+        return seq, fin
+
+    def turns(prio, passes, forward):
+        best = None
+        for _ in range(passes):
+            seq, fin = forward(pred, succ, prio, [0.0] * n)
+            end = max(fin[i] + ops[i]["lat"] for i in range(n))
+            if best is None or end < best[0]:
+                best = (end, seq, fin, prio)
+            prio = eager(succ, pred, fin, [o["lat"] for o in ops])[1]
+        return best
+
     prio = [0.0] * n
     for i in range(n - 1, -1, -1):
-        prio[i] = bump.get(ops[i]["key"], 0.0) + ops[i]["c"] + max([gap(i, k) + prio[k] for k in succ[i]] + [ops[i]["lat"]])
-    left = [len(x) for x in allp]
-    rt, fin, free = [0.0] * n, [0.0] * n, {}
-    ready = {}
-    for i in range(n):
-        if not left[i]:
-            ready.setdefault(ops[i]["e"], []).append(i)
-    seq = []
-    while len(seq) < n:
-        te, e = min((max(free.get(e, 0.0), min(rt[i] for i in l)), e) for e, l in ready.items() if l)
-        i = max((i for i in ready[e] if rt[i] <= te + 0.04), key=lambda i: (prio[i], -i))
-        ready[e].remove(i)
-        fin[i] = max(te, rt[i]) + ops[i]["c"]
-        free[e] = fin[i]
-        seq.append(i)
-        for k in succ[i]:
-            rt[k] = max(rt[k], fin[i] + gap(i, k))
-            left[k] -= 1
-            if not left[k]:
-                ready.setdefault(ops[k]["e"], []).append(k)
-    return ops, deps, seq, fin, order
+        prio[i] = ops[i]["c"] + max([w + prio[k] for k, w in succ[i]] + [ops[i]["lat"]])
+    best = now = turns(prio, 6, sweep)
+    keys = sorted({o["key"] for o in ops})
+    rng = np.random.RandomState(1)
+    for trial in range(PL["passes"]):
+        shift = {keys[int(k)]: float(v) for k, v in zip(rng.randint(0, len(keys), 3), rng.normal(0.0, 0.7, 3))}
+        new = turns([now[3][i] + shift.get(ops[i]["key"], 0.0) for i in range(n)], 2, (sweep, eager)[trial % 2])
+        if new[0] <= now[0] + 0.05:
+            now = new
+            best = min(best, new, key=lambda x: x[0])
+    return ops, deps, best[1], best[2], order
 
 
 PLAN = []
@@ -562,10 +639,10 @@ def rank_program(g, core, T, topo):
     queue = {"V": g.vector, "A": g.scalar, "T": g.tensor, "G": g, "S": g.sync}
     call = {
         "cp": lambda a, k: g.vector.tensor_copy(*a), "tt": lambda a, k: g.vector.tensor_tensor(*a),
-        "ts": lambda a, k: g.vector.tensor_scalar(*a), "red": lambda a, k: g.vector.tensor_reduce(*a),
+        "ts": lambda a, k: g.vector.tensor_scalar(*a), "red": lambda a, k: g.vector.tensor_reduce(*a, **k),
         "trn": lambda a, k: g.vector.transpose(*a), "ms": lambda a, k: g.vector.memset(*a),
         "scan": lambda a, k: g.vector.tensor_tensor_scan(*a), "act": lambda a, k: g.scalar.activation(*a, **k),
-        "mm": lambda a, k: g.tensor.matmul(*a), "iota": lambda a, k: g.iota(*a, **k), "sel": lambda a, k: g.affine_select(*a),
+        "mm": lambda a, k: g.tensor.matmul(*a), "iota": lambda a, k: g.iota(*a, **k),
     }
 
     def ap(r):

@@ -9,6 +9,8 @@ INNER = sorted(set(PAR))
 DEPTH = [(1, 9), (9, 19), (19, 24)]
 MID = 1856
 HIGH = 2.0 ** 24
+LOW = -8192.0
+ROUND = 1.5 * 2.0 ** 35
 STEP = 2.0 ** 17
 
 F32, BF, H16, I32, U16 = "float32", "bfloat16", "float16", "int32", "uint16"
@@ -20,29 +22,34 @@ def _decl(where, dtype, **shapes):
         SCRATCH[name] = (where, [128] + list(shape), dtype)
 
 
-_decl("sbuf", I32, Q=[V], A=[V + 64], lane=[12], H=[8], Pi=[80], Pj=[80], Ti=[24], Tj=[24])
-_decl("sbuf", BF, K=[V], kc=[6144], ge=[16, 384], gec=[256], colb=[128], cm=[128], SelT=[4, 128], Ge=[144], tie=[64], depb=[24],
+_decl("sbuf", I32, Q=[V], A=[V + 64], lane=[12], H=[8], Pi=[96], Pj=[96])
+_decl("sbuf", BF, K=[V], kc=[6144], ge=[16, 384], gec=[256], colb=[128], cm=[128], SelT=[4, 128], Ge=[144], row=[128], depb=[24],
       IdB=[128], own=[64], mid=[64], ones=[128], B3=[128], Ea=[224], Eb=[512], kns=[384], knl=[384])
 _decl("sbuf", H16, Mk=[512], Id=[128], Pk=[4, 128], Sel=[16, 128], Wx=[96], Wy=[96], E=[24], ch=[32], cT=[32], candh=[384])
-_decl("sbuf", U16, bc=[16], parl=[24], sell=[20], l17=[6], pairs=[4], rootd=[2], rootv=[2], Ws0=[48], Ws1=[48], Ws2=[48], Wp1=[16], Wq1=[16], Wp2=[16], Wq2=[16],
+_decl("sbuf", U16, bc=[16], parl=[24], sell=[20], l17=[6], pairs=[4], rootd=[2], rootv=[2], rs0=[4], rs1=[4], rl0=[4], rl1=[4], Ws0=[48], Ws1=[48], Ws2=[48], Wp1=[16], Wq1=[16], Wp2=[16], Wq2=[16],
       Wl0=[26], Wl1=[26], Wl2=[26], cand=[384], L=[24], bl=[2], CT=[8], cu=[32])
-_decl("sbuf", F32, sc=[16], z4=[4], m4=[4], i16=[16], d16=[16], sg=[4], wide=[144], RR=[224], Rm=[224], Rn=[224], Rz=[224],
-      PR=[24], Tt=[288], Gt=[256], t24=[24], u24=[24], w24=[24], mn=[24], trash=[24], Wf=[24], Z=[28], tf=[12], dep=[24], g8=[24], ok=[24], cmp=[24], mm=[24], Kt=[384], Km=[384], RS=[160], v=[8], x0s=[20], mv0=[20], mv1=[20], mv2=[20],
+_decl("sbuf", F32, sc=[16], z4=[4], m4=[4], i16=[16], d16=[16], sg=[4], wide=[144], RR=[224], Rm=[224], Rz=[224],
+      PR=[24], Tt=[320], Gt=[288], t24=[24], u24=[24], w24=[24], ok=[24], IdF=[128], trash=[24], Wf=[24], Z=[28], tf=[12], dep=[24], g8=[24], Ti=[24],
+      Kt=[384], Km=[384], RS=[160], Pv=[52], Pr=[48], v=[8], x0s=[20], mv0=[20], mv1=[20], mv2=[20],
       md0=[20], md1=[20], md2=[20], ms0=[20], ms1=[20], ms2=[20], CX=[64], chx=[16], thc=[256], xn=[384], xh=[256], kn=[384],
-      RL=[68], RT=[32], X2=[80], S1=[272], S2=[656], S3=[164], Os0=[384], Os1=[384], Ol0=[384], Ol1=[384])
+      RL=[51], RT=[32], X2=[64], X5=[32], S1=[272], S2=[566], S3=[164], Os0=[384], Os1=[384], Ol0=[384], Ol1=[384])
 _decl("psum", F32, kA=[512], kB=[512], kC=[512], thA=[512], thB=[512], tw=[512], dif=[512], cnt=[512])
 SC = ["lf", "l16", "grp", "odd", "l4", "evn", "o16", "g4", "nkp", "tokf", "g16", "look", "place", "back", "", "", "kp"]
 SCRATCH["sc"] = ("sbuf", [128, 20], F32)
 
 DMAS = ["dtok", "dx0", "dkap", "dQ", "dK", "dA", "dy0", "dy1", "dy2", "dyx", "dn0", "dn1"]
-MSGS = ["rx0", "rd0", "rd1", "rd2", "rv1", "rv2", "rka", "rkb", "rkc"] + ["r%s%d%d" % (m, t, j) for m in "WO" for t in range(3) for j in range(5)]
+MSGS = ["rx0", "rr0", "rr1", "rd0", "rd1", "rd2", "rv1", "rv2", "rka", "rkb", "rkc"] + ["r%s%d%d" % (m, t, j) for m in "WO" for t in range(3) for j in range(6)]
 SEMAPHORES = ["eV", "eA", "eT", "eG", "left"] + DMAS + MSGS
 
-PL = dict(cyc=0.83e-3, gather=1.56, scatter=3.8, hop=1.6, pe=0.83e-3, issue=0.3, byte=1.2e-3, same=0.24, cross=0.15, look=0.04, passes=800)
+PL = dict(cyc=0.83e-3, gather=1.56, scatter=3.8, hop=1.7, pe=0.83e-3, issue=0.3, byte=1.2e-3, same=0.22, cross=0.22, look=0.04, passes=1200)
 CHAINS = (2,)
 PIECES = [(0, 8), (8, 16), (16, 24)]
 CHUNKS = [(0, 4), (4, 8), (8, 12), (12, 16), (16, 20), (20, 24)]
-GATHERS = [(0, 1, "V"), (1, 3, "V"), (3, 5, "A"), (5, 9, "A"), (9, 12, "A"), (12, 16, "A"), (16, 19, "A"), (19, 21, "V"), (21, 24, "A")]
+LOOK_A = True
+FIRST = [[(1, 5), (5, 9)], [(1, 3), (3, 5), (5, 9)]]
+GATHERS = [[(0, 1, "V"), (1, 4, "V"), (4, 5, "A"), (5, 9, "A"), (9, 12, "A"), (12, 16, "A"), (16, 19, "A"), (19, 22, "A"), (22, 24, "V")],
+           [(0, 1, "V"), (1, 3, "A"), (3, 5, "A"), (5, 6, "V"), (6, 9, "A"), (9, 11, "V"), (11, 12, "A"), (12, 16, "A"), (16, 19, "A"), (19, 22, "A"),
+            (22, 24, "V")]]
 
 
 def c(name, *idx):
@@ -115,8 +122,9 @@ def build():
     def scan(out, a, b, init, op0, op1): add("V", "scan", [out, a, b, init, op0, op1], [out], [a, b], vcost(out, [a, b]))
     def act(out, a, fn=AF.Copy, **kw):
         n = vcost(out, [a]) if a[0] == "*" else max(64, len(elems(a))) * CYC
-        add("A", "act", [out, a, fn], [out], [a] + list(kw.values()), n + 0.015, kw)
-    def mmul(out, l, r, st, sp): add("T", "mm", [out, l, r, st, sp], [out], [l, r], max(64, len(elems(r))) * PL["pe"], st=st, sp=sp)
+        sums = [kw["accum_out"]] if "accum_out" in kw else []
+        add("A", "act", [out, a, fn], [out] + sums, [a] + [x for x in kw.values() if x not in sums], n + 0.015 + 0.02 * len(sums), kw)
+    def mmul(out, l, r, st, sp): add("T", "mm", [out, l, r, st, sp], [out], [l, r], max(64, len(elems(r))) * PL["pe"] * (4 if SCRATCH[l[0]][2] == F32 else 1), st=st, sp=sp)
     def iota(out, pat, base, cmul):
         kw = {} if SCRATCH[out[0]][2] == I32 else {"allow_small_or_imprecise_dtypes": True}
         add("G", "iota", [out, pat, base, cmul], [out], [], 0.14 + 2 * CYC * len(elems(out)), kw)
@@ -156,10 +164,10 @@ def build():
     iota(c("own"), [[1, 4], [0, 16]], 0, 0)
     iota(c("cm"), [[1, 32], [0, 4]], 0, 0)
     iota(c("B3"), [[1, 8], [0, 16]], 0, 0)
-    iota(p("tie", 0, 1), [[0, 4], [-4096, 16]], 15 * 4096, 0)
+    iota(p("row", 0, 1), [[0, 8], [-4096, 16]], 15 * 4096, 0)
     iota(c("depb"), [[1, 24]], 0, 0)
     ts(c("dep"), c("depb"), STEP, Op.mult)
-    cp(c("depb"), c("dep"))
+    ts(c("depb"), c("dep"), -2.0 ** 23, Op.add)
     cp(col("lf"), col("lane", 0))
     for j, (sh, an) in enumerate([(0, 15), (4, 7), (4, 1), (0, 3)]):
         ts(col("lane", 1 + j), col("lane", 0), sh, Op.arith_shift_right, an, Op.bitwise_and)
@@ -169,11 +177,10 @@ def build():
     ts(col("o16"), col("odd"), 16.0, Op.mult)
     ts(col("g4"), grp, 4.0, Op.mult)
     ts(col("g16"), grp, 16.0, Op.mult)
-    ts(col("place"), l16, -4096.0, Op.mult, 15 * 4096.0, Op.add)
-    ts(col("back"), col("place"), float(MID), Op.add)
+    ts(col("place"), l16, -4096.0, Op.mult, 15 * 4096.0 - MID, Op.add)
     ts(col("look"), col("odd"), 2.0 ** 22, Op.mult, col("place"), Op.add)
     ms(c("z4"), 0.0); ms(c("m4"), -float(MID)); ms(col("ok", 0), 1.0); ms(col("tf", 3), 0.0)
-    ms(c("RS"), HIGH); ms(c("RS", s(0, 160, 16)), 0.0)
+    ms(c("RS"), HIGH); ms(c("RS", s(0, 160, 16)), LOW)
     cp(col("tokf"), col("lane", 8))
     ts(c("x0s", s(16, 20)), c("z4"), col("tokf"), Op.add)
     send([(1, c("x0s"), c("mv0"), "rx0")])
@@ -184,8 +191,8 @@ def build():
     def entries(a, b):
         ts(c("Rm", s(a, b)), c("Ea", s(a, b)), l16, Op.is_equal)
         tt(c("RR", s(a, b)), c("RR", s(a, b)), c("Rm", s(a, b)), Op.mult)
-        ts(c("Rn", s(a, b)), c("Ea", s(a, b)), 0.5, Op.is_gt)
-        scan(c("Rz", s(a, b)), c("Rn", s(a, b)), c("RR", s(a, b)), 0.0, Op.mult, Op.add)
+        ts(c("Km", s(a, b)), c("Ea", s(a, b)), 0.5, Op.is_gt)
+        scan(c("Rz", s(a, b)), c("Km", s(a, b)), c("RR", s(a, b)), 0.0, Op.mult, Op.add)
 
     iota(c("RR", s(0, 6)), [[1, 3], [0, 2]], 0, 0)
     iota(c("RR", s(8, 16)), [[1, 8]], 0, 0)
@@ -195,7 +202,8 @@ def build():
     entries(0, 48)
     ts(c("sell", s(0, 6, 2)), c("Rz", s(15, 48, 16)), col("o16"), Op.add)
     iota(c("RR", s(48, 133)), [[32, 5], [1, 17]], 0, 0)
-    fill("RR", [96 + 70 * (ROW[n] - 8) + 17 * lane(n) + 16 if ROW[n] else 32 * lane(n) + 15 for n in range(9, 19)] + [15] * 6, 128)
+    leaf = lambda n: 96 + 52 * (ROW[n] - 8) + 17 * lane(n) + 16 if PAR[n] < 5 else 512 + 18 * (ROW[n] - 13) + 16
+    fill("RR", [leaf(n) if ROW[n] else 32 * lane(n) + 15 for n in range(9, 19)] + [15] * 6, 128)
     fill("RR", [{0: 16 + 32 * lane(n), 1: 115, 15: 147}[ROW[n]] for n in range(19, 24)] + [80] * 11, 144)
     iota(c("RR", s(160, 192)), [[1, 8], [1, 4]], 0, 0)
     iota(c("RR", s(192, 224)), [[1, 8], [0, 4]], 0, 0)
@@ -207,6 +215,8 @@ def build():
     ts(pick(3), col("sg", 0), col("o16"), Op.add)
     ts(col("sg", 1), col("sg", 0), 34.0 * 4 + 16, Op.min)
     ts(pick(7), col("sg", 1), col("o16"), Op.add)
+    ts(col("sg", 3), col("sg", 0), 34.0 * 2 + 16, Op.min)
+    ts(pick(8), col("sg", 3), col("o16"), Op.add)
     ts(col("sg", 2), col("Rz", 143), 96.0, Op.is_lt, col("o16"), Op.mult)
     ts(pick(4), col("Rz", 143), col("sg", 2), Op.add)
     ts(pick(5), col("Rz", 159), col("o16"), Op.add)
@@ -217,8 +227,9 @@ def build():
     cp(c("bc"), c("i16"))
     cp(c("colb"), c("wide", s(15, 143)))
     ts(c("Mk"), c("Eb"), l16, Op.is_le, 8192.0, Op.mult)
-    ts(c("own"), c("own"), col("l4"), Op.is_equal, 2.0 ** 21, Op.mult)
-    ts(c("IdB"), c("colb"), col("lf"), Op.is_equal)
+    ts(c("own"), c("own"), col("l4"), Op.is_equal, 0.25, Op.mult)
+    ts(c("IdB"), c("colb"), col("lf"), Op.is_equal, 2.0 ** 23, Op.mult)
+    cp(c("IdF"), c("IdB"))
     ts(c("Id"), c("colb"), col("lf"), Op.is_equal)
     ts(c("Ge"), c("wide"), col("g16"), Op.is_equal, 2.0 ** 17, Op.mult)
     ms(p("mid", 0, 1), float(MID)); ms(p("ones", 0, 1), 1.0)
@@ -232,15 +243,15 @@ def build():
     for j in range(16):
         ts(c("Sel", j), c("B3"), grp, Op.is_equal, col("d16", j), Op.mult)
     ts(c("trash"), c("trash"), l16, Op.add)
-    ms(c("RL"), 0.0); ms(c("RL", s(16, 68, 17)), HIGH); ms(c("RT"), 0.0); ms(c("RT", s(0, 32, 16)), HIGH)
-    ms(c("S1", s(0, 272, 34)), 0.0); ms(c("S1", s(33, 272, 34)), 0.0); ms(c("S2", s(96, 656, 70)), HIGH); ms(c("S2", s(165, 656, 70)), 0.0)
-    ms(col("S3", 0), 0.0); ms(c("S3", s(97, 100)), 0.0); ms(c("Tt", s(256, 288)), 0.0)
+    ms(c("RL"), LOW); ms(c("RL", s(16, 51, 17)), HIGH); ms(c("RT"), LOW); ms(c("RT", s(0, 32, 16)), HIGH)
+    ms(c("S1", s(0, 272, 34)), LOW); ms(c("S1", s(33, 272, 34)), LOW); ms(c("S2", s(96, 512, 52)), HIGH); ms(c("S2", s(512, 566, 18)), HIGH)
+    ms(col("S3", 0), LOW); ms(c("S3", s(97, 100)), LOW); ms(c("Tt", s(288, 320)), 0.0)
 
     SPAN = [(0, 32), (128, 256), (32, 128)]
     WS = [(0, 16), (16, 32), (32, 48)]
 
     def ship(t, level, W=None):
-        a, b, at = [(8, 16, 2), (16, 26, 10), (32, 38, 20), (8, 12, 2), (12, 16, 6)][level]
+        a, b, at = [(8, 16, 2), (16, 26, 10), (32, 38, 20), (8, 10, 2), (10, 12, 4), (12, 16, 6)][level]
         send([(1 + t, c(W or "Ws%d" % t, s(a, b)), c("Wl%d" % t, s(at, at + b - a)), "rW%d%d" % (t, level))])
 
     def draft0():
@@ -254,52 +265,69 @@ def build():
 
 
     def tokens(out, win, lst, at):
-        cp(c("Pi", s(at, at + 16)), ind(win, pick(lst)))
+        ts(c("Pi", s(at, at + 16)), ind(win, pick(lst)), float(MID), Op.add)
         ts(c("Pj", s(at, at + 16)), c("Pi", s(at, at + 16)), 4095, Op.bitwise_and)
         cp(out, c("Pj", s(at, at + 16)))
 
+    def parents(out, win, lst, at, pairs):
+        act(c("Pv", s(at, at + 16)), ind(win, pick(lst)))
+        ts(c("Pr", s(at, at + 16)), ind(win, pick(lst)), ROUND, Op.add, ROUND, Op.subtract)
+        for j, w in pairs:
+            ts(c(out, s(j, j + w)), c("Pv", s(at + j, at + j + w)), col("Pr", at + j), Op.subtract, float(MID), Op.add)
+
     def draft(t):
-        W = "Ws%d" % t
-        cp(c("rootd"), c("md%d" % (t - 1), s(16, 18)))
+        W, root = "Ws%d" % t, c("rl%d" % (t - 1), s(0, 2))
         Wp, Wq = "Wp%d" % t, "Wq%d" % t
 
         def turn(a, b, twice):
-            ts(c("Gt", s(a, b)), ind(Aw, twice), col("look"), Op.add)
+            if LOOK_A:
+                act(c("Gt", s(a, b)), ind(Aw, twice), AF.Identity, bias=col("look"))
+            else:
+                ts(c("Gt", s(a, b)), ind(Aw, twice), col("look"), Op.add)
             trn(c("Tt", s(a, b)), c("Gt", s(a, b)))
 
         tag[0] = "d%d0" % t
-        turn(0, 32, c("rootd"))
+        turn(0, 32, root)
         for r in range(8):
-            scan(c("S1", s(34 * r + 1, 34 * r + 33)), c("Tt", s(0, 32)), c("S1", s(34 * r - 34, 34 * r - 2)) if r else c("Tt", s(0, 32)), 0.0, Op.max, Op.min if r else Op.max)
-            if r == 4:
-                tokens(c(Wp), c("S1", s(0, 170)), 7, 64)
+            scan(c("S1", s(34 * r + 1, 34 * r + 33)), c("Tt", s(0, 32)), c("S1", s(34 * r - 34, 34 * r - 2)) if r else c("Tt", s(0, 32)), LOW, Op.max, Op.min if r else Op.max)
+            if r == 2:
+                parents(Wp, c("S1", s(0, 102)), 8, 0, [(0, 2), (2, 2), (4, 2)] + [(8, 1), (9, 1)] * (t == 1))
                 if t == 1:
                     ship(t, 3, Wp)
                 tag[0] = "e%d0" % t
+            if r == 4:
+                parents(Wp, c("S1", s(0, 170)), 7, 16, [(6, 2)] + [(10, 1), (11, 1)] * (t == 1))
+                if t == 1:
+                    ship(t, 4, Wp)
         tokens(c(W, s(0, 16)), c("S1"), 3, 0)
-        ship(t, 4 if t == 1 else 0)
+        ship(t, 5 if t == 1 else 0)
         tag[0] = "d%d1" % t
-        turn(128, 256, c(Wp, s(0, 8)))
-        scan(c("S2", s(0, 96)), c("RS", s(0, 96)), c("Tt", s(128, 224)), 0.0, Op.min, Op.max)
-        tokens(c(Wq), c("S2", s(0, 96)), 6, 48)
+        turn(128, 224, c(Wp, s(0, 6)))
+        scan(c("S2", s(0, 96)), c("RS", s(0, 96)), c("Tt", s(128, 224)), LOW, Op.min, Op.max)
+        parents(Wq, c("S2", s(0, 96)), 6, 32, [(10, 2), (12, 2), (14, 2)])
         tag[0] = "e%d1" % t
-        cp(c("X2"), ind(c("Tt", s(128, 288)), c("l17", s(0, 5))))
+        act(c("X2"), ind(c("Tt", s(128, 256)), c("l17", s(0, 4))))
         for r in range(7, -1, -1):
-            at = 96 + 70 * r
-            scan(c("S2", s(at + 1, at + 69)), c("X2", s(0, 68)), c("RL") if r == 7 else c("S2", s(at + 70, at + 138)), HIGH, Op.min, Op.max)
+            at = 96 + 52 * r
+            scan(c("S2", s(at + 1, at + 52)), c("X2", s(0, 51)), c("RL") if r == 7 else c("S2", s(at + 52, at + 103)), HIGH, Op.min, Op.max)
+        turn(256, 288, c(Wp, s(6, 8)))
+        act(c("X5"), ind(c("Tt", s(256, 320)), c("l17", s(0, 2))))
+        for r in range(2, -1, -1):
+            at = 512 + 18 * r
+            scan(c("S2", s(at + 1, at + 18)), c("X5", s(0, 17)), c("RL", s(0, 17)) if r == 2 else c("S2", s(at + 18, at + 35)), HIGH, Op.min, Op.max)
         tokens(c(W, s(16, 32)), c("S2"), 4, 16)
         ship(t, 1)
         tag[0] = "d%d2" % t
         turn(32, 128, c(Wq, s(10, 16)))
-        scan(c("S3", s(1, 97)), c("RS", s(0, 96)), c("Tt", s(32, 128)), 0.0, Op.min, Op.max)
-        scan(c("S3", s(132, 164)), c("RT"), c("Tt", s(64, 96)), 0.0, Op.max, Op.min)
-        scan(c("S3", s(100, 132)), c("Tt", s(32, 64)), c("S3", s(0, 32)), 0.0, Op.max, Op.min)
+        scan(c("S3", s(1, 97)), c("RS", s(0, 96)), c("Tt", s(32, 128)), LOW, Op.min, Op.max)
+        scan(c("S3", s(132, 164)), c("RT"), c("Tt", s(64, 96)), LOW, Op.max, Op.min)
+        scan(c("S3", s(100, 132)), c("Tt", s(32, 64)), c("S3", s(0, 32)), LOW, Op.max, Op.min)
         tokens(c(W, s(32, 48)), c("S3"), 5, 32)
         ship(t, 2)
 
     def spare(t):
         W = "Ws%d" % t
-        cp(col("Wf", 0), col("rootd", 0))
+        cp(col("Wf", 0), col("rl0" if t else "rootd", 0))
         cp(c("Wf", s(1, 9)), c(W, s(8, 16)))
         cp(c("Wf", s(9, 19)), c(W, s(16, 26)))
         cp(c("Wf", s(19, 24)), c(W, s(32, 37)))
@@ -312,9 +340,10 @@ def build():
             for q in range(16):
                 mmul(c(bank, s(q, 512, 16)), c("Sel", q), later, False, False)
                 mmul(c(bank, s(q, 512, 16)), c("Id"), own, False, q == 15)
+            act(c("Eb"), c(bank), AF.Abs)
             for n in range(8):
-                red(col("mn", a + n), c(bank, s(64 * n, 64 * n + 64 - 16 * (n % 4))), Op.min, apply_absolute_value=True)
-            ts(c("t24", s(a, b)), c("mn", s(a, b)), 0.5, Op.is_lt, 8192.0, Op.mult)
+                e = s(64 * n, 64 * n + 64 - 16 * (n % 4))
+                act(c("Eb", e), c("Eb", e), AF.Relu, bias=4096.0, scale=-4096.0, accum_out=col("t24", a + n))
             tt(c("u24", s(a, b)), c("t24", s(a, b)), c("trash", s(a, b)), Op.min)
             tt(c("w24", s(a, b)), c("u24", s(a, b)), c("Wf", s(a, b)), Op.max)
             cp(c("L", s(a, b)), c("w24", s(a, b)))
@@ -323,11 +352,11 @@ def build():
         for n in range(0, M, 4):
             cp(ind(c("A"), c("L", s(n, n + 4))), c("Ol%d" % t, cols(n, n + 4)))
 
-    def states(depth, kn, x=None, near=False):
+    def states(depth, kn, x=None, near=False, first=((1, 9),)):
         if depth == 1:
             act(c("xn", s(0, 16)), x)
             act(c("xh", s(0, 16)), x, AF.Identity, scale=0.5)
-            for a, b in ((1, 9),) if near else ((1, 5), (5, 9)):
+            for a, b in first:
                 tt(c("xn", cols(a, b)), ind(c("xh", s(0, 16)), c("parl", s(a - 1, b - 1))), c(kn, cols(a, b)), Op.add)
             act(c("xh", s(16, 96)), c("xn", s(16, 96)), AF.Identity, scale=0.5)
         elif depth == 2:
@@ -343,17 +372,18 @@ def build():
         W, mv = "Wl%d" % t, "mv%d" % t
         cp(c("rootv"), c(mv, s(16, 18)))
         cp(c("cand", cols(0, 1)), ind(Qw, col("rootv", 0)))
-        for a, b in [(1, 5), (5, 9)] + DEPTH[1:]:
+        for a, b in FIRST[t] + DEPTH[1:]:
             cp(c("cand", cols(a, b)), ind(Qw, c(W, s(a + 1, b + 1))))
             act(c("kn", cols(a, b)), ind(Kw, c(W, s(a + 1, b + 1))))
         for d in range(3):
-            states(d + 1, "kn", c(mv, s(0, 16)))
-        for lo, hi, who in GATHERS:
+            states(d + 1, "kn", c(mv, s(0, 16)), first=FIRST[t])
+        for lo, hi, who in GATHERS[t]:
             (cp if who == "V" else act)(c("kc", s(256 * lo, 256 * hi)), ind(Kw, c("cand", cols(lo, hi))))
         for j, (a, b) in enumerate(PIECES):
             bank = "k" + "ABC"[j % 3]
             ts(c("candh", cols(a, b)), c("cand", cols(a, b)), -float(MID), Op.add)
-            mmul(c(bank, cols(a, b)), c("Id"), c("candh", cols(a, b)), True, False)
+            mmul(c(bank, cols(a, b)), p("row", 0, 1), p("ones", 0, 1, cols(0, b - a)), True, False)
+            mmul(c(bank, cols(a, b)), c("Id"), c("candh", cols(a, b)), False, False)
             for u, (lo, hi) in enumerate(CHUNKS):
                 if a <= lo < b:
                     th = "th" + "AB"[u % 2]
@@ -361,7 +391,9 @@ def build():
                     for k in range(16):
                         tt(c("ge", k, cols(lo, hi)), c("kc", s(256 * lo + k, 256 * hi, 16)), c(th, cols(lo, hi)), Op.is_ge)
                         mmul(c(bank, cols(lo, hi)), c("Ge", s(15 - k, 143 - k)), c("ge", k, cols(lo, hi)), False, hi == b and k == 15)
-            act(c("Os%d" % t, cols(a, b)), c(bank, cols(a, b)), AF.Identity, bias=col("back"))
+            if t not in CHAINS:
+                trn(c("Kt", cols(a, b)), c(bank, cols(a, b)))
+            act(c("Os%d" % t, cols(a, b)), c(bank, cols(a, b)), AF.Identity, bias=float(MID))
             send([(-1 - t, c("Os%d" % t, cols(a, b)), c("Ol%d" % t, cols(a, b)), "rO%d%d" % (t, j))])
 
     def chain(t):
@@ -380,8 +412,8 @@ def build():
             if l < 3:
                 act(c("chx"), x, AF.Identity, scale=0.5)
             out = c("tw", s(0, 64))
-            mmul(out, p("ones", 0, 1), p("tie", 0, 1), True, False)
-            mmul(out, p("ones", 0, 1), p("mid", 0, 1), False, False)
+            mmul(out, p("ones", 0, 1, s(0, 128)), p("row", 0, 1, s(0, 64)), True, False)
+            mmul(out, p("ones", 0, 1, s(0, 128)), p("mid", 0, 1), False, False)
             mmul(out, c("IdB"), c("own"), False, False)
             for j in range(4):
                 mmul(c("tw", s(16 * j, 16 * j + 16)), c("Pk", 0), c("cT", s(0, 16)), False, False)
@@ -408,37 +440,43 @@ def build():
         red(col("v", 4), keys, Op.max)
         ts(col("bl", 0), col("v", 4), 16.0 / STEP, Op.mult, l16, Op.add)
         ts(c("H", s(4, 8)), c("z4"), col("v", 4), Op.add, 1.0 / STEP, Op.mult)
-        if t not in CHAINS:
-            ts(c(out, s(16, 20)), c("H", s(4, 8)), -STEP, Op.mult, col("v", 4), Op.add)
-        else:
-            ts(col("v", 5), col("H", 4), -STEP, Op.mult, col("v", 4), Op.add)
-            ts(c("tf", s(8, 12)), c("H", s(4, 8)), 3.0, Op.is_equal)
-            ts(c(out, s(16, 20)), c("tf", s(8, 12)), col("tf", 4), Op.mult, col("v", 5), Op.add)
+        for tok in [c("rs%d" % t)] * (t < 2) + [c(out, s(16, 20))]:
+            if t not in CHAINS:
+                ts(tok, c("H", s(4, 8)), -STEP, Op.mult, col("v", 4), Op.add)
+            else:
+                if tok[0] == out and t < 2:
+                    cp(tok, c("rs%d" % t))
+                    continue
+                ts(col("v", 5), col("H", 4), -STEP, Op.mult, col("v", 4), Op.add)
+                ts(c("tf", s(8, 12)), c("H", s(4, 8)), 3.0, Op.is_equal)
+                ts(tok, c("tf", s(8, 12)), col("tf", 4), Op.mult, col("v", 5), Op.add)
+            if tok[0] != out:
+                send([(-1 - t, tok, c("rl%d" % t), "rr%d" % t)])
         cp(c(out, s(0, 16)), ind(win, col("bl", 0)))
         send([(-1 - t, c(out), c("md%d" % t), "rd%d" % t)] + [(1, c(out), c("mv%d" % (t + 1)), "rv%d" % (t + 1))] * (t < 2))
         dma("S", ("yt", (slice(None), cols(t, t + 1))), col("md%d" % t, 16), "dy%d" % t, 2.0)
 
     def commit(t):
-        W, O = "Wl%d" % t, "Os%d" % t
-        for a, b in PIECES:
-            trn(c("Kt", cols(a, b)), c(O, cols(a, b)))
-            scan(c("Km", cols(a, b)), c("RS", cols(0, b - a)), c("Kt", cols(a, b)), 0.0, Op.min, Op.max)
-            cp(c("Ti", s(a, b)), c("Km", s(16 * a + 15, 16 * b, 16)))
-            ts(c("Tj", s(a, b)), c("Ti", s(a, b)), 4095, Op.bitwise_and)
-            ts(c("E", s(a, b)), c("Tj", s(a, b)), -float(MID), Op.add)
-            mmul(c("tw", s(a, b)), p("ones", 0, 1), p("mid", 0, 1, s(a, b)), True, False)
-            if b == M:
-                mmul(c("tw", s(a, b)), p("ones", 0, 1), p("depb", 0, 1, s(a, b)), False, False)
-            for j in range(4):
-                mmul(c("tw", s(a + j % 2, b, 2)), c("Pk", j), c("E", s(a + j // 2, b, 2)), False, j == 3)
+        W = "Wl%d" % t
+        for tw, (a, b) in zip(("tw", "kA", "thA"), PIECES):
+            top = c("Km", s(16 * a + 15, 16 * b, 16))
+            scan(c("Km", cols(a, b)), c("RS", cols(0, b - a)), c("Kt", cols(a, b)), LOW, Op.min, Op.max)
+            ts(c("Ti", s(a, b)), top, ROUND, Op.add, ROUND, Op.subtract)
+            tt(c("E", s(a, b)), top, c("Ti", s(a, b)), Op.subtract)
             if b < M:
-                tt(c("cmp", s(a, b)), c("tw", s(a, b)), c("dep", s(a, b)), Op.add)
+                mmul(c(tw, s(a, b)), p("ones", 0, 1), p("mid", 0, 1, s(a, b)), True, False)
+                for j in range(4):
+                    mmul(c(tw, s(a + j % 2, b, 2)), c("Pk", j), c("E", s(a + j // 2, b, 2)), False, j == 3)
             for q in INNER:
                 if a <= q < b:
-                    ts(c("ok", kids(q, 0)), c(W, kids(q, 1)), col("tw", q), Op.is_equal, col("ok", q), Op.mult)
-        tt(c("mm", s(0, a)), c("ok", s(0, a)), c("cmp", s(0, a)), Op.mult)
-        tt(c("mm", s(a, M)), c("ok", s(a, M)), c("tw", s(a, M)), Op.mult)
-        settle(t, c("mm"), c("xn"))
+                    ts(c("ok", kids(q, 0)), c(W, kids(q, 1)), col(tw, q), Op.is_equal, col("ok", q), Op.mult)
+        mmul(c(tw, s(0, M)), p("ones", 0, 1), p("mid", 0, 1, s(0, M)), True, False)
+        mmul(c(tw, s(0, M)), p("ones", 0, 1), p("depb", 0, 1), False, False)
+        mmul(c(tw, s(0, M)), c("IdF"), c("ok"), False, False)
+        for lo, hi in ((0, a), (a, M)):
+            for j in range(4):
+                mmul(c(tw, s(lo + j % 2, hi, 2)), c("Pk", j), c("E", s(lo + j // 2, hi, 2)), False, lo == a and j == 3)
+        settle(t, c(tw, s(0, M)), c("xn"))
 
     def chain_commit(t):
         W = "Wl%d" % t
@@ -606,7 +644,9 @@ def arrange(ops, deps, order):
     rng = np.random.RandomState(1)
     for trial in range(PL["passes"]):
         shift = {keys[int(k)]: float(v) for k, v in zip(rng.randint(0, len(keys), 3), rng.normal(0.0, 0.7, 3))}
-        new = turns([now[3][i] + shift.get(ops[i]["key"], 0.0) for i in range(n)], 2, (sweep, eager)[trial % 2])
+        if trial % 3 == 0:
+            shift[keys[rng.randint(0, len(keys))].split(".")[0]] = float(rng.normal(0.0, 1.5))
+        new = turns([now[3][i] + shift.get(ops[i]["key"], 0.0) + shift.get(ops[i]["key"].split(".")[0], 0.0) for i in range(n)], 2, (sweep, eager)[trial % 2])
         if new[0] <= now[0] + 0.05:
             now = new
             best = min(best, new, key=lambda x: x[0])

@@ -22,34 +22,33 @@ def _decl(where, dtype, **shapes):
         SCRATCH[name] = (where, [128] + list(shape), dtype)
 
 
-_decl("sbuf", I32, Q=[V], A=[V + 64], lane=[12], H=[8], Pi=[96], Pj=[96])
-_decl("sbuf", BF, K=[V], kc=[6144], ge=[16, 384], gec=[256], colb=[128], cm=[128], SelT=[4, 128], Ge=[144], row=[128], depb=[24],
-      IdB=[128], own=[64], mid=[64], ones=[128], B3=[128], Ea=[224], Eb=[512], kns=[384], knl=[384])
-_decl("sbuf", H16, Mk=[512], Id=[128], Pk=[4, 128], Sel=[16, 128], Wx=[96], Wy=[96], E=[24], ch=[32], cT=[32], candh=[384])
-_decl("sbuf", U16, bc=[16], parl=[24], sell=[20], l17=[6], pairs=[4], rootd=[2], rootv=[2], rs0=[4], rs1=[4], rl0=[4], rl1=[4], Ws0=[48], Ws1=[48], Ws2=[48], Wp1=[16], Wq1=[16], Wp2=[16], Wq2=[16],
-      Wl0=[26], Wl1=[26], Wl2=[26], cand=[384], L=[24], bl=[2], CT=[8], cu=[32])
-_decl("sbuf", F32, sc=[16], z4=[4], m4=[4], i16=[16], d16=[16], sg=[4], wide=[144], RR=[224], Rm=[224], Rz=[224],
-      PR=[24], Tt=[320], Gt=[288], t24=[24], u24=[24], w24=[24], ok=[24], IdF=[128], trash=[24], Wf=[24], Z=[28], tf=[12], dep=[24], g8=[24], Ti=[24],
-      Kt=[384], Km=[384], RS=[160], Pv=[52], Pr=[48], v=[8], x0s=[20], mv0=[20], mv1=[20], mv2=[20],
-      md0=[20], md1=[20], md2=[20], ms0=[20], ms1=[20], ms2=[20], CX=[64], chx=[16], thc=[256], xn=[384], xh=[256], kn=[384],
+_decl("sbuf", I32, Q=[V], A=[V + 64], lane=[12], Pi=[48], Pj=[48])
+_decl("sbuf", BF, K=[V], kc=[6144], ge=[16, 384], gec=[256], kqs=[96], kql=[96], colb=[128], cm=[128], SelT=[4, 128], Ge=[144], row=[128],
+      IdB=[128], own=[128], mid=[24], ones=[128], B3=[128], Ea=[224], Eb=[512], kns=[384], knl=[384])
+_decl("sbuf", H16, Mk=[512], Id=[128], Pk=[4, 128], Sel=[16, 128], Wx=[96], E=[24], ch=[32], cT=[32], candh=[384])
+_decl("sbuf", U16, bc=[16], parl=[36], sell=[20], l17=[6], pairs=[2], rootd=[2], rootv=[2], rs0=[4], rs1=[4], rl0=[4], rl1=[4], rn0=[4], rn1=[4], Ws0=[48], Ws1=[48], Ws2=[48], Wp1=[16], Wq1=[16], Wp2=[16], Wq2=[16],
+      Wl0=[26], Wl1=[26], Wl2=[26], cand=[384], L=[24], bl=[2], CT=[8], cu=[16])
+_decl("sbuf", F32, sc=[20], z4=[4], m4=[4], i16=[16], d16=[16], wide=[144], RR=[192], Rm=[192], Rz=[192],
+      PR=[36], Tt=[320], Gt=[288], t24=[24], u24=[24], w24=[24], ok=[24], trash=[24], Wf=[24], Wy=[24], Z=[24], tf=[16], dep=[24], g8=[24], Ti=[24],
+      Kt=[320], Km=[256], RS=[160], Pv=[52], Pr=[48], v=[12], x0s=[20], mv0=[20], mv1=[16], mv2=[16],
+      md1=[16], md2=[20], ms0=[16], ms1=[16], ms2=[20], CX=[64], chx=[16], thc=[256], xn=[384], xh=[256], kn=[384],
       RL=[51], RT=[32], X2=[64], X5=[32], S1=[272], S2=[566], S3=[164], Os0=[384], Os1=[384], Ol0=[384], Ol1=[384])
 _decl("psum", F32, kA=[512], kB=[512], kC=[512], thA=[512], thB=[512], tw=[512], dif=[512], cnt=[512])
 SC = ["lf", "l16", "grp", "odd", "l4", "evn", "o16", "g4", "nkp", "tokf", "g16", "look", "place", "back", "", "", "kp"]
-SCRATCH["sc"] = ("sbuf", [128, 20], F32)
 
 DMAS = ["dtok", "dx0", "dkap", "dQ", "dK", "dA", "dy0", "dy1", "dy2", "dyx", "dn0", "dn1"]
-MSGS = ["rx0", "rr0", "rr1", "rd0", "rd1", "rd2", "rv1", "rv2", "rka", "rkb", "rkc"] + ["r%s%d%d" % (m, t, j) for m in "WO" for t in range(3) for j in range(6)]
+MSGS = ["rx0", "rr0", "rr1", "rn0", "rn1", "rkq", "rd1", "rd2", "rv1", "rv2", "rka", "rkb", "rkc"] + ["r%s%d%d" % (m, t, j) for m in "WO" for t in range(3) for j in range(6)]
 SEMAPHORES = ["eV", "eA", "eT", "eG", "left"] + DMAS + MSGS
 
-PL = dict(cyc=0.83e-3, gather=1.56, scatter=3.8, hop=1.7, pe=0.83e-3, issue=0.3, byte=1.2e-3, same=0.22, cross=0.22, look=0.04, passes=1200)
-CHAINS = (2,)
-PIECES = [(0, 8), (8, 16), (16, 24)]
+PL = dict(cyc=1.0e-3, gather=1.56, scatter=3.8, hop=2.0, pe=1.0e-3, issue=0.4, byte=1.2e-3, same=0.24, cross=0.24, look=0.04, passes=1200, paces=(0.83, 1.25))
+PIECES = [(0, 8), (8, 16), (16, 20), (20, 24)]
 CHUNKS = [(0, 4), (4, 8), (8, 12), (12, 16), (16, 20), (20, 24)]
-LOOK_A = True
+EARLY = True
+CUTS = (0, 8, 16)
 FIRST = [[(1, 5), (5, 9)], [(1, 3), (3, 5), (5, 9)]]
-GATHERS = [[(0, 1, "V"), (1, 4, "V"), (4, 5, "A"), (5, 9, "A"), (9, 12, "A"), (12, 16, "A"), (16, 19, "A"), (19, 22, "A"), (22, 24, "V")],
-           [(0, 1, "V"), (1, 3, "A"), (3, 5, "A"), (5, 6, "V"), (6, 9, "A"), (9, 11, "V"), (11, 12, "A"), (12, 16, "A"), (16, 19, "A"), (19, 22, "A"),
-            (22, 24, "V")]]
+GATHERS = [[(0, 1, "V"), (1, 4, "V"), (4, 5, "A"), (5, 9, "A"), (9, 10, "V"), (10, 12, "A"), (12, 16, "A"), (16, 19, "A"), (19, 22, "A"), (22, 24, "A")],
+           [(0, 1, "V"), (1, 3, "A"), (3, 5, "A"), (5, 6, "V"), (6, 9, "A"), (9, 10, "V"), (10, 12, "A"), (12, 13, "V"), (13, 16, "A"), (16, 17, "V"),
+            (17, 19, "A"), (19, 22, "A"), (22, 24, "A")]]
 
 
 def c(name, *idx):
@@ -161,13 +160,12 @@ def build():
     iota(c("Ea"), [[0, 14], [1, 16]], 0, 0)
     iota(c("Eb"), [[0, 8], [32, 4], [1, 16]], 0, 0)
     iota(c("trash"), [[0, 6], [16, 4]], V, 0)
-    iota(c("own"), [[1, 4], [0, 16]], 0, 0)
+    iota(c("own"), [[0, 2], [1, 4], [0, 16]], 0, 0)
     iota(c("cm"), [[1, 32], [0, 4]], 0, 0)
     iota(c("B3"), [[1, 8], [0, 16]], 0, 0)
     iota(p("row", 0, 1), [[0, 8], [-4096, 16]], 15 * 4096, 0)
-    iota(c("depb"), [[1, 24]], 0, 0)
-    ts(c("dep"), c("depb"), STEP, Op.mult)
-    ts(c("depb"), c("dep"), -2.0 ** 23, Op.add)
+    ts(c("dep"), c("wide", s(15, 39)), STEP, Op.mult)
+    ts(c("tf", s(12, 16)), c("dep", s(0, 4)), float(MID), Op.add)
     cp(col("lf"), col("lane", 0))
     for j, (sh, an) in enumerate([(0, 15), (4, 7), (4, 1), (0, 3)]):
         ts(col("lane", 1 + j), col("lane", 0), sh, Op.arith_shift_right, an, Op.bitwise_and)
@@ -179,7 +177,7 @@ def build():
     ts(col("g16"), grp, 16.0, Op.mult)
     ts(col("place"), l16, -4096.0, Op.mult, 15 * 4096.0 - MID, Op.add)
     ts(col("look"), col("odd"), 2.0 ** 22, Op.mult, col("place"), Op.add)
-    ms(c("z4"), 0.0); ms(c("m4"), -float(MID)); ms(col("ok", 0), 1.0); ms(col("tf", 3), 0.0)
+    ms(c("z4"), 0.0); ms(c("m4"), float(MID)); ms(col("ok", 0), 1.0); ms(c("ms2", s(16, 20)), 0.0)
     ms(c("RS"), HIGH); ms(c("RS", s(0, 160, 16)), LOW)
     cp(col("tokf"), col("lane", 8))
     ts(c("x0s", s(16, 20)), c("z4"), col("tokf"), Op.add)
@@ -206,30 +204,27 @@ def build():
     fill("RR", [leaf(n) if ROW[n] else 32 * lane(n) + 15 for n in range(9, 19)] + [15] * 6, 128)
     fill("RR", [{0: 16 + 32 * lane(n), 1: 115, 15: 147}[ROW[n]] for n in range(19, 24)] + [80] * 11, 144)
     iota(c("RR", s(160, 192)), [[1, 8], [1, 4]], 0, 0)
-    iota(c("RR", s(192, 224)), [[1, 8], [0, 4]], 0, 0)
     ts(c("RR", s(160, 176)), c("RR", s(160, 176)), 3.0, Op.min)
     ts(c("RR", s(176, 192)), c("RR", s(176, 192)), 7.0, Op.min)
-    entries(48, 224)
+    entries(48, 192)
     ts(c("l17", s(0, 5)), c("Rz", s(63, 128, 16)), col("o16"), Op.add)
-    ts(col("sg", 0), col("Rz", 15), 34.0, Op.mult, 16.0, Op.add)
-    ts(pick(3), col("sg", 0), col("o16"), Op.add)
-    ts(col("sg", 1), col("sg", 0), 34.0 * 4 + 16, Op.min)
-    ts(pick(7), col("sg", 1), col("o16"), Op.add)
-    ts(col("sg", 3), col("sg", 0), 34.0 * 2 + 16, Op.min)
-    ts(pick(8), col("sg", 3), col("o16"), Op.add)
-    ts(col("sg", 2), col("Rz", 143), 96.0, Op.is_lt, col("o16"), Op.mult)
-    ts(pick(4), col("Rz", 143), col("sg", 2), Op.add)
+    ts(col("g8", 0), col("Rz", 15), 34.0, Op.mult, 16.0, Op.add)
+    ts(pick(3), col("g8", 0), col("o16"), Op.add)
+    ts(pick(7), col("g8", 0), 34.0 * 4 + 16, Op.min, col("o16"), Op.add)
+    ts(pick(8), col("g8", 0), 34.0 * 2 + 16, Op.min, col("o16"), Op.add)
+    ts(col("g8", 2), col("Rz", 143), 96.0, Op.is_lt, col("o16"), Op.mult)
+    ts(pick(4), col("Rz", 143), col("g8", 2), Op.add)
     ts(pick(5), col("Rz", 159), col("o16"), Op.add)
     ts(pick(6), pick(1), 15.0, Op.add, 95.0, Op.min)
-    cp(c("pairs"), c("Rz", s(175, 224, 16)))
-    fill("PR", [16 * PAR[n] for n in range(1, 19)] + [16 * (PAR[n] - 8) for n in range(19, 24)] + [112])
+    cp(c("pairs"), c("Rz", s(175, 192, 16)))
+    fill("PR", [16 * PAR[n] for n in range(1, 19)] + [16 * (PAR[n] - 8) for n in range(19, 24)] + [112]
+         + [16 * PAR[n] for n in (12, 12, 9, 9, 15, 15)] + [32 * lane(n) for n in range(19, 24)] + [64])
     ts(c("parl"), c("PR"), l16, Op.add)
     cp(c("bc"), c("i16"))
     cp(c("colb"), c("wide", s(15, 143)))
     ts(c("Mk"), c("Eb"), l16, Op.is_le, 8192.0, Op.mult)
     ts(c("own"), c("own"), col("l4"), Op.is_equal, 0.25, Op.mult)
     ts(c("IdB"), c("colb"), col("lf"), Op.is_equal, 2.0 ** 23, Op.mult)
-    cp(c("IdF"), c("IdB"))
     ts(c("Id"), c("colb"), col("lf"), Op.is_equal)
     ts(c("Ge"), c("wide"), col("g16"), Op.is_equal, 2.0 ** 17, Op.mult)
     ms(p("mid", 0, 1), float(MID)); ms(p("ones", 0, 1), 1.0)
@@ -280,10 +275,7 @@ def build():
         Wp, Wq = "Wp%d" % t, "Wq%d" % t
 
         def turn(a, b, twice):
-            if LOOK_A:
-                act(c("Gt", s(a, b)), ind(Aw, twice), AF.Identity, bias=col("look"))
-            else:
-                ts(c("Gt", s(a, b)), ind(Aw, twice), col("look"), Op.add)
+            act(c("Gt", s(a, b)), ind(Aw, twice), AF.Identity, bias=col("look"))
             trn(c("Tt", s(a, b)), c("Gt", s(a, b)))
 
         tag[0] = "d%d0" % t
@@ -305,6 +297,8 @@ def build():
         turn(128, 224, c(Wp, s(0, 6)))
         scan(c("S2", s(0, 96)), c("RS", s(0, 96)), c("Tt", s(128, 224)), LOW, Op.min, Op.max)
         parents(Wq, c("S2", s(0, 96)), 6, 32, [(10, 2), (12, 2), (14, 2)])
+        if t == 2 and EARLY:
+            send([(3, c(Wq, s(10, 16)), c("Wq1", s(0, 6)), "rW23")])
         tag[0] = "e%d1" % t
         act(c("X2"), ind(c("Tt", s(128, 256)), c("l17", s(0, 4))))
         for r in range(7, -1, -1):
@@ -333,16 +327,15 @@ def build():
         cp(c("Wf", s(19, 24)), c(W, s(32, 37)))
         for j, bank in enumerate(("dif", "cnt", "dif")):
             a, b = 8 * j, 8 * j + 8
-            later, own = c("Wx", s(32 * j, 32 * j + 32)), c("Wy", s(32 * j, 32 * j + 32))
+            later = c("Wx", s(32 * j, 32 * j + 32))
             ts(later, ind(c("Wf", s(a, b)), c("pairs", s(0, 2))), -float(MID), Op.add)
-            ts(own, ind(c("Wf", s(a, b)), c("pairs", s(2, 4))), -1.0, Op.mult, float(MID), Op.add)
+            act(c("Wy", s(a, b)), c("Wf", s(a, b)), AF.Identity, scale=-1.0, bias=float(MID))
             mmul(c(bank), c("Id"), c("Mk"), True, False)
             for q in range(16):
-                mmul(c(bank, s(q, 512, 16)), c("Sel", q), later, False, False)
-                mmul(c(bank, s(q, 512, 16)), c("Id"), own, False, q == 15)
-            act(c("Eb"), c(bank), AF.Abs)
+                mmul(c(bank, s(q, 512, 16)), c("Sel", q), later, False, q == 15)
             for n in range(8):
                 e = s(64 * n, 64 * n + 64 - 16 * (n % 4))
+                act(c("Eb", e), c(bank, e), AF.Abs, bias=col("Wy", a + n))
                 act(c("Eb", e), c("Eb", e), AF.Relu, bias=4096.0, scale=-4096.0, accum_out=col("t24", a + n))
             tt(c("u24", s(a, b)), c("t24", s(a, b)), c("trash", s(a, b)), Op.min)
             tt(c("w24", s(a, b)), c("u24", s(a, b)), c("Wf", s(a, b)), Op.max)
@@ -370,8 +363,9 @@ def build():
 
     def verify(t):
         W, mv = "Wl%d" % t, "mv%d" % t
-        cp(c("rootv"), c(mv, s(16, 18)))
-        cp(c("cand", cols(0, 1)), ind(Qw, col("rootv", 0)))
+        if t == 0:
+            cp(c("rootv"), c(mv, s(16, 18)))
+        cp(c("cand", cols(0, 1)), ind(Qw, col("rn0" if t else "rootv", 0)))
         for a, b in FIRST[t] + DEPTH[1:]:
             cp(c("cand", cols(a, b)), ind(Qw, c(W, s(a + 1, b + 1))))
             act(c("kn", cols(a, b)), ind(Kw, c(W, s(a + 1, b + 1))))
@@ -380,7 +374,7 @@ def build():
         for lo, hi, who in GATHERS[t]:
             (cp if who == "V" else act)(c("kc", s(256 * lo, 256 * hi)), ind(Kw, c("cand", cols(lo, hi))))
         for j, (a, b) in enumerate(PIECES):
-            bank = "k" + "ABC"[j % 3]
+            bank = "k" + "ABCB"[j]
             ts(c("candh", cols(a, b)), c("cand", cols(a, b)), -float(MID), Op.add)
             mmul(c(bank, cols(a, b)), p("row", 0, 1), p("ones", 0, 1, cols(0, b - a)), True, False)
             mmul(c(bank, cols(a, b)), c("Id"), c("candh", cols(a, b)), False, False)
@@ -391,103 +385,104 @@ def build():
                     for k in range(16):
                         tt(c("ge", k, cols(lo, hi)), c("kc", s(256 * lo + k, 256 * hi, 16)), c(th, cols(lo, hi)), Op.is_ge)
                         mmul(c(bank, cols(lo, hi)), c("Ge", s(15 - k, 143 - k)), c("ge", k, cols(lo, hi)), False, hi == b and k == 15)
-            if t not in CHAINS:
+            if j < 2:
                 trn(c("Kt", cols(a, b)), c(bank, cols(a, b)))
             act(c("Os%d" % t, cols(a, b)), c(bank, cols(a, b)), AF.Identity, bias=float(MID))
             send([(-1 - t, c("Os%d" % t, cols(a, b)), c("Ol%d" % t, cols(a, b)), "rO%d%d" % (t, j))])
 
     def chain(t):
         mv = "mv%d" % t
-        cp(c("CT", s(0, 2)), c(mv, s(16, 18)))
         act(c("CX", s(0, 16)), c(mv, s(0, 16)))
         for l in range(4):
-            tk, x = c("CT", s(2 * l, 2 * l + 2)), c("CX", s(16 * l, 16 * l + 16))
-            cp(c("cu"), ind(Qw, tk))
+            tk = c("CT", s(2 * l, 2 * l + 2)) if l else c("rn%d" % (t - 1), s(0, 2))
+            x = c("CX", s(16 * l, 16 * l + 16)) if l else c(mv, s(0, 16))
+            cp(c("cu"), ind(Qw, c(tk[0], s(tk[1][1].start, tk[1][1].start + 1))))
             if l:
                 tt(x, ind(Kw, col("CT", 2 * l)), c("chx"), Op.add)
-            for j in range(2):
-                act(c("thc", s(128 * j, 128 * j + 128)), ind(x, c("bc", s(8 * j, 8 * j + 8))), AF.Identity, bias=col("nkp"))
-            ts(c("ch"), c("cu"), -float(MID), Op.add)
+            for a, b in zip(CUTS, CUTS[1:]):
+                act(c("thc", cols(a, b)), ind(x, c("bc", s(a, b))), AF.Identity, bias=col("nkp"))
+            ts(c("ch"), ind(Qw, tk), -float(MID), Op.add)
             trn(c("cT"), c("ch"))
             if l < 3:
                 act(c("chx"), x, AF.Identity, scale=0.5)
-            out = c("tw", s(0, 64))
-            mmul(out, p("ones", 0, 1, s(0, 128)), p("row", 0, 1, s(0, 64)), True, False)
-            mmul(out, p("ones", 0, 1, s(0, 128)), p("mid", 0, 1), False, False)
-            mmul(out, c("IdB"), c("own"), False, False)
+            tw = ("tw", "thA")[l % 2]
+            out, bare = c(tw, s(0, 64)), c(tw, s(64, 128))
+            mmul(c(tw, s(0, 128)), p("ones", 0, 1), p("row", 0, 1), True, False)
+            mmul(c(tw, s(0, 128)), c("IdB"), c("own"), False, False)
             for j in range(4):
-                mmul(c("tw", s(16 * j, 16 * j + 16)), c("Pk", 0), c("cT", s(0, 16)), False, False)
-                mmul(c("tw", s(16 * j, 16 * j + 16)), c("Pk", 3), c("cT", s(16, 32)), False, False)
-            for j in range(2):
-                tt(c("gec", s(128 * j, 128 * j + 128)), ind(Kw, c("cu", s(8 * j, 8 * j + 8))), c("thc", s(128 * j, 128 * j + 128)), Op.is_ge)
+                mmul(c(tw, s(16 * j, 16 * j + 16)), c("Pk", 0), c("cT", s(0, 16)), False, False)
+                mmul(c(tw, s(16 * j, 16 * j + 16)), c("Pk", 3), c("cT", s(16, 32)), False, False)
+            for a, b in zip(CUTS, CUTS[1:]):
+                tt(c("gec", cols(a, b)), ind(Kw, c("cu", s(a, b))), c("thc", cols(a, b)), Op.is_ge)
             for j in range(4):
-                mmul(out, c("SelT", j), c("gec", s(64 * j, 64 * j + 64)), False, j == 3)
+                mmul(out, c("SelT", j), c("gec", s(64 * j, 64 * j + 64)), False, False)
+                mmul(bare, c("SelT", j), c("gec", s(64 * j, 64 * j + 64)), False, j == 3)
             red(col("v", l), out, Op.max)
-            ts(c("H", s(0, 2)), c("m4", s(0, 2)), col("v", l), Op.add, 2.0 ** -12, Op.mult)
+            red(col("v", 8 + l), bare, Op.max)
             if l < 3:
-                ts(c("CT", s(2 * l + 2, 2 * l + 4)), c("H", s(0, 2)), -4096.0, Op.mult, col("v", l), Op.add)
-            if l == 2:
-                cp(c("tf", s(0, 3)), c("CT", s(2, 8, 2)))
-                tt(c("Z", s(0, 4)), c("tf", s(0, 4)), c("dep", s(0, 4)), Op.add)
-                cp(col("Z", 4), col("Z", 0))
-            if l == 3:
-                ts(col("tf", 4), col("H", 0), -4096.0, Op.mult, col("v", l), Op.add)
+                ts(c("CT", s(2 * l + 2, 2 * l + 4)), c("m4", s(0, 2)), col("v", l), Op.add, col("v", 8 + l), Op.subtract)
+                ts(col("tf", l), col("m4", 0), col("v", l), Op.add, col("v", 8 + l), Op.subtract)
+                ts(col("tf", 4 + l), col("tf", 12 + l), col("v", l), Op.add, col("v", 8 + l), Op.subtract)
 
     kids = lambda q, by: s(PAR.index(q, 1) + by, M - PAR[::-1].index(q) + by)
 
-    def settle(t, keys, win):
+    def settle(t, win):
         out = "ms%d" % t
-        red(col("v", 4), keys, Op.max)
-        ts(col("bl", 0), col("v", 4), 16.0 / STEP, Op.mult, l16, Op.add)
-        ts(c("H", s(4, 8)), c("z4"), col("v", 4), Op.add, 1.0 / STEP, Op.mult)
-        for tok in [c("rs%d" % t)] * (t < 2) + [c(out, s(16, 20))]:
-            if t not in CHAINS:
-                ts(tok, c("H", s(4, 8)), -STEP, Op.mult, col("v", 4), Op.add)
-            else:
-                if tok[0] == out and t < 2:
-                    cp(tok, c("rs%d" % t))
-                    continue
-                ts(col("v", 5), col("H", 4), -STEP, Op.mult, col("v", 4), Op.add)
-                ts(c("tf", s(8, 12)), c("H", s(4, 8)), 3.0, Op.is_equal)
-                ts(tok, c("tf", s(8, 12)), col("tf", 4), Op.mult, col("v", 5), Op.add)
-            if tok[0] != out:
-                send([(-1 - t, tok, c("rl%d" % t), "rr%d" % t)])
+        ts(col("bl", 0), col("v", 6), 16.0 / STEP, Op.mult, l16, Op.add)
         cp(c(out, s(0, 16)), ind(win, col("bl", 0)))
-        send([(-1 - t, c(out), c("md%d" % t), "rd%d" % t)] + [(1, c(out), c("mv%d" % (t + 1)), "rv%d" % (t + 1))] * (t < 2))
-        dma("S", ("yt", (slice(None), cols(t, t + 1))), col("md%d" % t, 16), "dy%d" % t, 2.0)
+        send([(1, c(out), c("mv%d" % (t + 1)), "rv%d" % (t + 1))] * (t < 2) + [(-1 - t, c(out), c("md%d" % t), "rd%d" % t)] * (t > 0))
+
+    def note(t):
+        if t < 2:
+            cp(col("Pv", 48 + t), col("rl%d" % t, 0))
+        dma("S", ("yt", (slice(None), cols(t, t + 1))), col("Pv", 48 + t) if t < 2 else col("md2", 16), "dy%d" % t, 2.0)
 
     def commit(t):
         W = "Wl%d" % t
-        for tw, (a, b) in zip(("tw", "kA", "thA"), PIECES):
+        for tw, (a, b) in zip(("tw", "kA"), PIECES[:2]):
             top = c("Km", s(16 * a + 15, 16 * b, 16))
             scan(c("Km", cols(a, b)), c("RS", cols(0, b - a)), c("Kt", cols(a, b)), LOW, Op.min, Op.max)
             ts(c("Ti", s(a, b)), top, ROUND, Op.add, ROUND, Op.subtract)
             tt(c("E", s(a, b)), top, c("Ti", s(a, b)), Op.subtract)
-            if b < M:
-                mmul(c(tw, s(a, b)), p("ones", 0, 1), p("mid", 0, 1, s(a, b)), True, False)
-                for j in range(4):
-                    mmul(c(tw, s(a + j % 2, b, 2)), c("Pk", j), c("E", s(a + j // 2, b, 2)), False, j == 3)
-            for q in INNER:
-                if a <= q < b:
-                    ts(c("ok", kids(q, 0)), c(W, kids(q, 1)), col(tw, q), Op.is_equal, col("ok", q), Op.mult)
-        mmul(c(tw, s(0, M)), p("ones", 0, 1), p("mid", 0, 1, s(0, M)), True, False)
-        mmul(c(tw, s(0, M)), p("ones", 0, 1), p("depb", 0, 1), False, False)
-        mmul(c(tw, s(0, M)), c("IdF"), c("ok"), False, False)
-        for lo, hi in ((0, a), (a, M)):
+            mmul(c(tw, s(a, b)), p("ones", 0, 1), p("mid", 0, 1, s(a, b)), True, False)
             for j in range(4):
-                mmul(c(tw, s(lo + j % 2, hi, 2)), c("Pk", j), c("E", s(lo + j // 2, hi, 2)), False, lo == a and j == 3)
-        settle(t, c(tw, s(0, M)), c("xn"))
+                mmul(c(tw, s(a + j % 2, b, 2)), c("Pk", j), c("E", s(a + j // 2, b, 2)), False, j == 3)
+            for q in INNER:
+                if a <= q < min(b, 9):
+                    ts(c("ok", kids(q, 0)), c(W, kids(q, 1)), col(tw, q), Op.is_equal, col("ok", q), Op.mult)
+        tt(c("Z", s(0, 19)), c("ok", s(0, 19)), c("dep", s(0, 19)), Op.mult)
+        for q in INNER[5:]:
+            ts(c("ok", kids(q, 0)), c("dep", kids(q, 0)), col("ok", q), Op.mult)
+        for n in range(19, M):
+            ts(col("Z", n), col(W, n + 1), col(tw, PAR[n]), Op.is_equal, col("ok", n), Op.mult)
+        red(col("v", 6), c("Z"), Op.max)
+        settle(t, c("xn"))
+        for j, who in enumerate(("evn", "odd")):
+            ts(c("Kt", s(256 + 16 * j, 272 + 16 * j)), ind(c("Os%d" % t), col("bl", 0)), -float(MID), Op.add, col(who), Op.mult)
+        trn(c("Kt", s(288, 320)), c("Kt", s(256, 288)))
+        red(col("v", 4), c("Kt", s(288, 320)), Op.max)
+        ts(col("v", 5), col("v", 4), ROUND, Op.add, ROUND, Op.subtract)
+        ts(c("rs%d" % t), c("m4"), col("v", 4), Op.add, col("v", 5), Op.subtract)
+        send([(-1 - t, c("rs%d" % t), c("rl%d" % t), "rr%d" % t), (1, c("rs%d" % t), c("rn%d" % t), "rn%d" % t)])
+        note(t)
 
     def chain_commit(t):
         W = "Wl%d" % t
-        ts(c("Z", kids(0, 4)), c(W, kids(0, 1)), col("tf", 0), Op.is_equal, col("Z", 1), Op.mult)
-        ts(c("g8", s(1, 6)), c("Z", s(5, 10)), 0.5, Op.is_gt, col("Z", 2), Op.mult)
-        ts(c("g8", s(17, 20)), c("Z", s(5, 8)), 0.5, Op.is_gt, col("Z", 3), Op.mult)
+        ts(c("Z", kids(0, 0)), c(W, kids(0, 1)), col("tf", 0), Op.is_equal, STEP, Op.mult)
+        ts(c("g8", s(1, 6)), c("Z", s(1, 6)), 2.0, Op.mult)
+        ts(c("g8", s(17, 20)), c("Z", s(1, 4)), 3.0, Op.mult)
         for q in INNER[1:]:
             if q > 8:
-                ts(col("g8", q), col(W, q + 1), col("tf", 1), Op.is_equal, col("g8", 16 + PAR[q]), Op.mult)
-            ts(c("Z", kids(q, 4)), c(W, kids(q, 1)), col("tf", 1 + (q > 8)), Op.is_equal, col("g8", q), Op.mult)
-        settle(t, c("Z", s(4, 28)), c("CX"))
+                own = col("Wq1", 2 * [12, 9, 15].index(q)) if EARLY else col(W, q + 1)
+                ts(col("g8", q), own, col("tf", 1), Op.is_equal, col("g8", 16 + PAR[q]), Op.mult)
+            ts(c("Z", kids(q, 0)), c(W, kids(q, 1)), col("tf", 1 + (q > 8)), Op.is_equal, col("g8", q), Op.mult)
+        red(col("v", 6), c("Z", s(1, M)), Op.max)
+        ts(c("tf", s(8, 11)), c("tf", s(4, 7)), col("v", 6), Op.subtract)
+        ts(col("tf", 7), col("tf", 15), col("v", 6), Op.subtract)
+        ts(col("tf", 11), col("tf", 7), col("v", 3), Op.add, col("v", 11), Op.subtract)
+        red(col("ms2", 16), c("tf", s(8, 12)), Op.min, apply_absolute_value=True)
+        settle(t, c("CX"))
+        note(t)
 
     for t in range(2):
         tag[0] = "d%d" % t
@@ -498,13 +493,10 @@ def build():
             draft(t)
         tag[0] = "u%d" % t
         spare(t)
-        if t in CHAINS:
-            tag[0] = "h%d" % t
-            chain(t)
         tag[0] = "v%d" % t
         verify(t)
         tag[0] = "m%d" % t
-        (chain_commit if t in CHAINS else commit)(t)
+        commit(t)
         tag[0] = "s%d" % t
         scatter(t)
     tag[0] = "d2"
@@ -512,6 +504,9 @@ def build():
     tag[0] = "h2"
     chain(2)
     tag[0] = "v2"
+    if EARLY:
+        act(c("kqs"), ind(Kw, c("Wq1", s(0, 6))))
+        send([(-3, c("kqs"), c("kql"), "rkq")])
     for d, (a, b) in enumerate(DEPTH):
         act(c("kns", cols(a, b)), ind(Kw, c("Wl2", s(a + 1, b + 1))))
         send([(-3, c("kns", cols(a, b)), c("knl", cols(a, b)), "rk" + "abc"[d])])
@@ -519,8 +514,14 @@ def build():
     chain_commit(2)
     tag[0] = "f"
     states(1, "knl", c("md1", s(0, 16)), near=True)
-    states(2, "knl", near=True)
-    states(3, "knl")
+    if EARLY:
+        tt(c("kn", s(0, 96)), ind(c("xh", s(0, 96)), c("parl", s(24, 30))), c("kql"), Op.add)
+        act(c("xh", s(128, 224)), c("kn", s(0, 96)), AF.Identity, scale=0.5)
+        tt(c("xn", s(144, 304)), ind(c("xh", s(0, 96)), c("parl", s(8, 18))), c("knl", s(144, 304)), Op.add)
+        tt(c("xn", s(304, 384)), ind(c("xh", s(128, 224)), c("parl", s(30, 35))), c("knl", s(304, 384)), Op.add)
+    else:
+        states(2, "knl", near=True)
+        states(3, "knl")
     dma("S", ("yn", (slice(None), s(0, 304))), c("xn", s(0, 304)), "dn0", 2.4)
     dma("A", ("yn", (slice(None), s(304, 384))), c("xn", s(304, 384)), "dn1", 2.1)
     dma("A", ("yx", (slice(None),)), c("md2", s(0, 16)), "dyx", 2.0)
@@ -636,10 +637,21 @@ def arrange(ops, deps, order):
             prio = eager(succ, pred, fin, [o["lat"] for o in ops])[1]
         return best
 
+    def replay(seq, pace):
+        fin, free = [0.0] * n, {}
+        for i in seq:
+            o = ops[i]
+            at = max([free.get(o["e"], 0.0)] + [fin[j] + w for j, w in pred[i]])
+            fin[i] = at + o["c"] * (1.0 if o["m"] in ("send", "dma") else pace)
+            if o["e"] != "R":
+                free[o["e"]] = fin[i]
+        return max(fin[i] + ops[i]["lat"] for i in range(n))
+
+    judge = lambda x: (x[0] + sum(replay(x[1], pace) / pace ** 0.6 for pace in PL["paces"]),) + x[1:]
     prio = [0.0] * n
     for i in range(n - 1, -1, -1):
         prio[i] = ops[i]["c"] + max([w + prio[k] for k, w in succ[i]] + [ops[i]["lat"]])
-    best = now = turns(prio, 6, sweep)
+    best = now = judge(turns(prio, 6, sweep))
     keys = sorted({o["key"] for o in ops})
     rng = np.random.RandomState(1)
     for trial in range(PL["passes"]):
@@ -647,7 +659,8 @@ def arrange(ops, deps, order):
         if trial % 3 == 0:
             shift[keys[rng.randint(0, len(keys))].split(".")[0]] = float(rng.normal(0.0, 1.5))
         new = turns([now[3][i] + shift.get(ops[i]["key"], 0.0) + shift.get(ops[i]["key"].split(".")[0], 0.0) for i in range(n)], 2, (sweep, eager)[trial % 2])
-        if new[0] <= now[0] + 0.05:
+        new = judge(new)
+        if new[0] <= now[0] + 0.12:
             now = new
             best = min(best, new, key=lambda x: x[0])
     return ops, deps, best[1], best[2], order

import numpy as np
from concourse.bass import DstId, RemoteDMATransfer
from concourse.mybir import AluOpType as Op, AxisListType, ActivationFunctionType as AF

N, V, M = 8, 3712, 24
PAR = [0, 0, 0, 0, 0, 0, 0, 0, 0, 1, 1, 1, 2, 2, 2, 3, 3, 5, 5, 9, 9, 12, 12, 15]
ROW = [0, 0, 1, 2, 3, 4, 5, 6, 7, 0, 8, 9, 0, 10, 11, 0, 12, 13, 14, 0, 15, 0, 1, 0]
INNER = sorted(set(PAR))
DEPTH = [(1, 9), (9, 19), (19, 24)]
MID = 1856
HIGH = 2.0 ** 24
LOW = -8192.0
ROUND = 1.5 * 2.0 ** 35
STEP = 2.0 ** 17

F32, BF, H16, I32, U16 = "float32", "bfloat16", "float16", "int32", "uint16"
SCRATCH = {}


def _decl(where, dtype, **shapes):
    for name, shape in shapes.items():
        SCRATCH[name] = (where, [128] + list(shape), dtype)


_decl("sbuf", I32, Q=[V], A=[V + 64], lane=[12], Pi=[48], Pj=[48])
_decl("sbuf", BF, K=[V], kc=[6144], ge=[16, 384], gec=[256], kqs=[96], kql=[96], colb=[128], cm=[128], SelT=[4, 128], Ge=[144], row=[128],
      IdB=[128], own=[128], mid=[24], ones=[128], B3=[128], Ea=[224], Eb=[512], kns=[384], knl=[384])
_decl("sbuf", H16, Mk=[512], Id=[128], Pk=[4, 128], Sel=[16, 128], Wx=[96], E=[24], ch=[32], cT=[32], candh=[384])
_decl("sbuf", U16, bc=[16], parl=[36], sell=[20], l17=[6], pairs=[2], rootd=[2], rootv=[2], rs0=[4], rs1=[4], rl0=[4], rl1=[4], rn0=[4], rn1=[4], Ws0=[48], Ws1=[48], Ws2=[48], Wp1=[16], Wq1=[16], Wp2=[16], Wq2=[16],
      Wl0=[26], Wl1=[26], Wl2=[26], cand=[384], L=[24], bl=[2], CT=[8], cu=[16])
_decl("sbuf", F32, sc=[20], z4=[4], m4=[4], i16=[16], d16=[16], wide=[144], RR=[192], Rm=[192], Rz=[192],
      PR=[36], Tt=[320], Gt=[288], t24=[24], u24=[24], w24=[24], ok=[24], trash=[24], Wf=[24], Wy=[24], Z=[24], tf=[16], dep=[24], g8=[24], Ti=[24],
      Kt=[320], Km=[256], RS=[160], Pv=[52], Pr=[48], v=[12], x0s=[20], mv0=[20], mv1=[16], mv2=[16],
      md1=[16], md2=[20], ms0=[16], ms1=[16], ms2=[20], CX=[64], chx=[16], thc=[256], xn=[384], xh=[256], kn=[384],
      RL=[51], RT=[32], X2=[64], X5=[32], S1=[272], S2=[566], S3=[164], Os0=[384], Os1=[384], Ol0=[384], Ol1=[384])
_decl("psum", F32, kA=[512], kB=[512], kC=[512], thA=[512], thB=[512], tw=[512], dif=[512], cnt=[512])
SC = ["lf", "l16", "grp", "odd", "l4", "evn", "o16", "g4", "nkp", "tokf", "g16", "look", "place", "back", "", "", "kp"]

DMAS = ["dtok", "dx0", "dkap", "dQ", "dK", "dA", "dy0", "dy1", "dy2", "dyx", "dn0", "dn1"]
MSGS = ["rx0", "rr0", "rr1", "rn0", "rn1", "rkq", "rd1", "rd2", "rv1", "rv2", "rka", "rkb", "rkc"] + ["r%s%d%d" % (m, t, j) for m in "WO" for t in range(3) for j in range(6)]
SEMAPHORES = ["eV", "eA", "eT", "eG", "left"] + DMAS + MSGS

PL = dict(cyc=1.0e-3, gather=1.56, scatter=3.8, hop=2.0, pe=1.0e-3, issue=0.4, byte=1.2e-3, same=0.24, cross=0.24, look=0.04, passes=1200, paces=(0.83, 1.25))
PIECES = [(0, 8), (8, 16), (16, 20), (20, 24)]
CHUNKS = [(0, 4), (4, 8), (8, 12), (12, 16), (16, 20), (20, 24)]
EARLY = True
CUTS = (0, 8, 16)
FIRST = [[(1, 5), (5, 9)], [(1, 3), (3, 5), (5, 9)]]
GATHERS = [[(0, 1, "V"), (1, 4, "V"), (4, 5, "A"), (5, 9, "A"), (9, 10, "V"), (10, 12, "A"), (12, 16, "A"), (16, 19, "A"), (19, 22, "A"), (22, 24, "A")],
           [(0, 1, "V"), (1, 3, "A"), (3, 5, "A"), (5, 6, "V"), (6, 9, "A"), (9, 10, "V"), (10, 12, "A"), (12, 13, "V"), (13, 16, "A"), (16, 17, "V"),
            (17, 19, "A"), (19, 22, "A"), (22, 24, "A")]]


def c(name, *idx):
    return (name, (slice(None),) + idx)


def p(name, lo, hi, *idx):
    return (name, (slice(lo, hi),) + idx)


def s(a, b, step=None):
    return slice(a, b, step)


def ind(win, off):
    return ("*", win, off)


def elems(r):
    key = (r[0], str(r[1][1:]))
    if key not in ELEMS:
        shape = SCRATCH[r[0]][1][1:]
        ELEMS[key] = np.arange(int(np.prod(shape))).reshape(shape)[r[1][1:]].reshape(-1)
    return ELEMS[key]


ELEMS = {}


def build():
    ops, tag = [], ["c"]
    CYC, GATHER, SCATTER, HOP = PL["cyc"], PL["gather"], PL["scatter"], PL["hop"]

    def add(eng, meth, args, outs, ins, cost, kw=None, **more):
        reads = []
        for r in ins:
            if isinstance(r, tuple):
                reads += [r[1], r[2]] if r[0] == "*" else [r]
        writes = []
        for r in outs:
            if r[0] == "*":
                writes.append(r[1])
                reads.append(r[2])
            else:
                writes.append(r)
        d = dict(e=eng, m=meth, a=args, k=kw or {}, r=[x for x in reads if x[0] in SCRATCH], w=[x for x in writes if x[0] in SCRATCH], c=cost, lat=0.0)
        d["key"] = tag[0] + "." + (args[0][3] if meth == "send" else writes[0][0])
        d.update(more)
        ops.append(d)

    def vcost(out, ins, two=False):
        if out[0] == "*":
            return 0.05 + SCATTER * CYC * 16 * len(elems(out[2]))
        if ins[0][0] == "*":
            return 0.05 + GATHER * CYC * len(elems(out))
        n = len(elems(ins[0]))
        if two:
            n *= 1 if "psum" in (SCRATCH[ins[0][0]][0], SCRATCH[ins[1][0]][0]) else 2
        elif all(SCRATCH[x[0]][2] in (BF, H16, U16) for x in [out] + ins):
            n *= 0.5
        return max(64, n) * CYC

    def cp(out, a): add("V", "cp", [out, a], [out], [a], vcost(out, [a]))
    def tt(out, a, b, op): add("V", "tt", [out, a, b, op], [out], [a, b], vcost(out, [a, b], True))
    def ts(out, a, s1, op0, s2=None, op1=None):
        add("V", "ts", [out, a, s1, s2, op0] + ([op1] if op1 is not None else []), [out], [a, s1, s2], vcost(out, [a]))
    def red(out, a, op, **kw): add("V", "red", [out, a, AxisListType.X, op], [out], [a], vcost(out, [a]), kw)
    def trn(out, a): add("V", "trn", [out, a], [out], [a], vcost(out, [a]))
    def ms(out, val): add("V", "ms", [out, val], [out], [], vcost(out, [out]))
    def scan(out, a, b, init, op0, op1): add("V", "scan", [out, a, b, init, op0, op1], [out], [a, b], vcost(out, [a, b]))
    def act(out, a, fn=AF.Copy, **kw):
        n = vcost(out, [a]) if a[0] == "*" else max(64, len(elems(a))) * CYC
        sums = [kw["accum_out"]] if "accum_out" in kw else []
        add("A", "act", [out, a, fn], [out] + sums, [a] + [x for x in kw.values() if x not in sums], n + 0.015 + 0.02 * len(sums), kw)
    def mmul(out, l, r, st, sp): add("T", "mm", [out, l, r, st, sp], [out], [l, r], max(64, len(elems(r))) * PL["pe"] * (4 if SCRATCH[l[0]][2] == F32 else 1), st=st, sp=sp)
    def iota(out, pat, base, cmul):
        kw = {} if SCRATCH[out[0]][2] == I32 else {"allow_small_or_imprecise_dtypes": True}
        add("G", "iota", [out, pat, base, cmul], [out], [], 0.14 + 2 * CYC * len(elems(out)), kw)
    def dma(q, out, a, sem, lat, behind=None): add(q, "dma", [out, a], [out], [a, behind], 0.06, sem=sem, lat=lat)
    def send(parts):
        nb = len(elems(parts[0][1])) * (4 if SCRATCH[parts[0][1][0]][2] in (F32, I32) else 2)
        add("G", "send", parts, [], [x[1] for x in parts], PL["issue"])
        me = len(ops) - 1
        for i, x in enumerate(parts):
            add("R", "recv", [parts, i], [x[2]], [], 0.0, sem=x[3], after=me, lat=HOP + nb * PL["byte"])
    def fill(name, vals, at=0):
        j = 0
        while j < len(vals):
            e = j + 1
            while e < len(vals) and vals[e] == vals[j]:
                e += 1
            ms(c(name, s(at + j, at + e)), float(vals[j]))
            j = e

    col = lambda name, j=0: c("sc", s(SC.index(name), SC.index(name) + 1)) if name in SC else c(name, s(j, j + 1))
    cols = lambda a, b: s(16 * a, 16 * b)
    Kw, Qw, Aw = c("K"), c("Q"), c("A", s(0, V))

    dma("A", col("lane", 8), ("tok", (slice(None),)), "dtok", 2.0)
    dma("A", c("x0s", s(0, 16)), ("x0", (slice(None),)), "dx0", 2.0)
    dma("A", col("kp"), ("kap", (slice(None),)), "dkap", 2.0)
    dma("S", Qw, ("qt", (slice(None),)), "dQ", 7.0)
    dma("S", Kw, ("kt", (slice(None),)), "dK", 9.5)
    ops[-1]["after"] = len(ops) - 2

    iota(col("lane", 0), [[0, 1]], 0, 1)
    iota(c("i16"), [[1, 16]], 0, 0)
    iota(c("wide"), [[1, 144]], -15, 0)
    iota(c("Ea"), [[0, 14], [1, 16]], 0, 0)
    iota(c("Eb"), [[0, 8], [32, 4], [1, 16]], 0, 0)
    iota(c("trash"), [[0, 6], [16, 4]], V, 0)
    iota(c("own"), [[0, 2], [1, 4], [0, 16]], 0, 0)
    iota(c("cm"), [[1, 32], [0, 4]], 0, 0)
    iota(c("B3"), [[1, 8], [0, 16]], 0, 0)
    iota(p("row", 0, 1), [[0, 8], [-4096, 16]], 15 * 4096, 0)
    ts(c("dep"), c("wide", s(15, 39)), STEP, Op.mult)
    ts(c("tf", s(12, 16)), c("dep", s(0, 4)), float(MID), Op.add)
    cp(col("lf"), col("lane", 0))
    for j, (sh, an) in enumerate([(0, 15), (4, 7), (4, 1), (0, 3)]):
        ts(col("lane", 1 + j), col("lane", 0), sh, Op.arith_shift_right, an, Op.bitwise_and)
    cp(c("sc", s(1, 5)), c("lane", s(1, 5)))
    l16, grp = col("l16"), col("grp")
    ts(col("evn"), col("odd"), -1.0, Op.mult, 1.0, Op.add)
    ts(col("o16"), col("odd"), 16.0, Op.mult)
    ts(col("g4"), grp, 4.0, Op.mult)
    ts(col("g16"), grp, 16.0, Op.mult)
    ts(col("place"), l16, -4096.0, Op.mult, 15 * 4096.0 - MID, Op.add)
    ts(col("look"), col("odd"), 2.0 ** 22, Op.mult, col("place"), Op.add)
    ms(c("z4"), 0.0); ms(c("m4"), float(MID)); ms(col("ok", 0), 1.0); ms(c("ms2", s(16, 20)), 0.0)
    ms(c("RS"), HIGH); ms(c("RS", s(0, 160, 16)), LOW)
    cp(col("tokf"), col("lane", 8))
    ts(c("x0s", s(16, 20)), c("z4"), col("tokf"), Op.add)
    send([(1, c("x0s"), c("mv0"), "rx0")])
    ts(col("nkp"), col("kp"), -1.0, Op.mult)
    lane = lambda n: ([1, 2, 3, 5] if n < 19 else [12, 9, 15]).index(PAR[n])
    pick = lambda j: col("sell", 2 * j)

    def entries(a, b):
        ts(c("Rm", s(a, b)), c("Ea", s(a, b)), l16, Op.is_equal)
        tt(c("RR", s(a, b)), c("RR", s(a, b)), c("Rm", s(a, b)), Op.mult)
        ts(c("Km", s(a, b)), c("Ea", s(a, b)), 0.5, Op.is_gt)
        scan(c("Rz", s(a, b)), c("Km", s(a, b)), c("RR", s(a, b)), 0.0, Op.mult, Op.add)

    iota(c("RR", s(0, 6)), [[1, 3], [0, 2]], 0, 0)
    iota(c("RR", s(8, 16)), [[1, 8]], 0, 0)
    fill("RR", [4, 4], 6)
    fill("RR", [32 * lane(n) + ROW[n] for n in range(9, 19)] + [32, 32, 0, 0, 64, 64], 16)
    fill("RR", [32 * lane(n) + ROW[n] for n in range(19, 24)] + [64] * 11, 32)
    entries(0, 48)
    ts(c("sell", s(0, 6, 2)), c("Rz", s(15, 48, 16)), col("o16"), Op.add)
    iota(c("RR", s(48, 133)), [[32, 5], [1, 17]], 0, 0)
    leaf = lambda n: 96 + 52 * (ROW[n] - 8) + 17 * lane(n) + 16 if PAR[n] < 5 else 512 + 18 * (ROW[n] - 13) + 16
    fill("RR", [leaf(n) if ROW[n] else 32 * lane(n) + 15 for n in range(9, 19)] + [15] * 6, 128)
    fill("RR", [{0: 16 + 32 * lane(n), 1: 115, 15: 147}[ROW[n]] for n in range(19, 24)] + [80] * 11, 144)
    iota(c("RR", s(160, 192)), [[1, 8], [1, 4]], 0, 0)
    ts(c("RR", s(160, 176)), c("RR", s(160, 176)), 3.0, Op.min)
    ts(c("RR", s(176, 192)), c("RR", s(176, 192)), 7.0, Op.min)
    entries(48, 192)
    ts(c("l17", s(0, 5)), c("Rz", s(63, 128, 16)), col("o16"), Op.add)
    ts(col("g8", 0), col("Rz", 15), 34.0, Op.mult, 16.0, Op.add)
    ts(pick(3), col("g8", 0), col("o16"), Op.add)
    ts(pick(7), col("g8", 0), 34.0 * 4 + 16, Op.min, col("o16"), Op.add)
    ts(pick(8), col("g8", 0), 34.0 * 2 + 16, Op.min, col("o16"), Op.add)
    ts(col("g8", 2), col("Rz", 143), 96.0, Op.is_lt, col("o16"), Op.mult)
    ts(pick(4), col("Rz", 143), col("g8", 2), Op.add)
    ts(pick(5), col("Rz", 159), col("o16"), Op.add)
    ts(pick(6), pick(1), 15.0, Op.add, 95.0, Op.min)
    cp(c("pairs"), c("Rz", s(175, 192, 16)))
    fill("PR", [16 * PAR[n] for n in range(1, 19)] + [16 * (PAR[n] - 8) for n in range(19, 24)] + [112]
         + [16 * PAR[n] for n in (12, 12, 9, 9, 15, 15)] + [32 * lane(n) for n in range(19, 24)] + [64])
    ts(c("parl"), c("PR"), l16, Op.add)
    cp(c("bc"), c("i16"))
    cp(c("colb"), c("wide", s(15, 143)))
    ts(c("Mk"), c("Eb"), l16, Op.is_le, 8192.0, Op.mult)
    ts(c("own"), c("own"), col("l4"), Op.is_equal, 0.25, Op.mult)
    ts(c("IdB"), c("colb"), col("lf"), Op.is_equal, 2.0 ** 23, Op.mult)
    ts(c("Id"), c("colb"), col("lf"), Op.is_equal)
    ts(c("Ge"), c("wide"), col("g16"), Op.is_equal, 2.0 ** 17, Op.mult)
    ms(p("mid", 0, 1), float(MID)); ms(p("ones", 0, 1), 1.0)
    ts(c("colb"), c("colb"), col("lf"), Op.subtract)
    for j, (shift, who) in enumerate([(0, "evn"), (-16, "odd"), (16, "evn"), (0, "odd")]):
        ts(c("Pk", j), c("colb"), float(shift), Op.is_equal, col(who), Op.mult)
    ts(c("cm"), c("cm"), col("g4"), Op.subtract)
    for j in range(4):
        ts(c("SelT", j), c("cm"), float(j), Op.is_equal, 65536.0, Op.mult)
    ts(c("d16"), c("i16"), l16, Op.is_equal)
    for j in range(16):
        ts(c("Sel", j), c("B3"), grp, Op.is_equal, col("d16", j), Op.mult)
    ts(c("trash"), c("trash"), l16, Op.add)
    ms(c("RL"), LOW); ms(c("RL", s(16, 51, 17)), HIGH); ms(c("RT"), LOW); ms(c("RT", s(0, 32, 16)), HIGH)
    ms(c("S1", s(0, 272, 34)), LOW); ms(c("S1", s(33, 272, 34)), LOW); ms(c("S2", s(96, 512, 52)), HIGH); ms(c("S2", s(512, 566, 18)), HIGH)
    ms(col("S3", 0), LOW); ms(c("S3", s(97, 100)), LOW); ms(c("Tt", s(288, 320)), 0.0)

    SPAN = [(0, 32), (128, 256), (32, 128)]
    WS = [(0, 16), (16, 32), (32, 48)]

    def ship(t, level, W=None):
        a, b, at = [(8, 16, 2), (16, 26, 10), (32, 38, 20), (8, 10, 2), (10, 12, 4), (12, 16, 6)][level]
        send([(1 + t, c(W or "Ws%d" % t, s(a, b)), c("Wl%d" % t, s(at, at + b - a)), "rW%d%d" % (t, level))])

    def draft0():
        cp(c("rootd"), c("x0s", s(16, 18)))
        for level, twice in enumerate((c("rootd"), c("Ws0", s(0, 8)), c("Ws0", s(26, 32)))):
            a, b = SPAN[level]
            cp(c("Gt", s(a, b)), ind(Qw, twice))
            trn(c("Tt", s(a, b)), c("Gt", s(a, b)))
            cp(c("Ws0", s(*WS[level])), ind(c("Tt", s(a, b)), pick(level)))
            ship(0, level)


    def tokens(out, win, lst, at):
        ts(c("Pi", s(at, at + 16)), ind(win, pick(lst)), float(MID), Op.add)
        ts(c("Pj", s(at, at + 16)), c("Pi", s(at, at + 16)), 4095, Op.bitwise_and)
        cp(out, c("Pj", s(at, at + 16)))

    def parents(out, win, lst, at, pairs):
        act(c("Pv", s(at, at + 16)), ind(win, pick(lst)))
        ts(c("Pr", s(at, at + 16)), ind(win, pick(lst)), ROUND, Op.add, ROUND, Op.subtract)
        for j, w in pairs:
            ts(c(out, s(j, j + w)), c("Pv", s(at + j, at + j + w)), col("Pr", at + j), Op.subtract, float(MID), Op.add)

    def draft(t):
        W, root = "Ws%d" % t, c("rl%d" % (t - 1), s(0, 2))
        Wp, Wq = "Wp%d" % t, "Wq%d" % t

        def turn(a, b, twice):
            act(c("Gt", s(a, b)), ind(Aw, twice), AF.Identity, bias=col("look"))
            trn(c("Tt", s(a, b)), c("Gt", s(a, b)))

        tag[0] = "d%d0" % t
        turn(0, 32, root)
        for r in range(8):
            scan(c("S1", s(34 * r + 1, 34 * r + 33)), c("Tt", s(0, 32)), c("S1", s(34 * r - 34, 34 * r - 2)) if r else c("Tt", s(0, 32)), LOW, Op.max, Op.min if r else Op.max)
            if r == 2:
                parents(Wp, c("S1", s(0, 102)), 8, 0, [(0, 2), (2, 2), (4, 2)] + [(8, 1), (9, 1)] * (t == 1))
                if t == 1:
                    ship(t, 3, Wp)
                tag[0] = "e%d0" % t
            if r == 4:
                parents(Wp, c("S1", s(0, 170)), 7, 16, [(6, 2)] + [(10, 1), (11, 1)] * (t == 1))
                if t == 1:
                    ship(t, 4, Wp)
        tokens(c(W, s(0, 16)), c("S1"), 3, 0)
        ship(t, 5 if t == 1 else 0)
        tag[0] = "d%d1" % t
        turn(128, 224, c(Wp, s(0, 6)))
        scan(c("S2", s(0, 96)), c("RS", s(0, 96)), c("Tt", s(128, 224)), LOW, Op.min, Op.max)
        parents(Wq, c("S2", s(0, 96)), 6, 32, [(10, 2), (12, 2), (14, 2)])
        if t == 2 and EARLY:
            send([(3, c(Wq, s(10, 16)), c("Wq1", s(0, 6)), "rW23")])
        tag[0] = "e%d1" % t
        act(c("X2"), ind(c("Tt", s(128, 256)), c("l17", s(0, 4))))
        for r in range(7, -1, -1):
            at = 96 + 52 * r
            scan(c("S2", s(at + 1, at + 52)), c("X2", s(0, 51)), c("RL") if r == 7 else c("S2", s(at + 52, at + 103)), HIGH, Op.min, Op.max)
        turn(256, 288, c(Wp, s(6, 8)))
        act(c("X5"), ind(c("Tt", s(256, 320)), c("l17", s(0, 2))))
        for r in range(2, -1, -1):
            at = 512 + 18 * r
            scan(c("S2", s(at + 1, at + 18)), c("X5", s(0, 17)), c("RL", s(0, 17)) if r == 2 else c("S2", s(at + 18, at + 35)), HIGH, Op.min, Op.max)
        tokens(c(W, s(16, 32)), c("S2"), 4, 16)
        ship(t, 1)
        tag[0] = "d%d2" % t
        turn(32, 128, c(Wq, s(10, 16)))
        scan(c("S3", s(1, 97)), c("RS", s(0, 96)), c("Tt", s(32, 128)), LOW, Op.min, Op.max)
        scan(c("S3", s(132, 164)), c("RT"), c("Tt", s(64, 96)), LOW, Op.max, Op.min)
        scan(c("S3", s(100, 132)), c("Tt", s(32, 64)), c("S3", s(0, 32)), LOW, Op.max, Op.min)
        tokens(c(W, s(32, 48)), c("S3"), 5, 32)
        ship(t, 2)

    def spare(t):
        W = "Ws%d" % t
        cp(col("Wf", 0), col("rl0" if t else "rootd", 0))
        cp(c("Wf", s(1, 9)), c(W, s(8, 16)))
        cp(c("Wf", s(9, 19)), c(W, s(16, 26)))
        cp(c("Wf", s(19, 24)), c(W, s(32, 37)))
        for j, bank in enumerate(("dif", "cnt", "dif")):
            a, b = 8 * j, 8 * j + 8
            later = c("Wx", s(32 * j, 32 * j + 32))
            ts(later, ind(c("Wf", s(a, b)), c("pairs", s(0, 2))), -float(MID), Op.add)
            act(c("Wy", s(a, b)), c("Wf", s(a, b)), AF.Identity, scale=-1.0, bias=float(MID))
            mmul(c(bank), c("Id"), c("Mk"), True, False)
            for q in range(16):
                mmul(c(bank, s(q, 512, 16)), c("Sel", q), later, False, q == 15)
            for n in range(8):
                e = s(64 * n, 64 * n + 64 - 16 * (n % 4))
                act(c("Eb", e), c(bank, e), AF.Abs, bias=col("Wy", a + n))
                act(c("Eb", e), c("Eb", e), AF.Relu, bias=4096.0, scale=-4096.0, accum_out=col("t24", a + n))
            tt(c("u24", s(a, b)), c("t24", s(a, b)), c("trash", s(a, b)), Op.min)
            tt(c("w24", s(a, b)), c("u24", s(a, b)), c("Wf", s(a, b)), Op.max)
            cp(c("L", s(a, b)), c("w24", s(a, b)))

    def scatter(t):
        for n in range(0, M, 4):
            cp(ind(c("A"), c("L", s(n, n + 4))), c("Ol%d" % t, cols(n, n + 4)))

    def states(depth, kn, x=None, near=False, first=((1, 9),)):
        if depth == 1:
            act(c("xn", s(0, 16)), x)
            act(c("xh", s(0, 16)), x, AF.Identity, scale=0.5)
            for a, b in first:
                tt(c("xn", cols(a, b)), ind(c("xh", s(0, 16)), c("parl", s(a - 1, b - 1))), c(kn, cols(a, b)), Op.add)
            act(c("xh", s(16, 96)), c("xn", s(16, 96)), AF.Identity, scale=0.5)
        elif depth == 2:
            tt(c("xn", s(144, 304)), ind(c("xh", s(0, 96)), c("parl", s(8, 18))), c(kn, s(144, 304)), Op.add)
            if near:
                ts(c("xh", s(128, 256)), c("xn", s(128, 256)), 0.5, Op.mult)
            else:
                act(c("xh", s(128, 256)), c("xn", s(128, 256)), AF.Identity, scale=0.5)
        else:
            tt(c("xn", s(304, 384)), ind(c("xh", s(128, 256)), c("parl", s(18, 23))), c(kn, s(304, 384)), Op.add)

    def verify(t):
        W, mv = "Wl%d" % t, "mv%d" % t
        if t == 0:
            cp(c("rootv"), c(mv, s(16, 18)))
        cp(c("cand", cols(0, 1)), ind(Qw, col("rn0" if t else "rootv", 0)))
        for a, b in FIRST[t] + DEPTH[1:]:
            cp(c("cand", cols(a, b)), ind(Qw, c(W, s(a + 1, b + 1))))
            act(c("kn", cols(a, b)), ind(Kw, c(W, s(a + 1, b + 1))))
        for d in range(3):
            states(d + 1, "kn", c(mv, s(0, 16)), first=FIRST[t])
        for lo, hi, who in GATHERS[t]:
            (cp if who == "V" else act)(c("kc", s(256 * lo, 256 * hi)), ind(Kw, c("cand", cols(lo, hi))))
        for j, (a, b) in enumerate(PIECES):
            bank = "k" + "ABCB"[j]
            ts(c("candh", cols(a, b)), c("cand", cols(a, b)), -float(MID), Op.add)
            mmul(c(bank, cols(a, b)), p("row", 0, 1), p("ones", 0, 1, cols(0, b - a)), True, False)
            mmul(c(bank, cols(a, b)), c("Id"), c("candh", cols(a, b)), False, False)
            for u, (lo, hi) in enumerate(CHUNKS):
                if a <= lo < b:
                    th = "th" + "AB"[u % 2]
                    act(c(th, cols(lo, hi)), c("xn", cols(lo, hi)), AF.Identity, bias=col("nkp"))
                    for k in range(16):
                        tt(c("ge", k, cols(lo, hi)), c("kc", s(256 * lo + k, 256 * hi, 16)), c(th, cols(lo, hi)), Op.is_ge)
                        mmul(c(bank, cols(lo, hi)), c("Ge", s(15 - k, 143 - k)), c("ge", k, cols(lo, hi)), False, hi == b and k == 15)
            if j < 2:
                trn(c("Kt", cols(a, b)), c(bank, cols(a, b)))
            act(c("Os%d" % t, cols(a, b)), c(bank, cols(a, b)), AF.Identity, bias=float(MID))
            send([(-1 - t, c("Os%d" % t, cols(a, b)), c("Ol%d" % t, cols(a, b)), "rO%d%d" % (t, j))])

    def chain(t):
        mv = "mv%d" % t
        act(c("CX", s(0, 16)), c(mv, s(0, 16)))
        for l in range(4):
            tk = c("CT", s(2 * l, 2 * l + 2)) if l else c("rn%d" % (t - 1), s(0, 2))
            x = c("CX", s(16 * l, 16 * l + 16)) if l else c(mv, s(0, 16))
            cp(c("cu"), ind(Qw, c(tk[0], s(tk[1][1].start, tk[1][1].start + 1))))
            if l:
                tt(x, ind(Kw, col("CT", 2 * l)), c("chx"), Op.add)
            for a, b in zip(CUTS, CUTS[1:]):
                act(c("thc", cols(a, b)), ind(x, c("bc", s(a, b))), AF.Identity, bias=col("nkp"))
            ts(c("ch"), ind(Qw, tk), -float(MID), Op.add)
            trn(c("cT"), c("ch"))
            if l < 3:
                act(c("chx"), x, AF.Identity, scale=0.5)
            tw = ("tw", "thA")[l % 2]
            out, bare = c(tw, s(0, 64)), c(tw, s(64, 128))
            mmul(c(tw, s(0, 128)), p("ones", 0, 1), p("row", 0, 1), True, False)
            mmul(c(tw, s(0, 128)), c("IdB"), c("own"), False, False)
            for j in range(4):
                mmul(c(tw, s(16 * j, 16 * j + 16)), c("Pk", 0), c("cT", s(0, 16)), False, False)
                mmul(c(tw, s(16 * j, 16 * j + 16)), c("Pk", 3), c("cT", s(16, 32)), False, False)
            for a, b in zip(CUTS, CUTS[1:]):
                tt(c("gec", cols(a, b)), ind(Kw, c("cu", s(a, b))), c("thc", cols(a, b)), Op.is_ge)
            for j in range(4):
                mmul(out, c("SelT", j), c("gec", s(64 * j, 64 * j + 64)), False, False)
                mmul(bare, c("SelT", j), c("gec", s(64 * j, 64 * j + 64)), False, j == 3)
            red(col("v", l), out, Op.max)
            red(col("v", 8 + l), bare, Op.max)
            if l < 3:
                ts(c("CT", s(2 * l + 2, 2 * l + 4)), c("m4", s(0, 2)), col("v", l), Op.add, col("v", 8 + l), Op.subtract)
                ts(col("tf", l), col("m4", 0), col("v", l), Op.add, col("v", 8 + l), Op.subtract)
                ts(col("tf", 4 + l), col("tf", 12 + l), col("v", l), Op.add, col("v", 8 + l), Op.subtract)

    kids = lambda q, by: s(PAR.index(q, 1) + by, M - PAR[::-1].index(q) + by)

    def settle(t, win):
        out = "ms%d" % t
        ts(col("bl", 0), col("v", 6), 16.0 / STEP, Op.mult, l16, Op.add)
        cp(c(out, s(0, 16)), ind(win, col("bl", 0)))
        send([(1, c(out), c("mv%d" % (t + 1)), "rv%d" % (t + 1))] * (t < 2) + [(-1 - t, c(out), c("md%d" % t), "rd%d" % t)] * (t > 0))

    def note(t):
        if t < 2:
            cp(col("Pv", 48 + t), col("rl%d" % t, 0))
        dma("S", ("yt", (slice(None), cols(t, t + 1))), col("Pv", 48 + t) if t < 2 else col("md2", 16), "dy%d" % t, 2.0)

    def commit(t):
        W = "Wl%d" % t
        for tw, (a, b) in zip(("tw", "kA"), PIECES[:2]):
            top = c("Km", s(16 * a + 15, 16 * b, 16))
            scan(c("Km", cols(a, b)), c("RS", cols(0, b - a)), c("Kt", cols(a, b)), LOW, Op.min, Op.max)
            ts(c("Ti", s(a, b)), top, ROUND, Op.add, ROUND, Op.subtract)
            tt(c("E", s(a, b)), top, c("Ti", s(a, b)), Op.subtract)
            mmul(c(tw, s(a, b)), p("ones", 0, 1), p("mid", 0, 1, s(a, b)), True, False)
            for j in range(4):
                mmul(c(tw, s(a + j % 2, b, 2)), c("Pk", j), c("E", s(a + j // 2, b, 2)), False, j == 3)
            for q in INNER:
                if a <= q < min(b, 9):
                    ts(c("ok", kids(q, 0)), c(W, kids(q, 1)), col(tw, q), Op.is_equal, col("ok", q), Op.mult)
        tt(c("Z", s(0, 19)), c("ok", s(0, 19)), c("dep", s(0, 19)), Op.mult)
        for q in INNER[5:]:
            ts(c("ok", kids(q, 0)), c("dep", kids(q, 0)), col("ok", q), Op.mult)
        for n in range(19, M):
            ts(col("Z", n), col(W, n + 1), col(tw, PAR[n]), Op.is_equal, col("ok", n), Op.mult)
        red(col("v", 6), c("Z"), Op.max)
        settle(t, c("xn"))
        for j, who in enumerate(("evn", "odd")):
            ts(c("Kt", s(256 + 16 * j, 272 + 16 * j)), ind(c("Os%d" % t), col("bl", 0)), -float(MID), Op.add, col(who), Op.mult)
        trn(c("Kt", s(288, 320)), c("Kt", s(256, 288)))
        red(col("v", 4), c("Kt", s(288, 320)), Op.max)
        ts(col("v", 5), col("v", 4), ROUND, Op.add, ROUND, Op.subtract)
        ts(c("rs%d" % t), c("m4"), col("v", 4), Op.add, col("v", 5), Op.subtract)
        send([(-1 - t, c("rs%d" % t), c("rl%d" % t), "rr%d" % t), (1, c("rs%d" % t), c("rn%d" % t), "rn%d" % t)])
        note(t)

    def chain_commit(t):
        W = "Wl%d" % t
        ts(c("Z", kids(0, 0)), c(W, kids(0, 1)), col("tf", 0), Op.is_equal, STEP, Op.mult)
        ts(c("g8", s(1, 6)), c("Z", s(1, 6)), 2.0, Op.mult)
        ts(c("g8", s(17, 20)), c("Z", s(1, 4)), 3.0, Op.mult)
        for q in INNER[1:]:
            if q > 8:
                own = col("Wq1", 2 * [12, 9, 15].index(q)) if EARLY else col(W, q + 1)
                ts(col("g8", q), own, col("tf", 1), Op.is_equal, col("g8", 16 + PAR[q]), Op.mult)
            ts(c("Z", kids(q, 0)), c(W, kids(q, 1)), col("tf", 1 + (q > 8)), Op.is_equal, col("g8", q), Op.mult)
        red(col("v", 6), c("Z", s(1, M)), Op.max)
        ts(c("tf", s(8, 11)), c("tf", s(4, 7)), col("v", 6), Op.subtract)
        ts(col("tf", 7), col("tf", 15), col("v", 6), Op.subtract)
        ts(col("tf", 11), col("tf", 7), col("v", 3), Op.add, col("v", 11), Op.subtract)
        red(col("ms2", 16), c("tf", s(8, 12)), Op.min, apply_absolute_value=True)
        settle(t, c("CX"))
        note(t)

    for t in range(2):
        tag[0] = "d%d" % t
        if t == 0:
            draft0()
            dma("S", Aw, ("qt", (slice(None),)), "dA", 7.0, c("Wl0", s(20, 26)))
        else:
            draft(t)
        tag[0] = "u%d" % t
        spare(t)
        tag[0] = "v%d" % t
        verify(t)
        tag[0] = "m%d" % t
        commit(t)
        tag[0] = "s%d" % t
        scatter(t)
    tag[0] = "d2"
    draft(2)
    tag[0] = "h2"
    chain(2)
    tag[0] = "v2"
    if EARLY:
        act(c("kqs"), ind(Kw, c("Wq1", s(0, 6))))
        send([(-3, c("kqs"), c("kql"), "rkq")])
    for d, (a, b) in enumerate(DEPTH):
        act(c("kns", cols(a, b)), ind(Kw, c("Wl2", s(a + 1, b + 1))))
        send([(-3, c("kns", cols(a, b)), c("knl", cols(a, b)), "rk" + "abc"[d])])
    tag[0] = "m2"
    chain_commit(2)
    tag[0] = "f"
    states(1, "knl", c("md1", s(0, 16)), near=True)
    if EARLY:
        tt(c("kn", s(0, 96)), ind(c("xh", s(0, 96)), c("parl", s(24, 30))), c("kql"), Op.add)
        act(c("xh", s(128, 224)), c("kn", s(0, 96)), AF.Identity, scale=0.5)
        tt(c("xn", s(144, 304)), ind(c("xh", s(0, 96)), c("parl", s(8, 18))), c("knl", s(144, 304)), Op.add)
        tt(c("xn", s(304, 384)), ind(c("xh", s(128, 224)), c("parl", s(30, 35))), c("knl", s(304, 384)), Op.add)
    else:
        states(2, "knl", near=True)
        states(3, "knl")
    dma("S", ("yn", (slice(None), s(0, 304))), c("xn", s(0, 304)), "dn0", 2.4)
    dma("A", ("yn", (slice(None), s(304, 384))), c("xn", s(304, 384)), "dn1", 2.1)
    dma("A", ("yx", (slice(None),)), c("md2", s(0, 16)), "dyx", 2.0)
    return ops


def plan():
    ops = build()
    lastw, readers, bank, group = {}, {}, {}, {}
    deps, order = [set() for _ in ops], [set() for _ in ops]
    for i, o in enumerate(ops):
        for r in o["r"]:
            w = lastw.setdefault(r[0], np.full(len(elems(c(r[0]))), -1))
            deps[i].update(int(x) for x in np.unique(w[elems(r)]) if x >= 0)
        for r in o["w"]:
            e = elems(r)
            w = lastw.setdefault(r[0], np.full(len(elems(c(r[0]))), -1))
            deps[i].update(int(x) for x in np.unique(w[e]) if x >= 0)
            keep = []
            for j, mask in readers.get(r[0], []):
                if mask[e].any():
                    deps[i].add(j)
                    mask[e] = False
                if mask.any():
                    keep.append((j, mask))
            readers[r[0]] = keep
            w[e] = i
        for r in o["r"]:
            mask = np.zeros(len(lastw[r[0]]), bool)
            mask[elems(r)] = True
            readers.setdefault(r[0], []).append((i, mask))
        for name in {r[0] for r in o["r"] + o["w"] if SCRATCH[r[0]][0] == "psum"}:
            b = bank.setdefault(name, [o["e"], [], []])
            if b[0] != o["e"]:
                b[0], b[1], b[2] = o["e"], [], b[1]
            deps[i].update(b[2])
            b[1].append(i)
        if o["m"] == "mm":
            name = o["w"][0][0]
            if o["st"]:
                order[i].update(group.get(name, [])[-1:])
                group[name] = [i]
            else:
                order[i].update(group[name] if o["sp"] else group[name][:1])
                group[name].append(i)
        if "after" in o:
            order[i].add(o["after"])
        deps[i].discard(i)
        if o["e"] == "T":
            deps[i] = {j for j in deps[i] if ops[j]["e"] != "T"}
    return arrange(ops, deps, order)


def arrange(ops, deps, order):
    n = len(ops)
    gap = lambda j, i: (ops[j]["lat"] + (PL["same"] if ops[j]["e"] == ops[i]["e"] else PL["cross"])) * (j in deps[i])
    pred = [[(j, gap(j, i)) for j in deps[i] | order[i]] for i in range(n)]
    succ = [[] for _ in ops]
    for i in range(n):
        for j, w in pred[i]:
            succ[j].append((i, w))

    def sweep(before, after, prio, start):
        left = [len(x) for x in before]
        rt, fin, busy, turn = list(start), [0.0] * n, {}, [0] * n
        ready = [i for i in range(n) if not left[i]]
        for step in range(n):
            i = max(ready, key=lambda i: (prio[i], -i))
            ready.remove(i)
            at, took, slots = rt[i], ops[i]["c"], busy.setdefault(ops[i]["e"], [])
            if took:
                pos = len(slots)
                while pos and slots[pos - 1][1] > at:
                    pos -= 1
                while pos < len(slots) and at + took > slots[pos][0] + 1e-9:
                    at = max(at, slots[pos][1])
                    pos += 1
                slots.insert(pos, (at, at + took))
            fin[i], turn[i] = at + took, step
            for k, w in after[i]:
                rt[k] = max(rt[k], fin[i] + w)
                left[k] -= 1
                if not left[k]:
                    ready.append(k)
        return sorted(range(n), key=lambda i: (round(fin[i] - ops[i]["c"], 6), turn[i])), fin

    def eager(before, after, prio, start):
        left = [len(x) for x in before]
        rt, fin, free, ready, seq = list(start), [0.0] * n, {}, {}, []
        for i in range(n):
            if not left[i]:
                ready.setdefault(ops[i]["e"], []).append(i)
        while len(seq) < n:
            te, e = min((max(free.get(e, 0.0), min(rt[i] for i in l)), e) for e, l in ready.items() if l)
            i = max((i for i in ready[e] if rt[i] <= te + PL["look"]), key=lambda i: (prio[i], -i))
            ready[e].remove(i)
            fin[i] = free[e] = max(te, rt[i]) + ops[i]["c"]
            seq.append(i)
            for k, w in after[i]:
                rt[k] = max(rt[k], fin[i] + w)
                left[k] -= 1
                if not left[k]:
                    ready.setdefault(ops[k]["e"], []).append(k)
        return seq, fin

    def turns(prio, passes, forward):
        best = None
        for _ in range(passes):
            seq, fin = forward(pred, succ, prio, [0.0] * n)
            end = max(fin[i] + ops[i]["lat"] for i in range(n))
            if best is None or end < best[0]:
                best = (end, seq, fin, prio)
            prio = eager(succ, pred, fin, [o["lat"] for o in ops])[1]
        return best

    def replay(seq, pace):
        fin, free = [0.0] * n, {}
        for i in seq:
            o = ops[i]
            at = max([free.get(o["e"], 0.0)] + [fin[j] + w for j, w in pred[i]])
            fin[i] = at + o["c"] * (1.0 if o["m"] in ("send", "dma") else pace)
            if o["e"] != "R":
                free[o["e"]] = fin[i]
        return max(fin[i] + ops[i]["lat"] for i in range(n))

    judge = lambda x: (x[0] + sum(replay(x[1], pace) / pace ** 0.6 for pace in PL["paces"]),) + x[1:]
    prio = [0.0] * n
    for i in range(n - 1, -1, -1):
        prio[i] = ops[i]["c"] + max([w + prio[k] for k, w in succ[i]] + [ops[i]["lat"]])
    best = now = judge(turns(prio, 6, sweep))
    keys = sorted({o["key"] for o in ops})
    rng = np.random.RandomState(1)
    for trial in range(PL["passes"]):
        shift = {keys[int(k)]: float(v) for k, v in zip(rng.randint(0, len(keys), 3), rng.normal(0.0, 0.7, 3))}
        if trial % 3 == 0:
            shift[keys[rng.randint(0, len(keys))].split(".")[0]] = float(rng.normal(0.0, 1.5))
        new = turns([now[3][i] + shift.get(ops[i]["key"], 0.0) + shift.get(ops[i]["key"].split(".")[0], 0.0) for i in range(n)], 2, (sweep, eager)[trial % 2])
        new = judge(new)
        if new[0] <= now[0] + 0.12:
            now = new
            best = min(best, new, key=lambda x: x[0])
    return ops, deps, best[1], best[2], order


PLAN = []


def masks(topo, src, dsts):
    out, used = {}, set()
    todo = sorted(range(len(dsts)), key=lambda i: len(topo.engines(src, dsts[i])))
    for pos, i in enumerate(todo):
        can = [e for e in topo.engines(src, dsts[i]) if e not in used]
        rivals = sum(1 for j in todo[pos:] if set(topo.engines(src, dsts[j])) <= set(topo.engines(src, dsts[i])))
        k = len(can) // rivals
        k = 1 << (k.bit_length() - 1)
        out[i] = can[:k]
        used.update(can[:k])
    return [out[i] for i in range(len(dsts))]


def rank_program(g, core, T, topo):
    rank = T.rank_of(core)
    if rank is None:
        return
    if not PLAN:
        PLAN.append(plan())
    ops, deps, seq = PLAN[0][:3]
    queue = {"V": g.vector, "A": g.scalar, "T": g.tensor, "G": g, "S": g.sync}
    call = {
        "cp": lambda a, k: g.vector.tensor_copy(*a), "tt": lambda a, k: g.vector.tensor_tensor(*a),
        "ts": lambda a, k: g.vector.tensor_scalar(*a), "red": lambda a, k: g.vector.tensor_reduce(*a, **k),
        "trn": lambda a, k: g.vector.transpose(*a), "ms": lambda a, k: g.vector.memset(*a),
        "scan": lambda a, k: g.vector.tensor_tensor_scan(*a), "act": lambda a, k: g.scalar.activation(*a, **k),
        "mm": lambda a, k: g.tensor.matmul(*a), "iota": lambda a, k: g.iota(*a, **k),
    }

    def ap(r):
        if not isinstance(r, tuple):
            return r
        if r[0] == "*":
            return ap(r[1]).indirect(ap(r[2]))
        return T[r[0]][r[1]]

    peer = lambda r, off: T.cores[(r + off) % N]
    needed = set()
    for d in deps:
        needed.update(d)
    count, mark, known, total = {}, {}, {e: {} for e in queue}, {}
    for i in seq:
        o = ops[i]
        e = o["e"]
        if e == "R":
            parts, k = o["a"]
            sender = (rank - parts[k][0]) % N
            n = len(masks(topo, T.cores[sender], [peer(sender, x[0]) for x in parts])[k])
            mark[i] = (o["sem"], n, {})
            total[o["sem"]] = n
            continue
        want = {}
        for j in deps[i]:
            if j in mark and mark[j][1] > want.get(mark[j][0], (0,))[0]:
                want[mark[j][0]] = mark[j][1:]
        for sem, (val, clock) in sorted(want.items(), key=lambda z: -len(z[1][1])):
            if known[e].get(sem, 0) < val:
                queue[e].wait_ge(T.sem[sem], val)
                known[e][sem] = val
            for s2, v2 in clock.items():
                known[e][s2] = max(known[e].get(s2, 0), v2)
        if o["m"] == "send":
            dsts = [peer(rank, x[0]) for x in o["a"]]
            trs = []
            for x, d, eng in zip(o["a"], dsts, masks(topo, core, dsts)):
                rid, pid = topo.addr(d)[:2]
                trs.append((ap(x[2]), ap(x[1]), T.sem[x[3]], pid, rid, sum(1 << b for b in eng)))
                total["left"] = total.get("left", 0) + len(eng)
            if len(trs) == 1:
                dst, src, sem, pid, rid, m = trs[0]
                g.remote_dma(dst, src, sem, T.sem.left, pid, rid, m)
            else:
                g.remote_dma_fused([RemoteDMATransfer(dst_ids=[DstId(rid=rid, pnc=pid)], dma_engine_mask=m, remote_sem=sem, src=src, dst=dst)
                                    for dst, src, sem, pid, rid, m in trs], local_sem=T.sem.left)
        elif o["m"] == "dma":
            queue[e].dma_start(ap(o["a"][0]), ap(o["a"][1])).then_inc(T.sem[o["sem"]], 16)
            mark[i] = (o["sem"], 16, dict(known[e]))
            total[o["sem"]] = 16
        else:
            ins = call[o["m"]]([ap(x) for x in o["a"]], {k: ap(x) for k, x in o["k"].items()})
            if i in needed:
                count[e] = count.get(e, 0) + 1
                ins.then_inc(T.sem["e" + e], 1)
                mark[i] = ("e" + e, count[e], dict(known[e]))
                total["e" + e] = count[e]
    for sem, val in total.items():
        if known["G"].get(sem, 0) < val:
            g.wait_ge(T.sem[sem], val)
